import numpy as np
import ml_dtypes


def mxq(x, axis, fmt="e4m3"):
    dtype, down = {"e4m3": (ml_dtypes.float8_e4m3fn, 7), "e5m2": (ml_dtypes.float8_e5m2, 14)}[fmt]
    v = np.moveaxis(np.asarray(x, np.float32).astype(ml_dtypes.bfloat16).astype(np.float64), axis, -1)
    blocks = v.reshape(v.shape[:-1] + (-1, 32))
    amax = np.abs(blocks).max(-1, keepdims=True)
    byte = np.maximum(np.where(amax > 0, np.frexp(amax)[1] - 1 + 127, 0) - down, 1)
    scale = np.exp2(byte - 127.0)
    codes = (blocks / scale).astype(np.float32).astype(dtype).astype(np.float64)
    return np.moveaxis((codes * scale).reshape(v.shape), -1, axis)


WIDE = False


def mx_kscale(k):
    if not WIDE:
        return np.ones(k)
    levels = np.array([10, -10, 5, -5, 0])
    if k % 512:
        return np.exp2(np.random.permutation(np.resize(levels, k // 32))).repeat(32)
    a = np.empty((k // 512, 16))
    for p in range(k // 512):
        a[p, :8] = np.random.permutation(np.resize(levels, 8))
        for g in range(8):
            far = levels[np.abs(levels - a[p, g]) >= 10]
            a[p, g + 8] = far[np.random.randint(len(far))]
    return np.exp2(a.ravel()).repeat(32)


def f64(x):
    return np.asarray(x).astype(np.float64)


def striped(idx):
    return np.tile(idx.reshape(-1, 16).T, (8, 1)).astype(np.uint16)


def unstriped(offs):
    return offs[:16].T.reshape(-1).astype(np.int64)


E2M1 = np.array([0.0, 0.5, 1.0, 1.5, 2.0, 3.0, 4.0, 6.0, -0.0, -0.5, -1.0, -1.5, -2.0, -3.0, -4.0, -6.0])


def pack_weight(w, fmt):
    k, n = w.shape
    w = f64(np.asarray(w, np.float32).astype(ml_dtypes.bfloat16)).reshape(k // 32, 32, n)
    amax = np.abs(w).max(1)
    if fmt == "e4m3":
        byte = np.frexp(amax)[1] - 1 + 127 - 7
    else:
        mant, ex = np.frexp(amax / 6.0)
        byte = np.where(mant > 0.5, ex, ex - 1) + 127
    byte = np.clip(np.where(amax > 0, byte, 1), 1, 254)
    scaled = (w * np.exp2(127.0 - byte)[:, None, :]).reshape(k, n).astype(np.float32)
    by_word = np.ascontiguousarray(scaled.reshape(k // 512, 128, 4, n).transpose(0, 1, 3, 2))
    if fmt == "e4m3":
        words = by_word.astype(ml_dtypes.float8_e4m3fn).view(np.uint8)
    else:
        c = by_word.astype(ml_dtypes.float4_e2m1fn).view(np.uint8) & 0xF
        words = (c[..., 0::2] | (c[..., 1::2] << 4)).reshape(k // 512, 128, 2 * n)
    return np.ascontiguousarray(words), np.ascontiguousarray(byte.astype(np.uint8).reshape(k // 512, 16, n))


def unpack_weight(words, scales, fmt):
    g, _, n = scales.shape
    words = np.ascontiguousarray(words).reshape(g, 128, n, -1)
    if fmt == "e4m3":
        vals = words.view(ml_dtypes.float8_e4m3fn).astype(np.float64)
    else:
        nib = np.empty((g, 128, n, 4), np.uint8)
        nib[..., 0::2] = words & 0xF
        nib[..., 1::2] = words >> 4
        vals = E2M1[nib]
    vals = vals * np.repeat(np.exp2(scales.astype(np.float64) - 127.0), 8, axis=1)[..., None]
    return vals.transpose(0, 1, 3, 2).reshape(g * 512, n)


def relu(v):
    return np.maximum(v, 0.0)


K, T, E, C, H, N, HOT = 512, 1024, 16, 256, 512, 128, 3


def by_expert(wq, xq):
    return np.concatenate([wq[e].T @ xq[:, e * C:(e + 1) * C] for e in range(E)], axis=1)


def setup_inputs():
    n = np.random.standard_normal
    s = mx_kscale(K)
    u = mx_kscale(H)
    slot_token = np.concatenate([np.random.permutation(T)[:C] for e in range(E)])
    x = pack_weight(n((K, T)) * s[:, None], "e4m3")
    w1h = [pack_weight(m, "e4m3") for m in n((HOT, K, H)) / np.sqrt(K) / s[None, :, None] * u]
    w2h = [pack_weight(m, "e4m3") for m in n((HOT, H, N)) / np.sqrt(H) / u[None, :, None]]
    w1c = [pack_weight(m, "e2m1") for m in n((E - HOT, K, H)) / np.sqrt(K) / s[None, :, None] * u]
    w2c = [pack_weight(m, "e2m1") for m in n((E - HOT, H, N)) / np.sqrt(H) / u[None, :, None]]
    return {
        "x_words": x[0],
        "x_scales": x[1],
        "w1h_words": np.stack([m[0] for m in w1h]),
        "w1h_scales": np.stack([m[1] for m in w1h]),
        "w2h_words": np.stack([m[0] for m in w2h]),
        "w2h_scales": np.stack([m[1] for m in w2h]),
        "w1c_words": np.stack([m[0] for m in w1c]),
        "w1c_scales": np.stack([m[1] for m in w1c]),
        "w2c_words": np.stack([m[0] for m in w2c]),
        "w2c_scales": np.stack([m[1] for m in w2c]),
        "offs": striped(slot_token),
    }


def reference(x_words, x_scales, w1h_words, w1h_scales, w2h_words, w2h_scales, w1c_words, w1c_scales, w2c_words, w2c_scales, offs):
    w1h = np.stack([unpack_weight(w1h_words[e], w1h_scales[e], "e4m3") for e in range(HOT)])
    w2h = np.stack([unpack_weight(w2h_words[e], w2h_scales[e], "e4m3") for e in range(HOT)])
    w1c = np.stack([unpack_weight(w1c_words[e], w1c_scales[e], "e2m1") for e in range(E - HOT)])
    w2c = np.stack([unpack_weight(w2c_words[e], w2c_scales[e], "e2m1") for e in range(E - HOT)])
    idx = unstriped(offs)
    xq = unpack_weight(x_words, x_scales, "e4m3")[:, idx]
    w1 = [*w1h, *w1c]
    w2 = [*w2h, *w2c]
    h = relu(by_expert(w1, xq))
    y = by_expert(w2, mxq(h, 0, "e4m3"))
    out = y
    return out

@@ -1,0 +1,169 @@
+from contextlib import ExitStack
+
+import concourse.mybir as mybir
+from concourse.masks import make_identity
+
+K, T, E, C, H, N, HOT = 512, 1024, 16, 256, 512, 128, 3
+FLOPS = 2 * E * C * (K * H + H * N)
+
+F32 = mybir.dt.float32
+BF16 = mybir.dt.bfloat16
+I32 = mybir.dt.int32
+U32 = mybir.dt.uint32
+U16 = mybir.dt.uint16
+U8 = mybir.dt.uint8
+FP8X4 = mybir.dt.float8_e4m3fn_x4
+FP4X4 = mybir.dt.float4_e2m1fn_x4
+RELU = mybir.ActivationFunctionType.Relu
+
+P = 128
+ORDER = list(range(E - 1, -1, -1))
+GATHERS = [(e, e + 1) for e in ORDER]
+W1_LOADS = [(15, 16), (14, 15), (12, 14), (10, 12), (7, 10), (5, 7), (3, 5), (2, 3), (0, 2)]
+W2_LOADS = [(15, 16), (12, 15), (8, 12), (3, 8), (0, 3)]
+S1_LOADS = [(12, 16), (3, 12), (0, 3)]
+
+
+def tile_moe_hot_s_mlp_relu_kernel(
+    tc, x_words, x_scales, w1h_words, w1h_scales, w2h_words, w2h_scales,
+    w1c_words, w1c_scales, w2c_words, w2c_scales, offs, out,
+):
+    nc = tc.nc
+    with ExitStack() as ctx:
+        held = ctx.enter_context(tc.tile_pool(name="held", bufs=1))
+        stream = ctx.enter_context(tc.tile_pool(name="stream", bufs=2))
+        ring = ctx.enter_context(tc.tile_pool(name="ring", bufs=3))
+        psum = ctx.enter_context(tc.psum_pool(name="psum", bufs=2))
+
+        def load_words(into, name, depth, hot, cold, first, last):
+            if first < HOT:
+                rows = hot.rearrange("e s p n d -> p (e s) (n d)")[:, first:last, :]
+            else:
+                rows = cold.rearrange("e s p w -> p (e s) w")[:, first - HOT : last - HOT, :]
+            tile = stream.tile([P, last - first, rows.shape[2]], U8, name=name, bufs=depth, align_bytes=64)
+            nc.sync.dma_start(tile[:].bitcast(I32), rows.bitcast(I32))
+            for e in range(first, last):
+                into[e] = tile[:, e - first, :]
+
+        def load_plane(name, rows, engine):
+            tile = held.tile([P, rows.shape[2], rows.shape[3]], U8, name=name, align_bytes=64)
+            engine.memset(tile[:].bitcast(I32), 0)
+            for r in range(4):
+                nc.sync.dma_start(tile[r:P:32, :, :].bitcast(I32), rows[r].bitcast(I32))
+            return tile
+
+        def load_scales(into, name, engine, hot, cold, first, last):
+            source, base = (hot, 0) if first < HOT else (cold, HOT)
+            rows = source.rearrange("e s (q r) n -> r q (e s) n", r=4)[:, :, first - base : last - base, :]
+            tile = load_plane(name, rows, engine)
+            for e in range(first, last):
+                into[e] = tile[:, e - first, :]
+
+        offsets = held.tile([P, E * C // 16], U16, name="offsets")
+        nc.sync.dma_start(offsets[:], offs)
+        token_words = held.tile([P, T], I32, name="token_words", align_bytes=64)
+        nc.sync.dma_start(token_words[:], x_words.rearrange("s p t d -> p (s t d)").bitcast(I32))
+        token_scales = load_plane("token_scales", x_scales.rearrange("s (q r) t -> r q s t", r=4), nc.vector)
+
+        w1, s1, w2, s2 = {}, {}, {}, {}
+        load_words(w1, "w1", 3, w1h_words, w1c_words, *W1_LOADS[0])
+        load_scales(s1, "s1_0", nc.vector, w1h_scales, w1c_scales, *S1_LOADS[0])
+        load_words(w1, "w1", 3, w1h_words, w1c_words, *W1_LOADS[1])
+        load_words(w1, "w1", 3, w1h_words, w1c_words, *W1_LOADS[2])
+        load_words(w2, "w2", 2, w2h_words, w2c_words, *W2_LOADS[0])
+        load_scales(s2, "s2_cold", nc.gpsimd, w2h_scales, w2c_scales, HOT, E)
+        identity = held.tile([P, P], F32, name="identity")
+        make_identity(nc, identity[:])
+        load_words(w2, "w2", 2, w2h_words, w2c_words, *W2_LOADS[1])
+        load_scales(s1, "s1_1", nc.gpsimd, w1h_scales, w1c_scales, *S1_LOADS[1])
+        load_scales(s1, "s1_2", nc.gpsimd, w1h_scales, w1c_scales, *S1_LOADS[2])
+        load_scales(s2, "s2_hot", nc.gpsimd, w2h_scales, w2c_scales, 0, HOT)
+
+        def codes_of(words, e, first, last):
+            if e < HOT:
+                return words[:, 4 * first : 4 * last].bitcast(FP8X4)
+            return words[:, 2 * first : 2 * last].bitcast(FP4X4)
+
+        slot_words, slot_scales = {}, {}
+
+        def gather(first, last):
+            listed = offsets[:, first * C // 16 : last * C // 16]
+            words = stream.tile([P, (last - first) * C], U32, name="slot_words", align_bytes=64)
+            scales = stream.tile([P, (last - first) * C], U8, name="slot_scales", align_bytes=64)
+            nc.vector.tensor_copy(words[:], token_words[:].bitcast(U32).indirect(listed))
+            nc.vector.tensor_copy(scales[:], token_scales[:, 0, :].indirect(listed))
+            for e in range(first, last):
+                slot_words[e] = words[:, (e - first) * C : (e - first + 1) * C]
+                slot_scales[e] = scales[:, (e - first) * C : (e - first + 1) * C]
+
+        hidden, h_codes, h_scales, results = {}, {}, {}, {}
+
+        def first_layer(e):
+            hidden[e] = ring.tile([P, 2, 2, P, 2], BF16, name="hidden", align_bytes=64)
+            for half in range(2):
+                sums = psum.tile([P, 2, H // 2], F32, name="sums", bufs=4)
+                cols = (half * H // 2, (half + 1) * H // 2)
+                for j in range(2):
+                    nc.tensor.matmul_mx(
+                        out=sums[:, j, :],
+                        lhsT=slot_words[e][:, j * P : (j + 1) * P].bitcast(FP8X4),
+                        lhsT_scale=slot_scales[e][:, j * P : (j + 1) * P],
+                        rhs=codes_of(w1[e], e, *cols),
+                        rhs_scale=s1[e][:, cols[0] : cols[1]],
+                        start=True,
+                        stop=True,
+                    )
+                nc.scalar.activation(
+                    hidden[e][:, :, :, half * 64 : (half + 1) * 64, :].rearrange("s j u p v -> s u j p v"),
+                    sums[:].rearrange("s j (p u v) -> s u j p v", u=2, v=2),
+                    RELU,
+                )
+
+        def turn(e):
+            pairs = hidden[e][:].rearrange("s j u p v -> s j u (p v)").bitcast(F32)
+            turned = psum.tile([P, 2, C], F32, name="turned")
+            for j in range(2):
+                for u in range(2):
+                    nc.tensor.transpose(turned[:, u, j * P : (j + 1) * P], pairs[:, j, u, :], identity[:])
+            grouped = ring.tile([P, C * 4], BF16, name="grouped", align_bytes=64)
+            nc.scalar.copy(
+                grouped[:].bitcast(F32).rearrange("p (c u) -> p c u", u=2),
+                turned[:].rearrange("p u c -> p c u"),
+            )
+            h_codes[e] = ring.tile([P, C], U32, name="h_codes", align_bytes=64)
+            h_scales[e] = ring.tile([P, C], U8, name="h_scales", align_bytes=64)
+            nc.vector.quantize_mx(out=h_codes[e][:].bitcast(FP8X4), scales=h_scales[e][:], in_=grouped[:])
+
+        def second_layer(e):
+            if e % 2 == 1:
+                results[e // 2] = psum.tile([P, 2, C], F32, name="results")
+            nc.tensor.matmul_mx(
+                out=results[e // 2][:, e % 2, :],
+                lhsT=codes_of(w2[e], e, 0, N),
+                lhsT_scale=s2[e],
+                rhs=h_codes[e][:].bitcast(FP8X4),
+                rhs_scale=h_scales[e][:],
+                start=True,
+                stop=True,
+            )
+            if e % 2 == 0:
+                staged = ring.tile([P, 2 * C], F32, name="staged")
+                nc.vector.tensor_copy(staged[:], results[e // 2][:].rearrange("n a c -> n (a c)"))
+                nc.sync.dma_start(out[:, e * C : (e + 2) * C], staged[:])
+
+        for step in range(E + 2):
+            for first, last in GATHERS:
+                if max(0, E - 1 - last) == step:
+                    gather(first, last)
+            if step < E:
+                first_layer(ORDER[step])
+                for done, coming in zip(W1_LOADS, W1_LOADS[3:]):
+                    if done[0] == ORDER[step]:
+                        load_words(w1, "w1", 3, w1h_words, w1c_words, *coming)
+            if 1 <= step <= E:
+                turn(ORDER[step - 1])
+            if step >= 2:
+                second_layer(ORDER[step - 2])
+                for done, coming in zip(W2_LOADS, W2_LOADS[2:]):
+                    if done[0] == ORDER[step - 2]:
+                        load_words(w2, "w2", 2, w2h_words, w2c_words, *coming)

@@ -1,7 +1,6 @@
 from contextlib import ExitStack
 
 import concourse.mybir as mybir
-from concourse.masks import make_identity
 
 K, T, E, C, H, N, HOT = 512, 1024, 16, 256, 512, 128, 3
 FLOPS = 2 * E * C * (K * H + H * N)
@@ -17,11 +16,7 @@ FP4X4 = mybir.dt.float4_e2m1fn_x4
 RELU = mybir.ActivationFunctionType.Relu
 
 P = 128
-ORDER = list(range(E - 1, -1, -1))
-GATHERS = [(e, e + 1) for e in ORDER]
-W1_LOADS = [(15, 16), (14, 15), (12, 14), (10, 12), (7, 10), (5, 7), (3, 5), (2, 3), (0, 2)]
-W2_LOADS = [(15, 16), (12, 15), (8, 12), (3, 8), (0, 3)]
-S1_LOADS = [(12, 16), (3, 12), (0, 3)]
+GROUPS = [(15, 16), (14, 15), (12, 14), (10, 12), (8, 10), (6, 8), (4, 6), (2, 4), (1, 2), (0, 1)]
 
 
 def tile_moe_hot_s_mlp_relu_kernel(
@@ -35,15 +30,15 @@ def tile_moe_hot_s_mlp_relu_kernel(
         ring = ctx.enter_context(tc.tile_pool(name="ring", bufs=3))
         psum = ctx.enter_context(tc.psum_pool(name="psum", bufs=2))
 
-        def load_words(into, name, depth, hot, cold, first, last):
+        def load_words(into, name, hot, cold, first, last):
             if first < HOT:
                 rows = hot.rearrange("e s p n d -> p (e s) (n d)")[:, first:last, :]
             else:
                 rows = cold.rearrange("e s p w -> p (e s) w")[:, first - HOT : last - HOT, :]
-            tile = stream.tile([P, last - first, rows.shape[2]], U8, name=name, bufs=depth, align_bytes=64)
+            tile = held.tile([P, last - first, rows.shape[2]], U8, name=name, align_bytes=64)
             nc.sync.dma_start(tile[:].bitcast(I32), rows.bitcast(I32))
             for e in range(first, last):
-                into[e] = tile[:, e - first, :]
+                into[e] = (tile, e - first)
 
         def load_plane(name, rows, engine):
             tile = held.tile([P, rows.shape[2], rows.shape[3]], U8, name=name, align_bytes=64)
@@ -59,25 +54,31 @@ def tile_moe_hot_s_mlp_relu_kernel(
             for e in range(first, last):
                 into[e] = tile[:, e - first, :]
 
-        offsets = held.tile([P, E * C // 16], U16, name="offsets")
-        nc.sync.dma_start(offsets[:], offs)
+        token_scales = held.tile([P, T], U8, name="token_scales", align_bytes=64)
+        quadrants = x_scales.rearrange("s (q r) t -> q s r t", r=4).bitcast(I32)
+        for q in range(4):
+            nc.sync.dma_start(
+                token_scales[32 * q : 32 * (q + 1), :].bitcast(I32), quadrants[q].to_broadcast([8, 4, T // 4])
+            )
+        w1, s1, w2, s2 = {}, {}, {}, {}
+        load_words(w1, "room_a", w1h_words, w1c_words, 15, 16)
         token_words = held.tile([P, T], I32, name="token_words", align_bytes=64)
         nc.sync.dma_start(token_words[:], x_words.rearrange("s p t d -> p (s t d)").bitcast(I32))
-        token_scales = load_plane("token_scales", x_scales.rearrange("s (q r) t -> r q s t", r=4), nc.vector)
-
-        w1, s1, w2, s2 = {}, {}, {}, {}
-        load_words(w1, "w1", 3, w1h_words, w1c_words, *W1_LOADS[0])
-        load_scales(s1, "s1_0", nc.vector, w1h_scales, w1c_scales, *S1_LOADS[0])
-        load_words(w1, "w1", 3, w1h_words, w1c_words, *W1_LOADS[1])
-        load_words(w1, "w1", 3, w1h_words, w1c_words, *W1_LOADS[2])
-        load_words(w2, "w2", 2, w2h_words, w2c_words, *W2_LOADS[0])
-        load_scales(s2, "s2_cold", nc.gpsimd, w2h_scales, w2c_scales, HOT, E)
-        identity = held.tile([P, P], F32, name="identity")
-        make_identity(nc, identity[:])
-        load_words(w2, "w2", 2, w2h_words, w2c_words, *W2_LOADS[1])
-        load_scales(s1, "s1_1", nc.gpsimd, w1h_scales, w1c_scales, *S1_LOADS[1])
-        load_scales(s1, "s1_2", nc.gpsimd, w1h_scales, w1c_scales, *S1_LOADS[2])
-        load_scales(s2, "s2_hot", nc.gpsimd, w2h_scales, w2c_scales, 0, HOT)
+        offsets = held.tile([P, E * C // 16], U16, name="offsets")
+        nc.sync.dma_start(offsets[:], offs)
+        load_scales(s1, "room_c", nc.gpsimd, w1h_scales, w1c_scales, 12, 16)
+        load_words(w1, "room_b", w1h_words, w1c_words, 14, 15)
+        load_words(w1, "room_d", w1h_words, w1c_words, 12, 14)
+        load_scales(s1, "s1_cold", nc.vector, w1h_scales, w1c_scales, HOT, 12)
+        load_scales(s2, "s2_cold", nc.vector, w2h_scales, w2c_scales, HOT, E)
+        load_scales(s1, "s1_hot", nc.vector, w1h_scales, w1c_scales, 0, HOT)
+        load_scales(s2, "s2_hot", nc.vector, w2h_scales, w2c_scales, 0, HOT)
+        after_reorder = {
+            15: [(w2, "room_a", w2h_words, w2c_words, HOT, E)],
+            14: [(w1, "room_b", w1h_words, w1c_words, 8, 12)],
+            12: [(w1, "room_d", w1h_words, w1c_words, HOT, 8), (w2, "room_c", w2h_words, w2c_words, 0, HOT)],
+            8: [(w1, "room_b", w1h_words, w1c_words, 0, HOT)],
+        }
 
         def codes_of(words, e, first, last):
             if e < HOT:
@@ -88,82 +89,103 @@ def tile_moe_hot_s_mlp_relu_kernel(
 
         def gather(first, last):
             listed = offsets[:, first * C // 16 : last * C // 16]
-            words = stream.tile([P, (last - first) * C], U32, name="slot_words", align_bytes=64)
-            scales = stream.tile([P, (last - first) * C], U8, name="slot_scales", align_bytes=64)
+            words = stream.tile([P, (last - first) * C], U32, name="slot_words", bufs=2, align_bytes=64)
+            scales = stream.tile([P, (last - first) * C], U8, name="slot_scales", bufs=2, align_bytes=64)
             nc.vector.tensor_copy(words[:], token_words[:].bitcast(U32).indirect(listed))
-            nc.vector.tensor_copy(scales[:], token_scales[:, 0, :].indirect(listed))
+            nc.vector.tensor_copy(scales[:], token_scales[:].indirect(listed))
             for e in range(first, last):
                 slot_words[e] = words[:, (e - first) * C : (e - first + 1) * C]
                 slot_scales[e] = scales[:, (e - first) * C : (e - first + 1) * C]
 
-        hidden, h_codes, h_scales, results = {}, {}, {}, {}
+        w1_turned, planes, grouped = {}, {}, {}
 
-        def first_layer(e):
-            hidden[e] = ring.tile([P, 2, 2, P, 2], BF16, name="hidden", align_bytes=64)
-            for half in range(2):
-                sums = psum.tile([P, 2, H // 2], F32, name="sums", bufs=4)
-                cols = (half * H // 2, (half + 1) * H // 2)
-                for j in range(2):
-                    nc.tensor.matmul_mx(
-                        out=sums[:, j, :],
-                        lhsT=slot_words[e][:, j * P : (j + 1) * P].bitcast(FP8X4),
-                        lhsT_scale=slot_scales[e][:, j * P : (j + 1) * P],
-                        rhs=codes_of(w1[e], e, *cols),
-                        rhs_scale=s1[e][:, cols[0] : cols[1]],
-                        start=True,
-                        stop=True,
-                    )
-                nc.scalar.activation(
-                    hidden[e][:, :, :, half * 64 : (half + 1) * 64, :].rearrange("s j u p v -> s u j p v"),
-                    sums[:].rearrange("s j (p u v) -> s u j p v", u=2, v=2),
-                    RELU,
+        def reorder(first, last):
+            count = last - first
+            planes[first] = ring.tile([P, count * (H + C)], U8, name="planes", bufs=4, align_bytes=64)
+            turned = ring.tile([P, count, 4 * H], U8, name="w1_turned", bufs=3, align_bytes=64)
+            for e in range(first, last):
+                nc.gpsimd.tensor_copy(
+                    planes[first][:, (e - first) * H : (e - first + 1) * H].rearrange("p (t m) -> p t m", t=4),
+                    s1[e].rearrange("p (m t) -> p t m", t=4),
+                )
+                w1_turned[e] = turned[:, e - first, :]
+            for e in range(first, min(last, HOT)):
+                tile, place = w1[e]
+                nc.gpsimd.tensor_copy(
+                    w1_turned[e].bitcast(U32).rearrange("p (t m) -> p t m", t=4),
+                    tile[:, place, :].bitcast(U32).rearrange("p (m t) -> p t m", t=4),
+                )
+            cold = max(first, HOT)
+            if cold < last:
+                tile, place = w1[cold]
+                nc.vector.tensor_copy(
+                    turned[:, cold - first :, 0 : 2 * H].bitcast(U16).rearrange("p e (t m) -> p e t m", t=4),
+                    tile[:, place : place + last - cold, :].bitcast(U16).rearrange("p e (m t) -> p e t m", t=4),
                 )
 
-        def turn(e):
-            pairs = hidden[e][:].rearrange("s j u p v -> s j u (p v)").bitcast(F32)
-            turned = psum.tile([P, 2, C], F32, name="turned")
-            for j in range(2):
-                for u in range(2):
-                    nc.tensor.transpose(turned[:, u, j * P : (j + 1) * P], pairs[:, j, u, :], identity[:])
-            grouped = ring.tile([P, C * 4], BF16, name="grouped", align_bytes=64)
-            nc.scalar.copy(
-                grouped[:].bitcast(F32).rearrange("p (c u) -> p c u", u=2),
-                turned[:].rearrange("p u c -> p c u"),
-            )
-            h_codes[e] = ring.tile([P, C], U32, name="h_codes", align_bytes=64)
-            h_scales[e] = ring.tile([P, C], U8, name="h_scales", align_bytes=64)
-            nc.vector.quantize_mx(out=h_codes[e][:].bitcast(FP8X4), scales=h_scales[e][:], in_=grouped[:])
+        def first_layer(first, last):
+            grouped[first] = ring.tile([P, (last - first) * C, 4], BF16, name="grouped", bufs=3, align_bytes=64)
+            for e in range(first, last):
+                for j in range(2):
+                    sums = psum.tile([P, 4, P], F32, name="sums", bufs=5)
+                    for t in range(4):
+                        column = (e - first) * H + t * P
+                        nc.tensor.matmul_mx(
+                            out=sums[:, t, :],
+                            lhsT=codes_of(w1_turned[e], e, t * P, (t + 1) * P),
+                            lhsT_scale=planes[first][:, column : column + P],
+                            rhs=slot_words[e][:, j * P : (j + 1) * P].bitcast(FP8X4),
+                            rhs_scale=slot_scales[e][:, j * P : (j + 1) * P],
+                            start=True,
+                            stop=True,
+                        )
+                    slot = (e - first) * C + j * P
+                    if (e, j) in [(0, 1), (1, 1), (2, 1)]:
+                        nc.vector.tensor_scalar_max(
+                            grouped[first][:, slot : slot + P, :], sums[:].rearrange("p t s -> p s t"), 0.0
+                        )
+                    else:
+                        nc.scalar.activation(
+                            grouped[first][:, slot : slot + P, :], sums[:].rearrange("p t s -> p s t"), RELU
+                        )
 
-        def second_layer(e):
-            if e % 2 == 1:
-                results[e // 2] = psum.tile([P, 2, C], F32, name="results")
-            nc.tensor.matmul_mx(
-                out=results[e // 2][:, e % 2, :],
-                lhsT=codes_of(w2[e], e, 0, N),
-                lhsT_scale=s2[e],
-                rhs=h_codes[e][:].bitcast(FP8X4),
-                rhs_scale=h_scales[e][:],
-                start=True,
-                stop=True,
+        def second_layer(first, last):
+            count = last - first
+            h_codes = ring.tile([P, count * C], U32, name="h_codes", align_bytes=64)
+            h_scales = planes[first][:, count * H :]
+            nc.vector.quantize_mx(
+                out=h_codes[:].bitcast(FP8X4),
+                scales=h_scales,
+                in_=grouped[first][:].rearrange("p c t -> p (c t)"),
             )
-            if e % 2 == 0:
-                staged = ring.tile([P, 2 * C], F32, name="staged")
-                nc.vector.tensor_copy(staged[:], results[e // 2][:].rearrange("n a c -> n (a c)"))
-                nc.sync.dma_start(out[:, e * C : (e + 2) * C], staged[:])
+            results = psum.tile([P, count * C], F32, name="results", bufs=2)
+            for e in range(first, last):
+                tile, place = w2[e]
+                slots = slice((e - first) * C, (e - first + 1) * C)
+                nc.tensor.matmul_mx(
+                    out=results[:, slots],
+                    lhsT=codes_of(tile[:, place, :], e, 0, N),
+                    lhsT_scale=s2[e],
+                    rhs=h_codes[:, slots].bitcast(FP8X4),
+                    rhs_scale=h_scales[:, slots],
+                    start=True,
+                    stop=True,
+                )
+            staged = ring.tile([P, count * C], F32, name="staged")
+            copy = nc.vector.tensor_copy if first in [] else nc.scalar.copy
+            copy(staged[:], results[:])
+            nc.sync.dma_start(out[:, first * C : last * C], staged[:])
 
-        for step in range(E + 2):
-            for first, last in GATHERS:
-                if max(0, E - 1 - last) == step:
-                    gather(first, last)
-            if step < E:
-                first_layer(ORDER[step])
-                for done, coming in zip(W1_LOADS, W1_LOADS[3:]):
-                    if done[0] == ORDER[step]:
-                        load_words(w1, "w1", 3, w1h_words, w1c_words, *coming)
-            if 1 <= step <= E:
-                turn(ORDER[step - 1])
-            if step >= 2:
-                second_layer(ORDER[step - 2])
-                for done, coming in zip(W2_LOADS, W2_LOADS[2:]):
-                    if done[0] == ORDER[step - 2]:
-                        load_words(w2, "w2", 2, w2h_words, w2c_words, *coming)
+        for step in range(-1, len(GROUPS) + 1):
+            if step + 1 < len(GROUPS):
+                first, last = GROUPS[step + 1]
+                gather(first, last)
+                reorder(first, last)
+                for e in range(first, last):
+                    for load in after_reorder.get(e, []):
+                        load_words(*load)
+            if 0 <= step < len(GROUPS):
+                first_layer(*GROUPS[step])
+            if step >= 1:
+                first, last = GROUPS[step - 1]
+                second_layer(first, last)

@@ -1,6 +1,7 @@
 from contextlib import ExitStack
 
 import concourse.mybir as mybir
+from concourse.masks import make_identity
 
 K, T, E, C, H, N, HOT = 512, 1024, 16, 256, 512, 128, 3
 FLOPS = 2 * E * C * (K * H + H * N)
@@ -16,7 +17,9 @@ FP4X4 = mybir.dt.float4_e2m1fn_x4
 RELU = mybir.ActivationFunctionType.Relu
 
 P = 128
-GROUPS = [(15, 16), (14, 15), (12, 14), (10, 12), (8, 10), (6, 8), (4, 6), (2, 4), (1, 2), (0, 1)]
+GROUPS = [(15, 16), (14, 15), (12, 14), (10, 12), (8, 10), (6, 8), (4, 6), (2, 4), (0, 2)]
+GATHERS = [(15, 16), (14, 15), (12, 14), (10, 12), (8, 10), (6, 8), (4, 6), (2, 4), (0, 2)]
+REORDERED = [0, 1, 2, 3]
 
 
 def tile_moe_hot_s_mlp_relu_kernel(
@@ -61,24 +64,20 @@ def tile_moe_hot_s_mlp_relu_kernel(
                 token_scales[32 * q : 32 * (q + 1), :].bitcast(I32), quadrants[q].to_broadcast([8, 4, T // 4])
             )
         w1, s1, w2, s2 = {}, {}, {}, {}
-        load_words(w1, "room_a", w1h_words, w1c_words, 15, 16)
         token_words = held.tile([P, T], I32, name="token_words", align_bytes=64)
         nc.sync.dma_start(token_words[:], x_words.rearrange("s p t d -> p (s t d)").bitcast(I32))
         offsets = held.tile([P, E * C // 16], U16, name="offsets")
         nc.sync.dma_start(offsets[:], offs)
+        load_words(w1, "room_a", w1h_words, w1c_words, 14, 16)
         load_scales(s1, "room_c", nc.gpsimd, w1h_scales, w1c_scales, 12, 16)
-        load_words(w1, "room_b", w1h_words, w1c_words, 14, 15)
-        load_words(w1, "room_d", w1h_words, w1c_words, 12, 14)
+        load_words(w1, "room_b", w1h_words, w1c_words, 12, 14)
+        identity = held.tile([P, P], F32, name="identity")
+        make_identity(nc, identity[:])
         load_scales(s1, "s1_cold", nc.vector, w1h_scales, w1c_scales, HOT, 12)
         load_scales(s2, "s2_cold", nc.vector, w2h_scales, w2c_scales, HOT, E)
         load_scales(s1, "s1_hot", nc.vector, w1h_scales, w1c_scales, 0, HOT)
         load_scales(s2, "s2_hot", nc.vector, w2h_scales, w2c_scales, 0, HOT)
-        after_reorder = {
-            15: [(w2, "room_a", w2h_words, w2c_words, HOT, E)],
-            14: [(w1, "room_b", w1h_words, w1c_words, 8, 12)],
-            12: [(w1, "room_d", w1h_words, w1c_words, HOT, 8), (w2, "room_c", w2h_words, w2c_words, 0, HOT)],
-            8: [(w1, "room_b", w1h_words, w1c_words, 0, HOT)],
-        }
+        later_loads = {14: [(2, 'room_a', 3, 16)], 15: [(1, 'room_e', 8, 12)], 12: [(1, 'room_b', 3, 8), (2, 'room_c', 0, 3)], 8: [(1, 'room_e', 0, 3)]}
 
         def codes_of(words, e, first, last):
             if e < HOT:
@@ -97,66 +96,90 @@ def tile_moe_hot_s_mlp_relu_kernel(
                 slot_words[e] = words[:, (e - first) * C : (e - first + 1) * C]
                 slot_scales[e] = scales[:, (e - first) * C : (e - first + 1) * C]
 
-        w1_turned, planes, grouped = {}, {}, {}
+        hidden, turned, grouped = {}, {}, {}
 
-        def reorder(first, last):
-            count = last - first
-            planes[first] = ring.tile([P, count * (H + C)], U8, name="planes", bufs=4, align_bytes=64)
-            turned = ring.tile([P, count, 4 * H], U8, name="w1_turned", bufs=3, align_bytes=64)
-            for e in range(first, last):
-                nc.gpsimd.tensor_copy(
-                    planes[first][:, (e - first) * H : (e - first + 1) * H].rearrange("p (t m) -> p t m", t=4),
-                    s1[e].rearrange("p (m t) -> p t m", t=4),
-                )
-                w1_turned[e] = turned[:, e - first, :]
-            for e in range(first, min(last, HOT)):
-                tile, place = w1[e]
-                nc.gpsimd.tensor_copy(
-                    w1_turned[e].bitcast(U32).rearrange("p (t m) -> p t m", t=4),
-                    tile[:, place, :].bitcast(U32).rearrange("p (m t) -> p t m", t=4),
-                )
-            cold = max(first, HOT)
-            if cold < last:
-                tile, place = w1[cold]
-                nc.vector.tensor_copy(
-                    turned[:, cold - first :, 0 : 2 * H].bitcast(U16).rearrange("p e (t m) -> p e t m", t=4),
-                    tile[:, place : place + last - cold, :].bitcast(U16).rearrange("p e (m t) -> p e t m", t=4),
+        def reorder_scales(e, engine):
+            plane = held.tile([P, H], U8, name="plane_%d" % e, align_bytes=64)
+            engine.tensor_copy(plane[:].rearrange("p (t m) -> p t m", t=4), s1[e].rearrange("p (m t) -> p t m", t=4))
+            s1[e] = plane[:]
+
+        def reorder_words(e, engine):
+            tile, place = w1[e]
+            word = U32 if e < HOT else U16
+            words = ring.tile([P, 1, tile.shape[2]], U8, name="hot_words" if e < HOT else "cold_words", bufs=3 if e < HOT else 2, align_bytes=64)
+            engine.tensor_copy(
+                words[:, 0, :].bitcast(word).rearrange("p (t m) -> p t m", t=4),
+                tile[:, place, :].bitcast(word).rearrange("p (m t) -> p t m", t=4),
+            )
+            w1[e] = (words, 0)
+
+        def relu(e, j, written, sums):
+            if (e, j) in [(0, 1), (1, 1), (2, 1)]:
+                nc.vector.tensor_scalar_max(written, sums, 0.0)
+            else:
+                nc.scalar.activation(written, sums, RELU)
+
+        def first_layer_weights_stationary(e):
+            tile, place = w1[e]
+            for j in range(2):
+                sums = psum.tile([P, 4, P], F32, name="sums", bufs=4)
+                for t in range(4):
+                    nc.tensor.matmul_mx(
+                        out=sums[:, t, :],
+                        lhsT=codes_of(tile[:, place, :], e, t * P, (t + 1) * P),
+                        lhsT_scale=s1[e][:, t * P : (t + 1) * P],
+                        rhs=slot_words[e][:, j * P : (j + 1) * P].bitcast(FP8X4),
+                        rhs_scale=slot_scales[e][:, j * P : (j + 1) * P],
+                        start=True,
+                        stop=True,
+                    )
+                relu(e, j, grouped[e][:, j * P : (j + 1) * P, :], sums[:].rearrange("p t s -> p s t"))
+
+        def first_layer_tokens_stationary(e):
+            tile, place = w1[e]
+            hidden[e] = ring.tile([P, 2, 2, P, 2], BF16, name="hidden", bufs=4, align_bytes=64)
+            for half in range(2):
+                sums = psum.tile([P, 2, H // 2], F32, name="sums", bufs=4)
+                cols = (half * H // 2, (half + 1) * H // 2)
+                for j in (0, 1) if half == 0 else (0, 1):
+                    nc.tensor.matmul_mx(
+                        out=sums[:, j, :],
+                        lhsT=slot_words[e][:, j * P : (j + 1) * P].bitcast(FP8X4),
+                        lhsT_scale=slot_scales[e][:, j * P : (j + 1) * P],
+                        rhs=codes_of(tile[:, place, :], e, *cols),
+                        rhs_scale=s1[e][:, cols[0] : cols[1]],
+                        start=True,
+                        stop=True,
+                    )
+                relu(
+                    e,
+                    half,
+                    hidden[e][:, :, :, half * 64 : (half + 1) * 64, :].rearrange("s j u p v -> s u j p v"),
+                    sums[:].rearrange("s j (p u v) -> s u j p v", u=2, v=2),
                 )
 
-        def first_layer(first, last):
-            grouped[first] = ring.tile([P, (last - first) * C, 4], BF16, name="grouped", bufs=3, align_bytes=64)
-            for e in range(first, last):
-                for j in range(2):
-                    sums = psum.tile([P, 4, P], F32, name="sums", bufs=5)
-                    for t in range(4):
-                        column = (e - first) * H + t * P
-                        nc.tensor.matmul_mx(
-                            out=sums[:, t, :],
-                            lhsT=codes_of(w1_turned[e], e, t * P, (t + 1) * P),
-                            lhsT_scale=planes[first][:, column : column + P],
-                            rhs=slot_words[e][:, j * P : (j + 1) * P].bitcast(FP8X4),
-                            rhs_scale=slot_scales[e][:, j * P : (j + 1) * P],
-                            start=True,
-                            stop=True,
-                        )
-                    slot = (e - first) * C + j * P
-                    if (e, j) in [(0, 1), (1, 1), (2, 1)]:
-                        nc.vector.tensor_scalar_max(
-                            grouped[first][:, slot : slot + P, :], sums[:].rearrange("p t s -> p s t"), 0.0
-                        )
-                    else:
-                        nc.scalar.activation(
-                            grouped[first][:, slot : slot + P, :], sums[:].rearrange("p t s -> p s t"), RELU
-                        )
+        def turn(e):
+            pairs = hidden[e][:].rearrange("s j u p v -> s j u (p v)").bitcast(F32)
+            turned[e] = psum.tile([P, 2, C], F32, name="turned", bufs=2)
+            for j in range(2):
+                for u in range(2):
+                    nc.tensor.transpose(turned[e][:, u, j * P : (j + 1) * P], pairs[:, j, u, :], identity[:])
+
+        def interleave(e):
+            copy = nc.vector.tensor_copy if e in [4] else nc.scalar.copy
+            copy(
+                grouped[e].rearrange("p c t -> p (c t)").bitcast(F32).rearrange("p (c u) -> p c u", u=2),
+                turned[e][:].rearrange("p u c -> p c u"),
+            )
 
         def second_layer(first, last):
             count = last - first
             h_codes = ring.tile([P, count * C], U32, name="h_codes", align_bytes=64)
-            h_scales = planes[first][:, count * H :]
+            h_scales = ring.tile([P, count * C], U8, name="h_scales", align_bytes=64)
             nc.vector.quantize_mx(
                 out=h_codes[:].bitcast(FP8X4),
-                scales=h_scales,
-                in_=grouped[first][:].rearrange("p c t -> p (c t)"),
+                scales=h_scales[:],
+                in_=group_tile[first][:].rearrange("p c t -> p (c t)"),
             )
             results = psum.tile([P, count * C], F32, name="results", bufs=2)
             for e in range(first, last):
@@ -172,20 +195,51 @@ def tile_moe_hot_s_mlp_relu_kernel(
                     stop=True,
                 )
             staged = ring.tile([P, count * C], F32, name="staged")
-            copy = nc.vector.tensor_copy if first in [] else nc.scalar.copy
+            copy = nc.vector.tensor_copy if first in [0, 14, 15] else nc.scalar.copy
             copy(staged[:], results[:])
             nc.sync.dma_start(out[:, first * C : last * C], staged[:])
 
-        for step in range(-1, len(GROUPS) + 1):
-            if step + 1 < len(GROUPS):
-                first, last = GROUPS[step + 1]
-                gather(first, last)
-                reorder(first, last)
-                for e in range(first, last):
-                    for load in after_reorder.get(e, []):
-                        load_words(*load)
-            if 0 <= step < len(GROUPS):
-                first_layer(*GROUPS[step])
-            if step >= 1:
-                first, last = GROUPS[step - 1]
-                second_layer(first, last)
+        group_tile = {}
+        if 'G' == "G":
+            for e in sorted(REORDERED, reverse=True):
+                if e >= HOT:
+                    reorder_scales(e, nc.gpsimd)
+        gather(*GATHERS[0])
+        for step in range(E + 4):
+            e = E - 1 - step
+            for (first, last), coming in zip(GATHERS, GATHERS[1:]):
+                if e == last - 1:
+                    gather(*coming)
+                    for other in range(coming[1] - 1, coming[0] - 1, -1):
+                        if other in REORDERED:
+                            if other >= HOT or 'G' == "V":
+                                if other < HOT or 'G' == "V":
+                                    reorder_scales(other, nc.vector)
+                                reorder_words(other, nc.vector)
+            for first, last in GROUPS:
+                if e == last - 1:
+                    group_tile[first] = ring.tile([P, (last - first) * C, 4], BF16, name="grouped", bufs=4, align_bytes=64)
+                    for other in range(first, last):
+                        grouped[other] = group_tile[first][:, (other - first) * C : (other - first + 1) * C, :]
+            if e >= 0:
+                if e in REORDERED:
+                    first_layer_weights_stationary(e)
+                else:
+                    first_layer_tokens_stationary(e)
+                for into, room, first, last in later_loads.get(e, []):
+                    if into == 1:
+                        load_words(w1, room, w1h_words, w1c_words, first, last)
+                        if first == 0 and 'G' == "G":
+                            for other in range(HOT - 1, -1, -1):
+                                if other in REORDERED:
+                                    reorder_scales(other, nc.gpsimd)
+                                    reorder_words(other, nc.gpsimd)
+                    else:
+                        load_words(w2, room, w2h_words, w2c_words, first, last)
+            if 0 <= e + 1 < E and e + 1 not in REORDERED:
+                turn(e + 1)
+            if 0 <= e + 2 < E and e + 2 not in REORDERED:
+                interleave(e + 2)
+            for first, last in GROUPS:
+                if first == e + 4:
+                    second_layer(first, last)

@@ -18,7 +18,7 @@ RELU = mybir.ActivationFunctionType.Relu
 
 P = 128
 GROUPS = [(15, 16), (14, 15), (12, 14), (10, 12), (8, 10), (6, 8), (4, 6), (2, 4), (0, 2)]
-GATHERS = [(15, 16), (14, 15), (12, 14), (10, 12), (8, 10), (6, 8), (4, 6), (2, 4), (0, 2)]
+GATHERS = [(15, 16), (14, 15), (13, 14), (12, 13), (11, 12), (10, 11), (9, 10), (8, 9), (7, 8), (6, 7), (5, 6), (4, 5), (3, 4), (2, 3), (1, 2), (0, 1)]
 REORDERED = [0, 1, 2, 3]
 
 
@@ -64,19 +64,25 @@ def tile_moe_hot_s_mlp_relu_kernel(
                 token_scales[32 * q : 32 * (q + 1), :].bitcast(I32), quadrants[q].to_broadcast([8, 4, T // 4])
             )
         w1, s1, w2, s2 = {}, {}, {}, {}
+        engines = {"V": nc.vector, "G": nc.gpsimd}
         token_words = held.tile([P, T], I32, name="token_words", align_bytes=64)
-        nc.sync.dma_start(token_words[:], x_words.rearrange("s p t d -> p (s t d)").bitcast(I32))
         offsets = held.tile([P, E * C // 16], U16, name="offsets")
-        nc.sync.dma_start(offsets[:], offs)
-        load_words(w1, "room_a", w1h_words, w1c_words, 14, 16)
-        load_scales(s1, "room_c", nc.gpsimd, w1h_scales, w1c_scales, 12, 16)
+        for what in 'owxs':
+            if what == "x":
+                nc.sync.dma_start(token_words[:], x_words.rearrange("s p t d -> p (s t d)").bitcast(I32))
+            if what == "o":
+                nc.sync.dma_start(offsets[:], offs)
+            if what == "w":
+                load_words(w1, "room_a", w1h_words, w1c_words, 14, 16)
+            if what == "s":
+                load_scales(s1, "room_c", nc.gpsimd, w1h_scales, w1c_scales, 12, 16)
         load_words(w1, "room_b", w1h_words, w1c_words, 12, 14)
         identity = held.tile([P, P], F32, name="identity")
         make_identity(nc, identity[:])
-        load_scales(s1, "s1_cold", nc.vector, w1h_scales, w1c_scales, HOT, 12)
-        load_scales(s2, "s2_cold", nc.vector, w2h_scales, w2c_scales, HOT, E)
-        load_scales(s1, "s1_hot", nc.vector, w1h_scales, w1c_scales, 0, HOT)
-        load_scales(s2, "s2_hot", nc.vector, w2h_scales, w2c_scales, 0, HOT)
+        load_scales(s1, "s1_cold", engines['GGGG'[0]], w1h_scales, w1c_scales, HOT, 12)
+        load_scales(s2, "s2_cold", engines['GGGG'[1]], w2h_scales, w2c_scales, HOT, E)
+        load_scales(s1, "s1_hot", engines['GGGG'[2]], w1h_scales, w1c_scales, 0, HOT)
+        load_scales(s2, "s2_hot", engines['GGGG'[3]], w2h_scales, w2c_scales, 0, HOT)
         later_loads = {14: [(2, 'room_a', 3, 16)], 15: [(1, 'room_e', 8, 12)], 12: [(1, 'room_b', 3, 8), (2, 'room_c', 0, 3)], 8: [(1, 'room_e', 0, 3)]}
 
         def codes_of(words, e, first, last):
@@ -88,8 +94,8 @@ def tile_moe_hot_s_mlp_relu_kernel(
 
         def gather(first, last):
             listed = offsets[:, first * C // 16 : last * C // 16]
-            words = stream.tile([P, (last - first) * C], U32, name="slot_words", bufs=2, align_bytes=64)
-            scales = stream.tile([P, (last - first) * C], U8, name="slot_scales", bufs=2, align_bytes=64)
+            words = stream.tile([P, (last - first) * C], U32, name="slot_words", bufs=3, align_bytes=64)
+            scales = stream.tile([P, (last - first) * C], U8, name="slot_scales", bufs=3, align_bytes=64)
             nc.vector.tensor_copy(words[:], token_words[:].bitcast(U32).indirect(listed))
             nc.vector.tensor_copy(scales[:], token_scales[:].indirect(listed))
             for e in range(first, last):
@@ -114,7 +120,7 @@ def tile_moe_hot_s_mlp_relu_kernel(
             w1[e] = (words, 0)
 
         def relu(e, j, written, sums):
-            if (e, j) in [(0, 1), (1, 1), (2, 1)]:
+            if (e, j) in [(1, 0), (1, 1), (2, 0), (10, 0), (15, 0)]:
                 nc.vector.tensor_scalar_max(written, sums, 0.0)
             else:
                 nc.scalar.activation(written, sums, RELU)
@@ -137,11 +143,11 @@ def tile_moe_hot_s_mlp_relu_kernel(
 
         def first_layer_tokens_stationary(e):
             tile, place = w1[e]
-            hidden[e] = ring.tile([P, 2, 2, P, 2], BF16, name="hidden", bufs=4, align_bytes=64)
+            hidden[e] = ring.tile([P, 2, 2, P, 2], BF16, name="hidden", bufs=2, align_bytes=64)
             for half in range(2):
                 sums = psum.tile([P, 2, H // 2], F32, name="sums", bufs=4)
                 cols = (half * H // 2, (half + 1) * H // 2)
-                for j in (0, 1) if half == 0 else (0, 1):
+                for j in (0, 0, 1) if (e, half) in [] else (0, 1):
                     nc.tensor.matmul_mx(
                         out=sums[:, j, :],
                         lhsT=slot_words[e][:, j * P : (j + 1) * P].bitcast(FP8X4),
@@ -166,7 +172,7 @@ def tile_moe_hot_s_mlp_relu_kernel(
                     nc.tensor.transpose(turned[e][:, u, j * P : (j + 1) * P], pairs[:, j, u, :], identity[:])
 
         def interleave(e):
-            copy = nc.vector.tensor_copy if e in [4] else nc.scalar.copy
+            copy = nc.vector.tensor_copy if e in [4, 6] else nc.scalar.copy
             copy(
                 grouped[e].rearrange("p c t -> p (c t)").bitcast(F32).rearrange("p (c u) -> p c u", u=2),
                 turned[e][:].rearrange("p u c -> p c u"),
@@ -195,7 +201,7 @@ def tile_moe_hot_s_mlp_relu_kernel(
                     stop=True,
                 )
             staged = ring.tile([P, count * C], F32, name="staged")
-            copy = nc.vector.tensor_copy if first in [0, 14, 15] else nc.scalar.copy
+            copy = nc.vector.tensor_copy if first in [0, 10, 12] else nc.scalar.copy
             copy(staged[:], results[:])
             nc.sync.dma_start(out[:, first * C : last * C], staged[:])
 
@@ -218,7 +224,7 @@ def tile_moe_hot_s_mlp_relu_kernel(
                                 reorder_words(other, nc.vector)
             for first, last in GROUPS:
                 if e == last - 1:
-                    group_tile[first] = ring.tile([P, (last - first) * C, 4], BF16, name="grouped", bufs=4, align_bytes=64)
+                    group_tile[first] = ring.tile([P, (last - first) * C, 4], BF16, name="grouped", bufs=3, align_bytes=64)
                     for other in range(first, last):
                         grouped[other] = group_tile[first][:, (other - first) * C : (other - first + 1) * C, :]
             if e >= 0:

@@ -17,9 +17,12 @@ FP4X4 = mybir.dt.float4_e2m1fn_x4
 RELU = mybir.ActivationFunctionType.Relu
 
 P = 128
-GROUPS = [(15, 16), (14, 15), (12, 14), (10, 12), (8, 10), (6, 8), (4, 6), (2, 4), (0, 2)]
-GATHERS = [(15, 16), (14, 15), (13, 14), (12, 13), (11, 12), (10, 11), (9, 10), (8, 9), (7, 8), (6, 7), (5, 6), (4, 5), (3, 4), (2, 3), (1, 2), (0, 1)]
-REORDERED = [0, 1, 2, 3]
+GATHERS = [(3968, 4096),(3840, 3968),(3712, 3840),(3584, 3712),(3328, 3584),(3072, 3328),(2816, 3072),(2560, 2816),(2304, 2560),(2048, 2304),(1792, 2048),(1536, 1792),(1280, 1536),(1024, 1280),(768, 1024),(512, 768),(256, 512),(0, 256)]
+GATHER_ROOMS = [0,1,2,3,0,1,2,3,0,1,2,3,0,1,2,3,0,1]
+GROUPS = [(14, 16), (12, 14), (10, 12), (8, 10), (6, 8), (4, 6), (2, 4), (1, 2), (0, 1)]
+VECTOR_RELU = [(0,0),(1,0),(2,0)]
+VECTOR_WEAVE = []
+SCALAR_OUT = [14,10,6,2,0]
 
 
 def tile_moe_hot_s_mlp_relu_kernel(
@@ -29,9 +32,8 @@ def tile_moe_hot_s_mlp_relu_kernel(
     nc = tc.nc
     with ExitStack() as ctx:
         held = ctx.enter_context(tc.tile_pool(name="held", bufs=1))
-        stream = ctx.enter_context(tc.tile_pool(name="stream", bufs=2))
         ring = ctx.enter_context(tc.tile_pool(name="ring", bufs=3))
-        psum = ctx.enter_context(tc.psum_pool(name="psum", bufs=2))
+        psum = ctx.enter_context(tc.psum_pool(name="psum", bufs=1))
 
         def load_words(into, name, hot, cold, first, last):
             if first < HOT:
@@ -41,211 +43,208 @@ def tile_moe_hot_s_mlp_relu_kernel(
             tile = held.tile([P, last - first, rows.shape[2]], U8, name=name, align_bytes=64)
             nc.sync.dma_start(tile[:].bitcast(I32), rows.bitcast(I32))
             for e in range(first, last):
-                into[e] = (tile, e - first)
+                into[e] = tile[:, e - first, :]
 
-        def load_plane(name, rows, engine):
-            tile = held.tile([P, rows.shape[2], rows.shape[3]], U8, name=name, align_bytes=64)
+        def zeroed_planes(name, count, width, engine):
+            tile = held.tile([P, count, width], U8, name=name, align_bytes=64)
             engine.memset(tile[:].bitcast(I32), 0)
-            for r in range(4):
-                nc.sync.dma_start(tile[r:P:32, :, :].bitcast(I32), rows[r].bitcast(I32))
             return tile
 
-        def load_scales(into, name, engine, hot, cold, first, last):
+        def load_scales(into, tile, hot, cold, first, last):
             source, base = (hot, 0) if first < HOT else (cold, HOT)
             rows = source.rearrange("e s (q r) n -> r q (e s) n", r=4)[:, :, first - base : last - base, :]
-            tile = load_plane(name, rows, engine)
+            for r in range(4):
+                nc.sync.dma_start(tile[r:P:32, :, :].bitcast(I32), rows[r].bitcast(I32))
             for e in range(first, last):
                 into[e] = tile[:, e - first, :]
 
+        w1, s1, w2, s2 = {}, {}, {}, {}
+        s1_12 = zeroed_planes("s1_12", 4, H, nc.vector)
+        s1_8 = zeroed_planes("s1_8", 4, H, nc.vector)
+        identity = held.tile([P, P], F32, name="identity")
+        make_identity(nc, identity[:])
+        s1_3 = zeroed_planes("s1_3", 5, H, nc.gpsimd)
+        s2_3 = zeroed_planes("s2_3", 13, N, nc.gpsimd)
+        hot_packed = held.tile([P, H], U8, name="hot_packed", align_bytes=64)
+        nc.gpsimd.memset(hot_packed[:].bitcast(I32), 0)
+        s2_0 = zeroed_planes("s2_0", 3, N, nc.gpsimd)
+
         token_scales = held.tile([P, T], U8, name="token_scales", align_bytes=64)
+        token_words = held.tile([P, T], I32, name="token_words", align_bytes=64)
+        offsets = held.tile([P, E * C // 16], U16, name="offsets")
         quadrants = x_scales.rearrange("s (q r) t -> q s r t", r=4).bitcast(I32)
         for q in range(4):
             nc.sync.dma_start(
                 token_scales[32 * q : 32 * (q + 1), :].bitcast(I32), quadrants[q].to_broadcast([8, 4, T // 4])
             )
-        w1, s1, w2, s2 = {}, {}, {}, {}
-        engines = {"V": nc.vector, "G": nc.gpsimd}
-        token_words = held.tile([P, T], I32, name="token_words", align_bytes=64)
-        offsets = held.tile([P, E * C // 16], U16, name="offsets")
-        for what in 'owxs':
-            if what == "x":
-                nc.sync.dma_start(token_words[:], x_words.rearrange("s p t d -> p (s t d)").bitcast(I32))
-            if what == "o":
-                nc.sync.dma_start(offsets[:], offs)
-            if what == "w":
-                load_words(w1, "room_a", w1h_words, w1c_words, 14, 16)
-            if what == "s":
-                load_scales(s1, "room_c", nc.gpsimd, w1h_scales, w1c_scales, 12, 16)
-        load_words(w1, "room_b", w1h_words, w1c_words, 12, 14)
-        identity = held.tile([P, P], F32, name="identity")
-        make_identity(nc, identity[:])
-        load_scales(s1, "s1_cold", engines['GGGG'[0]], w1h_scales, w1c_scales, HOT, 12)
-        load_scales(s2, "s2_cold", engines['GGGG'[1]], w2h_scales, w2c_scales, HOT, E)
-        load_scales(s1, "s1_hot", engines['GGGG'[2]], w1h_scales, w1c_scales, 0, HOT)
-        load_scales(s2, "s2_hot", engines['GGGG'[3]], w2h_scales, w2c_scales, 0, HOT)
-        later_loads = {14: [(2, 'room_a', 3, 16)], 15: [(1, 'room_e', 8, 12)], 12: [(1, 'room_b', 3, 8), (2, 'room_c', 0, 3)], 8: [(1, 'room_e', 0, 3)]}
+        nc.sync.dma_start(offsets[:], offs)
+        nc.sync.dma_start(token_words[:], x_words.rearrange("s p t d -> p (s t d)").bitcast(I32))
+        load_words(w1, "w1_14", w1h_words, w1c_words, 14, 16)
+        load_scales(s1, s1_12, w1h_scales, w1c_scales, 12, 16)
+        load_words(w1, "w1_12", w1h_words, w1c_words, 12, 14)
+        load_words(w1, "w1_8", w1h_words, w1c_words, 8, 12)
+        load_scales(s1, s1_8, w1h_scales, w1c_scales, 8, 12)
+        load_words(w1, "w1_3", w1h_words, w1c_words, 3, 8)
+        load_scales(s1, s1_3, w1h_scales, w1c_scales, 3, 8)
+        load_scales(s2, s2_3, w2h_scales, w2c_scales, 3, 16)
+        load_words(w2, "w2_3", w2h_words, w2c_words, 3, 16)
+        hot_rows = w1h_scales.rearrange("e s (q r) n -> q (e s) r n", r=4).bitcast(I32)
+        for q in range(4):
+            nc.sync.dma_start(hot_packed[32 * q : 32 * q + 4 * HOT, :].bitcast(I32), hot_rows[q])
+        load_words(w1, "w1_0", w1h_words, w1c_words, 0, 3)
+        load_scales(s2, s2_0, w2h_scales, w2c_scales, 0, 3)
+        load_words(w2, "w2_0", w2h_words, w2c_words, 0, 3)
 
-        def codes_of(words, e, first, last):
-            if e < HOT:
-                return words[:, 4 * first : 4 * last].bitcast(FP8X4)
-            return words[:, 2 * first : 2 * last].bitcast(FP4X4)
+        def codes_of(words, e):
+            return words.bitcast(FP8X4 if e < HOT else FP4X4)
 
         slot_words, slot_scales = {}, {}
 
-        def gather(first, last):
-            listed = offsets[:, first * C // 16 : last * C // 16]
-            words = stream.tile([P, (last - first) * C], U32, name="slot_words", bufs=3, align_bytes=64)
-            scales = stream.tile([P, (last - first) * C], U8, name="slot_scales", bufs=3, align_bytes=64)
+        def gather(number):
+            first, last = GATHERS[number]
+            listed = offsets[:, first // 16 : last // 16]
+            room = GATHER_ROOMS[number]
+            words = held.tile([P, last - first], U32, name="slot_words_%d" % room, align_bytes=64)
+            scales = held.tile([P, last - first], U8, name="slot_scales_%d" % room, align_bytes=64)
             nc.vector.tensor_copy(words[:], token_words[:].bitcast(U32).indirect(listed))
             nc.vector.tensor_copy(scales[:], token_scales[:].indirect(listed))
-            for e in range(first, last):
-                slot_words[e] = words[:, (e - first) * C : (e - first + 1) * C]
-                slot_scales[e] = scales[:, (e - first) * C : (e - first + 1) * C]
+            for s in range(first, last, P):
+                slot_words[s // P] = words[:, s - first : s - first + P]
+                slot_scales[s // P] = scales[:, s - first : s - first + P]
 
-        hidden, turned, grouped = {}, {}, {}
+        hidden, turned, grouped, group_tile, quantised = {}, {}, {}, {}, {}
 
-        def reorder_scales(e, engine):
-            plane = held.tile([P, H], U8, name="plane_%d" % e, align_bytes=64)
-            engine.tensor_copy(plane[:].rearrange("p (t m) -> p t m", t=4), s1[e].rearrange("p (m t) -> p t m", t=4))
-            s1[e] = plane[:]
+        def bank(number, shape):
+            return psum.tile(shape, F32, name="bank_%d" % number)
 
-        def reorder_words(e, engine):
-            tile, place = w1[e]
-            word = U32 if e < HOT else U16
-            words = ring.tile([P, 1, tile.shape[2]], U8, name="hot_words" if e < HOT else "cold_words", bufs=3 if e < HOT else 2, align_bytes=64)
-            engine.tensor_copy(
-                words[:, 0, :].bitcast(word).rearrange("p (t m) -> p t m", t=4),
-                tile[:, place, :].bitcast(word).rearrange("p (m t) -> p t m", t=4),
+        def first_layer(e):
+            hidden[e] = ring.tile([P, 2, 2, P, 2], BF16, name="hidden", align_bytes=64)
+            for j in (1, 0):
+                sums = bank((2 * e + j) % 4, [P, H])
+                nc.tensor.matmul_mx(
+                    out=sums[:],
+                    lhsT=slot_words[2 * e + j].bitcast(FP8X4),
+                    lhsT_scale=slot_scales[2 * e + j],
+                    rhs=codes_of(w1[e], e),
+                    rhs_scale=s1[e],
+                    start=True,
+                    stop=True,
+                )
+                read = sums[:].rearrange("s (p u v) -> s u p v", u=2, v=2)
+                if (e, j) in VECTOR_RELU:
+                    nc.vector.tensor_scalar_max(hidden[e][:, j], read, 0.0)
+                else:
+                    nc.scalar.activation(hidden[e][:, j], read, RELU)
+
+        def reorder_hot_scales():
+            plane = held.tile([P, H], U8, name="hot_plane", align_bytes=64)
+            nc.vector.tensor_copy(
+                plane[:].rearrange("p (t m) -> p t m", t=4), hot_packed[:].rearrange("p (m t) -> p t m", t=4)
             )
-            w1[e] = (words, 0)
+            for e in range(HOT):
+                s1[e] = plane[4 * e : P, :]
 
-        def relu(e, j, written, sums):
-            if (e, j) in [(1, 0), (1, 1), (2, 0), (10, 0), (15, 0)]:
-                nc.vector.tensor_scalar_max(written, sums, 0.0)
-            else:
-                nc.scalar.activation(written, sums, RELU)
+        def reorder_hot_words(e):
+            words = held.tile([P, H], U32, name="hot_words_%d" % e, align_bytes=64)
+            nc.vector.tensor_copy(
+                words[:].rearrange("p (t m) -> p t m", t=4), w1[e].bitcast(U32).rearrange("p (m t) -> p t m", t=4)
+            )
+            w1[e] = words[:]
 
-        def first_layer_weights_stationary(e):
-            tile, place = w1[e]
-            for j in range(2):
-                sums = psum.tile([P, 4, P], F32, name="sums", bufs=4)
+        def first_layer_hot(e):
+            for j in (1, 0):
+                sums = bank((2 * e + j) % 4, [P, 4, P])
                 for t in range(4):
                     nc.tensor.matmul_mx(
                         out=sums[:, t, :],
-                        lhsT=codes_of(tile[:, place, :], e, t * P, (t + 1) * P),
+                        lhsT=w1[e][:, t * P : (t + 1) * P].bitcast(FP8X4),
                         lhsT_scale=s1[e][:, t * P : (t + 1) * P],
-                        rhs=slot_words[e][:, j * P : (j + 1) * P].bitcast(FP8X4),
-                        rhs_scale=slot_scales[e][:, j * P : (j + 1) * P],
+                        rhs=slot_words[2 * e + j].bitcast(FP8X4),
+                        rhs_scale=slot_scales[2 * e + j],
                         start=True,
                         stop=True,
                     )
-                relu(e, j, grouped[e][:, j * P : (j + 1) * P, :], sums[:].rearrange("p t s -> p s t"))
+                read = sums[:].rearrange("p t s -> p s t")
+                written = grouped[e][:, j * P : (j + 1) * P, :]
+                if (e, j) in VECTOR_RELU:
+                    nc.vector.tensor_scalar_max(written, read, 0.0)
+                else:
+                    nc.scalar.activation(written, read, RELU)
 
-        def first_layer_tokens_stationary(e):
-            tile, place = w1[e]
-            hidden[e] = ring.tile([P, 2, 2, P, 2], BF16, name="hidden", bufs=2, align_bytes=64)
-            for half in range(2):
-                sums = psum.tile([P, 2, H // 2], F32, name="sums", bufs=4)
-                cols = (half * H // 2, (half + 1) * H // 2)
-                for j in (0, 0, 1) if (e, half) in [] else (0, 1):
-                    nc.tensor.matmul_mx(
-                        out=sums[:, j, :],
-                        lhsT=slot_words[e][:, j * P : (j + 1) * P].bitcast(FP8X4),
-                        lhsT_scale=slot_scales[e][:, j * P : (j + 1) * P],
-                        rhs=codes_of(tile[:, place, :], e, *cols),
-                        rhs_scale=s1[e][:, cols[0] : cols[1]],
-                        start=True,
-                        stop=True,
-                    )
-                relu(
-                    e,
-                    half,
-                    hidden[e][:, :, :, half * 64 : (half + 1) * 64, :].rearrange("s j u p v -> s u j p v"),
-                    sums[:].rearrange("s j (p u v) -> s u j p v", u=2, v=2),
-                )
-
-        def turn(e):
+        def turn(e, number):
             pairs = hidden[e][:].rearrange("s j u p v -> s j u (p v)").bitcast(F32)
-            turned[e] = psum.tile([P, 2, C], F32, name="turned", bufs=2)
+            turned[e] = bank(number, [P, 2, C])
             for j in range(2):
                 for u in range(2):
                     nc.tensor.transpose(turned[e][:, u, j * P : (j + 1) * P], pairs[:, j, u, :], identity[:])
 
-        def interleave(e):
-            copy = nc.vector.tensor_copy if e in [4, 6] else nc.scalar.copy
+        def weave(e):
+            copy = nc.vector.tensor_copy if e in VECTOR_WEAVE else nc.scalar.copy
             copy(
                 grouped[e].rearrange("p c t -> p (c t)").bitcast(F32).rearrange("p (c u) -> p c u", u=2),
                 turned[e][:].rearrange("p u c -> p c u"),
             )
 
-        def second_layer(first, last):
+        def quantise(first, last):
             count = last - first
-            h_codes = ring.tile([P, count * C], U32, name="h_codes", align_bytes=64)
-            h_scales = ring.tile([P, count * C], U8, name="h_scales", align_bytes=64)
+            h_codes = ring.tile([P, count * C], U32, name="h_codes", bufs=9, align_bytes=64)
+            h_scales = ring.tile([P, count * C], U8, name="h_scales", bufs=9, align_bytes=64)
             nc.vector.quantize_mx(
                 out=h_codes[:].bitcast(FP8X4),
                 scales=h_scales[:],
                 in_=group_tile[first][:].rearrange("p c t -> p (c t)"),
             )
-            results = psum.tile([P, count * C], F32, name="results", bufs=2)
+            quantised[first] = (h_codes, h_scales)
+
+        def second_layer(first, last, number):
+            count = last - first
+            h_codes, h_scales = quantised[first]
+            results = bank(number, [P, count * C])
             for e in range(first, last):
-                tile, place = w2[e]
                 slots = slice((e - first) * C, (e - first + 1) * C)
                 nc.tensor.matmul_mx(
                     out=results[:, slots],
-                    lhsT=codes_of(tile[:, place, :], e, 0, N),
+                    lhsT=codes_of(w2[e], e),
                     lhsT_scale=s2[e],
                     rhs=h_codes[:, slots].bitcast(FP8X4),
                     rhs_scale=h_scales[:, slots],
                     start=True,
                     stop=True,
                 )
-            staged = ring.tile([P, count * C], F32, name="staged")
-            copy = nc.vector.tensor_copy if first in [0, 10, 12] else nc.scalar.copy
+            staged = ring.tile([P, count * C], F32, name="staged", bufs=9)
+            copy = nc.scalar.copy if first in SCALAR_OUT else nc.vector.tensor_copy
             copy(staged[:], results[:])
             nc.sync.dma_start(out[:, first * C : last * C], staged[:])
 
-        group_tile = {}
-        if 'G' == "G":
-            for e in sorted(REORDERED, reverse=True):
-                if e >= HOT:
-                    reorder_scales(e, nc.gpsimd)
-        gather(*GATHERS[0])
-        for step in range(E + 4):
+        issued = 0
+        tenants = 0
+        for step in range(E + 2):
             e = E - 1 - step
-            for (first, last), coming in zip(GATHERS, GATHERS[1:]):
-                if e == last - 1:
-                    gather(*coming)
-                    for other in range(coming[1] - 1, coming[0] - 1, -1):
-                        if other in REORDERED:
-                            if other >= HOT or 'G' == "V":
-                                if other < HOT or 'G' == "V":
-                                    reorder_scales(other, nc.vector)
-                                reorder_words(other, nc.vector)
+            while issued < len(GATHERS) and GATHERS[issued][1] > (e - 2) * C:
+                gather(issued)
+                issued = issued + 1
             for first, last in GROUPS:
                 if e == last - 1:
-                    group_tile[first] = ring.tile([P, (last - first) * C, 4], BF16, name="grouped", bufs=3, align_bytes=64)
+                    group_tile[first] = ring.tile([P, (last - first) * C, 4], BF16, name="grouped", bufs=9, align_bytes=64)
                     for other in range(first, last):
                         grouped[other] = group_tile[first][:, (other - first) * C : (other - first + 1) * C, :]
-            if e >= 0:
-                if e in REORDERED:
-                    first_layer_weights_stationary(e)
-                else:
-                    first_layer_tokens_stationary(e)
-                for into, room, first, last in later_loads.get(e, []):
-                    if into == 1:
-                        load_words(w1, room, w1h_words, w1c_words, first, last)
-                        if first == 0 and 'G' == "G":
-                            for other in range(HOT - 1, -1, -1):
-                                if other in REORDERED:
-                                    reorder_scales(other, nc.gpsimd)
-                                    reorder_words(other, nc.gpsimd)
-                    else:
-                        load_words(w2, room, w2h_words, w2c_words, first, last)
-            if 0 <= e + 1 < E and e + 1 not in REORDERED:
-                turn(e + 1)
-            if 0 <= e + 2 < E and e + 2 not in REORDERED:
-                interleave(e + 2)
+            if e == HOT + 2:
+                reorder_hot_scales()
+                for other in reversed(range(HOT)):
+                    reorder_hot_words(other)
+            if e >= HOT:
+                first_layer(e)
+            elif e >= 0:
+                first_layer_hot(e)
+            if HOT <= e + 1 < E:
+                turn(e + 1, 4 + tenants % 4)
+                tenants = tenants + 1
+                weave(e + 1)
             for first, last in GROUPS:
-                if first == e + 4:
-                    second_layer(first, last)
+                if first == e + (1 if first >= HOT else 0):
+                    quantise(first, last)
+                if first == e + 7:
+                    second_layer(first, last, 4 + tenants % 4)
+                    tenants = tenants + 1
+        for number, (first, last) in enumerate([group for group in GROUPS if group[0] < 7 - 2]):
+            second_layer(first, last, 4 + (tenants + number) % 4)

@@ -17,8 +17,8 @@ FP4X4 = mybir.dt.float4_e2m1fn_x4
 RELU = mybir.ActivationFunctionType.Relu
 
 P = 128
-GATHERS = [(3968, 4096),(3840, 3968),(3712, 3840),(3584, 3712),(3328, 3584),(3072, 3328),(2816, 3072),(2560, 2816),(2304, 2560),(2048, 2304),(1792, 2048),(1536, 1792),(1280, 1536),(1024, 1280),(768, 1024),(512, 768),(256, 512),(0, 256)]
-GATHER_ROOMS = [0,1,2,3,0,1,2,3,0,1,2,3,0,1,2,3,0,1]
+GATHERS = [(3968, 4096),(3840, 3968),(3584, 3840),(3328, 3584),(3072, 3328),(2560, 3072),(2048, 2560),(1536, 2048),(1024, 1536),(512, 1024),(0, 512)]
+GATHER_ROOMS = [0,1,2,0,1,2,0,1,2,0,1]
 GROUPS = [(14, 16), (12, 14), (10, 12), (8, 10), (6, 8), (4, 6), (2, 4), (1, 2), (0, 1)]
 VECTOR_RELU = [(0,0),(1,0),(2,0)]
 VECTOR_WEAVE = []

@@ -17,9 +17,11 @@ FP4X4 = mybir.dt.float4_e2m1fn_x4
 RELU = mybir.ActivationFunctionType.Relu
 
 P = 128
+REORDERED = 3
 GATHERS = [(3968, 4096),(3840, 3968),(3584, 3840),(3328, 3584),(3072, 3328),(2560, 3072),(2048, 2560),(1536, 2048),(1024, 1536),(512, 1024),(0, 512)]
 GATHER_ROOMS = [0,1,2,0,1,2,0,1,2,0,1]
 GROUPS = [(14, 16), (12, 14), (10, 12), (8, 10), (6, 8), (4, 6), (2, 4), (1, 2), (0, 1)]
+QUANTISED = [(12,16),(8,12),(6,8),(4,6),(2,4),(1,2),(0,1)]
 VECTOR_RELU = [(0,0),(1,0),(2,0)]
 VECTOR_WEAVE = []
 SCALAR_OUT = [14,10,6,2,0]
@@ -91,6 +93,8 @@ def tile_moe_hot_s_mlp_relu_kernel(
         hot_rows = w1h_scales.rearrange("e s (q r) n -> q (e s) r n", r=4).bitcast(I32)
         for q in range(4):
             nc.sync.dma_start(hot_packed[32 * q : 32 * q + 4 * HOT, :].bitcast(I32), hot_rows[q])
+        for e in range(HOT):
+            s1[e] = hot_packed[4 * e : P, :]
         load_words(w1, "w1_0", w1h_words, w1c_words, 0, 3)
         load_scales(s2, s2_0, w2h_scales, w2c_scales, 0, 3)
         load_words(w2, "w2_0", w2h_words, w2c_words, 0, 3)
@@ -141,13 +145,14 @@ def tile_moe_hot_s_mlp_relu_kernel(
             nc.vector.tensor_copy(
                 plane[:].rearrange("p (t m) -> p t m", t=4), hot_packed[:].rearrange("p (m t) -> p t m", t=4)
             )
-            for e in range(HOT):
+            for e in range(REORDERED):
                 s1[e] = plane[4 * e : P, :]
 
         def reorder_hot_words(e):
             words = held.tile([P, H], U32, name="hot_words_%d" % e, align_bytes=64)
             nc.vector.tensor_copy(
-                words[:].rearrange("p (t m) -> p t m", t=4), w1[e].bitcast(U32).rearrange("p (m t) -> p t m", t=4)
+                words[:].rearrange("p (t b m) -> p b t m", t=4, m=4),
+                w1[e].bitcast(U32).rearrange("p (b m t) -> p b t m", t=4, m=4),
             )
             w1[e] = words[:]
 
@@ -194,11 +199,12 @@ def tile_moe_hot_s_mlp_relu_kernel(
                 scales=h_scales[:],
                 in_=group_tile[first][:].rearrange("p c t -> p (c t)"),
             )
-            quantised[first] = (h_codes, h_scales)
+            for e in range(first, last):
+                slots = slice((e - first) * C, (e - first + 1) * C)
+                quantised[e] = (h_codes[:, slots], h_scales[:, slots])
 
         def second_layer(first, last, number):
             count = last - first
-            h_codes, h_scales = quantised[first]
             results = bank(number, [P, count * C])
             for e in range(first, last):
                 slots = slice((e - first) * C, (e - first + 1) * C)
@@ -206,8 +212,8 @@ def tile_moe_hot_s_mlp_relu_kernel(
                     out=results[:, slots],
                     lhsT=codes_of(w2[e], e),
                     lhsT_scale=s2[e],
-                    rhs=h_codes[:, slots].bitcast(FP8X4),
-                    rhs_scale=h_scales[:, slots],
+                    rhs=quantised[e][0].bitcast(FP8X4),
+                    rhs_scale=quantised[e][1],
                     start=True,
                     stop=True,
                 )
@@ -223,28 +229,29 @@ def tile_moe_hot_s_mlp_relu_kernel(
             while issued < len(GATHERS) and GATHERS[issued][1] > (e - 2) * C:
                 gather(issued)
                 issued = issued + 1
-            for first, last in GROUPS:
+            for first, last in QUANTISED:
                 if e == last - 1:
                     group_tile[first] = ring.tile([P, (last - first) * C, 4], BF16, name="grouped", bufs=9, align_bytes=64)
                     for other in range(first, last):
                         grouped[other] = group_tile[first][:, (other - first) * C : (other - first + 1) * C, :]
-            if e == HOT + 2:
+            if REORDERED > 0 and e == REORDERED + 2:
                 reorder_hot_scales()
-                for other in reversed(range(HOT)):
+                for other in reversed(range(REORDERED)):
                     reorder_hot_words(other)
-            if e >= HOT:
+            if e >= REORDERED:
                 first_layer(e)
             elif e >= 0:
                 first_layer_hot(e)
-            if HOT <= e + 1 < E:
+            if REORDERED <= e + 1 < E:
                 turn(e + 1, 4 + tenants % 4)
                 tenants = tenants + 1
                 weave(e + 1)
-            for first, last in GROUPS:
-                if first == e + (1 if first >= HOT else 0):
+            for first, last in QUANTISED:
+                if first == e + (1 if first >= REORDERED else 0):
                     quantise(first, last)
-                if first == e + 7:
+            for first, last in GROUPS:
+                if first == e + (7 if first >= 8 else 5):
                     second_layer(first, last, 4 + tenants % 4)
                     tenants = tenants + 1
-        for number, (first, last) in enumerate([group for group in GROUPS if group[0] < 7 - 2]):
+        for number, (first, last) in enumerate([group for group in GROUPS if group[0] < 5 - 2]):
             second_layer(first, last, 4 + (tenants + number) % 4)

@@ -17,14 +17,18 @@ FP4X4 = mybir.dt.float4_e2m1fn_x4
 RELU = mybir.ActivationFunctionType.Relu
 
 P = 128
-REORDERED = 3
-GATHERS = [(3968, 4096),(3840, 3968),(3584, 3840),(3328, 3584),(3072, 3328),(2560, 3072),(2048, 2560),(1536, 2048),(1024, 1536),(512, 1024),(0, 512)]
-GATHER_ROOMS = [0,1,2,0,1,2,0,1,2,0,1]
-GROUPS = [(14, 16), (12, 14), (10, 12), (8, 10), (6, 8), (4, 6), (2, 4), (1, 2), (0, 1)]
-QUANTISED = [(12,16),(8,12),(6,8),(4,6),(2,4),(1,2),(0,1)]
-VECTOR_RELU = [(0,0),(1,0),(2,0)]
-VECTOR_WEAVE = []
-SCALAR_OUT = [14,10,6,2,0]
+
+GATHER_WIDTHS = [P, P] + [C] * 3 + [2 * C] * 6
+GATHER_ROOMS = 3
+GATHER_AHEAD = 2
+
+QUANTISED = [(12, 16), (8, 12), (6, 8), (4, 6), (2, 4), (1, 2)]
+STORED = [(14, 16), (12, 14), (10, 12), (8, 10), (6, 8), (4, 6), (2, 4), (1, 2)]
+SCALAR_SHARE = 3
+LAG_EARLY, LAG_LATE, EARLY_FROM = 7, 4, 8
+
+SUM_BANKS = 4
+SHARED_BANKS = 4
 
 
 def tile_moe_hot_s_mlp_relu_kernel(
@@ -36,6 +40,8 @@ def tile_moe_hot_s_mlp_relu_kernel(
         held = ctx.enter_context(tc.tile_pool(name="held", bufs=1))
         ring = ctx.enter_context(tc.tile_pool(name="ring", bufs=3))
         psum = ctx.enter_context(tc.psum_pool(name="psum", bufs=1))
+
+        w1, s1, w2, s2 = {}, {}, {}, {}
 
         def load_words(into, name, hot, cold, first, last):
             if first < HOT:
@@ -60,16 +66,14 @@ def tile_moe_hot_s_mlp_relu_kernel(
             for e in range(first, last):
                 into[e] = tile[:, e - first, :]
 
-        w1, s1, w2, s2 = {}, {}, {}, {}
-        s1_12 = zeroed_planes("s1_12", 4, H, nc.vector)
-        s1_8 = zeroed_planes("s1_8", 4, H, nc.vector)
+        s1_first = zeroed_planes("s1_first", 4, H, nc.vector)
+        s1_second = zeroed_planes("s1_second", 4, H, nc.vector)
         identity = held.tile([P, P], F32, name="identity")
         make_identity(nc, identity[:])
-        s1_3 = zeroed_planes("s1_3", 5, H, nc.gpsimd)
-        s2_3 = zeroed_planes("s2_3", 13, N, nc.gpsimd)
-        hot_packed = held.tile([P, H], U8, name="hot_packed", align_bytes=64)
-        nc.gpsimd.memset(hot_packed[:].bitcast(I32), 0)
-        s2_0 = zeroed_planes("s2_0", 3, N, nc.gpsimd)
+        s1_third = zeroed_planes("s1_third", 5, H, nc.gpsimd)
+        s2_cold = zeroed_planes("s2_cold", E - HOT, N, nc.gpsimd)
+        hot_packed = zeroed_planes("hot_packed", 1, H, nc.gpsimd)
+        s2_hot = zeroed_planes("s2_hot", HOT, N, nc.gpsimd)
 
         token_scales = held.tile([P, T], U8, name="token_scales", align_bytes=64)
         token_words = held.tile([P, T], I32, name="token_words", align_bytes=64)
@@ -81,33 +85,40 @@ def tile_moe_hot_s_mlp_relu_kernel(
             )
         nc.sync.dma_start(offsets[:], offs)
         nc.sync.dma_start(token_words[:], x_words.rearrange("s p t d -> p (s t d)").bitcast(I32))
-        load_words(w1, "w1_14", w1h_words, w1c_words, 14, 16)
-        load_scales(s1, s1_12, w1h_scales, w1c_scales, 12, 16)
-        load_words(w1, "w1_12", w1h_words, w1c_words, 12, 14)
-        load_words(w1, "w1_8", w1h_words, w1c_words, 8, 12)
-        load_scales(s1, s1_8, w1h_scales, w1c_scales, 8, 12)
-        load_words(w1, "w1_3", w1h_words, w1c_words, 3, 8)
-        load_scales(s1, s1_3, w1h_scales, w1c_scales, 3, 8)
-        load_scales(s2, s2_3, w2h_scales, w2c_scales, 3, 16)
-        load_words(w2, "w2_3", w2h_words, w2c_words, 3, 16)
+
+        load_words(w1, "w1_first", w1h_words, w1c_words, 14, 16)
+        load_scales(s1, s1_first, w1h_scales, w1c_scales, 12, 16)
+        load_words(w1, "w1_second", w1h_words, w1c_words, 12, 14)
+        load_words(w1, "w1_third", w1h_words, w1c_words, 8, 12)
+        load_scales(s1, s1_second, w1h_scales, w1c_scales, 8, 12)
+        load_words(w1, "w1_fourth", w1h_words, w1c_words, HOT, 8)
+        load_scales(s1, s1_third, w1h_scales, w1c_scales, HOT, 8)
+        load_scales(s2, s2_cold, w2h_scales, w2c_scales, HOT, E)
+        load_words(w2, "w2_cold", w2h_words, w2c_words, HOT, E)
         hot_rows = w1h_scales.rearrange("e s (q r) n -> q (e s) r n", r=4).bitcast(I32)
         for q in range(4):
-            nc.sync.dma_start(hot_packed[32 * q : 32 * q + 4 * HOT, :].bitcast(I32), hot_rows[q])
-        for e in range(HOT):
-            s1[e] = hot_packed[4 * e : P, :]
-        load_words(w1, "w1_0", w1h_words, w1c_words, 0, 3)
-        load_scales(s2, s2_0, w2h_scales, w2c_scales, 0, 3)
-        load_words(w2, "w2_0", w2h_words, w2c_words, 0, 3)
+            nc.sync.dma_start(hot_packed[32 * q : 32 * q + 4 * HOT, 0, :].bitcast(I32), hot_rows[q])
+        load_words(w1, "w1_hot", w1h_words, w1c_words, 0, HOT)
+        load_scales(s2, s2_hot, w2h_scales, w2c_scales, 0, HOT)
+        load_words(w2, "w2_hot", w2h_words, w2c_words, 0, HOT)
 
         def codes_of(words, e):
             return words.bitcast(FP8X4 if e < HOT else FP4X4)
 
+        def sum_bank(e, half, shape):
+            return psum.tile(shape, F32, name="bank_%d" % ((2 * e + half) % SUM_BANKS))
+
+        tenants = []
+
+        def shared_bank(shape):
+            tenants.append(psum.tile(shape, F32, name="bank_%d" % (SUM_BANKS + len(tenants) % SHARED_BANKS)))
+            return tenants[-1]
+
         slot_words, slot_scales = {}, {}
 
-        def gather(number):
-            first, last = GATHERS[number]
+        def gather(number, first, last):
             listed = offsets[:, first // 16 : last // 16]
-            room = GATHER_ROOMS[number]
+            room = number % GATHER_ROOMS
             words = held.tile([P, last - first], U32, name="slot_words_%d" % room, align_bytes=64)
             scales = held.tile([P, last - first], U8, name="slot_scales_%d" % room, align_bytes=64)
             nc.vector.tensor_copy(words[:], token_words[:].bitcast(U32).indirect(listed))
@@ -116,142 +127,140 @@ def tile_moe_hot_s_mlp_relu_kernel(
                 slot_words[s // P] = words[:, s - first : s - first + P]
                 slot_scales[s // P] = scales[:, s - first : s - first + P]
 
-        hidden, turned, grouped, group_tile, quantised = {}, {}, {}, {}, {}
+        grouped, group_tile = {}, {}
+        hidden, quantised = {}, {}
 
-        def bank(number, shape):
-            return psum.tile(shape, F32, name="bank_%d" % number)
-
-        def first_layer(e):
+        def first_layer_cold(e):
             hidden[e] = ring.tile([P, 2, 2, P, 2], BF16, name="hidden", align_bytes=64)
-            for j in (1, 0):
-                sums = bank((2 * e + j) % 4, [P, H])
+            for half in (1, 0):
+                sums = sum_bank(e, half, [P, H])
                 nc.tensor.matmul_mx(
                     out=sums[:],
-                    lhsT=slot_words[2 * e + j].bitcast(FP8X4),
-                    lhsT_scale=slot_scales[2 * e + j],
+                    lhsT=slot_words[2 * e + half].bitcast(FP8X4),
+                    lhsT_scale=slot_scales[2 * e + half],
                     rhs=codes_of(w1[e], e),
                     rhs_scale=s1[e],
                     start=True,
                     stop=True,
                 )
-                read = sums[:].rearrange("s (p u v) -> s u p v", u=2, v=2)
-                if (e, j) in VECTOR_RELU:
-                    nc.vector.tensor_scalar_max(hidden[e][:, j], read, 0.0)
-                else:
-                    nc.scalar.activation(hidden[e][:, j], read, RELU)
+                nc.scalar.activation(hidden[e][:, half], sums[:].rearrange("s (p u v) -> s u p v", u=2, v=2), RELU)
 
-        def reorder_hot_scales():
+        def turn_and_weave(e):
+            pairs = hidden[e][:].rearrange("s half u p v -> s half u (p v)").bitcast(F32)
+            turned = shared_bank([P, 2, C])
+            for half in range(2):
+                for u in range(2):
+                    nc.tensor.transpose(turned[:, u, half * P : (half + 1) * P], pairs[:, half, u, :], identity[:])
+            nc.scalar.copy(
+                grouped[e].rearrange("p c t -> p (c t)").bitcast(F32).rearrange("p (c u) -> p c u", u=2),
+                turned[:].rearrange("p u c -> p c u"),
+            )
+
+        def reorder_hot():
             plane = held.tile([P, H], U8, name="hot_plane", align_bytes=64)
             nc.vector.tensor_copy(
-                plane[:].rearrange("p (t m) -> p t m", t=4), hot_packed[:].rearrange("p (m t) -> p t m", t=4)
+                plane[:].rearrange("p (t m) -> p t m", t=4), hot_packed[:, 0, :].rearrange("p (m t) -> p t m", t=4)
             )
-            for e in range(REORDERED):
+            for e in reversed(range(HOT)):
                 s1[e] = plane[4 * e : P, :]
-
-        def reorder_hot_words(e):
-            words = held.tile([P, H], U32, name="hot_words_%d" % e, align_bytes=64)
-            nc.vector.tensor_copy(
-                words[:].rearrange("p (t b m) -> p b t m", t=4, m=4),
-                w1[e].bitcast(U32).rearrange("p (b m t) -> p b t m", t=4, m=4),
-            )
-            w1[e] = words[:]
+                words = held.tile([P, H], U32, name="hot_words_%d" % e, align_bytes=64)
+                nc.vector.tensor_copy(
+                    words[:].rearrange("p (t b n) -> p b t n", t=4, n=4),
+                    w1[e].bitcast(U32).rearrange("p (b n t) -> p b t n", t=4, n=4),
+                )
+                w1[e] = words[:]
 
         def first_layer_hot(e):
-            for j in (1, 0):
-                sums = bank((2 * e + j) % 4, [P, 4, P])
+            for half in (1, 0):
+                sums = sum_bank(e, half, [P, 4, P])
                 for t in range(4):
                     nc.tensor.matmul_mx(
                         out=sums[:, t, :],
                         lhsT=w1[e][:, t * P : (t + 1) * P].bitcast(FP8X4),
                         lhsT_scale=s1[e][:, t * P : (t + 1) * P],
-                        rhs=slot_words[2 * e + j].bitcast(FP8X4),
-                        rhs_scale=slot_scales[2 * e + j],
+                        rhs=slot_words[2 * e + half].bitcast(FP8X4),
+                        rhs_scale=slot_scales[2 * e + half],
                         start=True,
                         stop=True,
                     )
                 read = sums[:].rearrange("p t s -> p s t")
-                written = grouped[e][:, j * P : (j + 1) * P, :]
-                if (e, j) in VECTOR_RELU:
+                written = grouped[e][:, half * P : (half + 1) * P, :]
+                if half == 0 and e > 0:
                     nc.vector.tensor_scalar_max(written, read, 0.0)
                 else:
                     nc.scalar.activation(written, read, RELU)
 
-        def turn(e, number):
-            pairs = hidden[e][:].rearrange("s j u p v -> s j u (p v)").bitcast(F32)
-            turned[e] = bank(number, [P, 2, C])
-            for j in range(2):
-                for u in range(2):
-                    nc.tensor.transpose(turned[e][:, u, j * P : (j + 1) * P], pairs[:, j, u, :], identity[:])
-
-        def weave(e):
-            copy = nc.vector.tensor_copy if e in VECTOR_WEAVE else nc.scalar.copy
-            copy(
-                grouped[e].rearrange("p c t -> p (c t)").bitcast(F32).rearrange("p (c u) -> p c u", u=2),
-                turned[e][:].rearrange("p u c -> p c u"),
-            )
-
-        def quantise(first, last):
-            count = last - first
-            h_codes = ring.tile([P, count * C], U32, name="h_codes", bufs=9, align_bytes=64)
-            h_scales = ring.tile([P, count * C], U8, name="h_scales", bufs=9, align_bytes=64)
+        def quantise(name, values):
+            columns = values.shape[1]
+            codes = held.tile([P, columns], U32, name=name + "_codes", align_bytes=64)
+            scales = held.tile([P, columns], U8, name=name + "_scales", align_bytes=64)
             nc.vector.quantize_mx(
-                out=h_codes[:].bitcast(FP8X4),
-                scales=h_scales[:],
-                in_=group_tile[first][:].rearrange("p c t -> p (c t)"),
+                out=codes[:].bitcast(FP8X4), scales=scales[:], in_=values.rearrange("p c t -> p (c t)")
             )
-            for e in range(first, last):
-                slots = slice((e - first) * C, (e - first + 1) * C)
-                quantised[e] = (h_codes[:, slots], h_scales[:, slots])
+            return codes, scales
 
-        def second_layer(first, last, number):
-            count = last - first
-            results = bank(number, [P, count * C])
-            for e in range(first, last):
-                slots = slice((e - first) * C, (e - first + 1) * C)
-                nc.tensor.matmul_mx(
-                    out=results[:, slots],
-                    lhsT=codes_of(w2[e], e),
-                    lhsT_scale=s2[e],
-                    rhs=quantised[e][0].bitcast(FP8X4),
-                    rhs_scale=quantised[e][1],
-                    start=True,
-                    stop=True,
-                )
-            staged = ring.tile([P, count * C], F32, name="staged", bufs=9)
-            copy = nc.scalar.copy if first in SCALAR_OUT else nc.vector.tensor_copy
+        def second_product(results, e, codes, scales):
+            nc.tensor.matmul_mx(
+                out=results,
+                lhsT=codes_of(w2[e], e),
+                lhsT_scale=s2[e],
+                rhs=codes.bitcast(FP8X4),
+                rhs_scale=scales,
+                start=True,
+                stop=True,
+            )
+
+        def store(results, first_slot, copy):
+            columns = results.shape[1]
+            staged = held.tile([P, columns], F32, name="staged_%d" % first_slot)
             copy(staged[:], results[:])
-            nc.sync.dma_start(out[:, first * C : last * C], staged[:])
+            nc.sync.dma_start(out[:, first_slot : first_slot + columns], staged[:])
 
-        issued = 0
-        tenants = 0
-        for step in range(E + 2):
-            e = E - 1 - step
-            while issued < len(GATHERS) and GATHERS[issued][1] > (e - 2) * C:
-                gather(issued)
-                issued = issued + 1
-            for first, last in QUANTISED:
+        def second_layer(number, first, last):
+            results = shared_bank([P, (last - first) * C])
+            for e in range(first, last):
+                second_product(results[:, (e - first) * C : (e - first + 1) * C], e, *quantised[e])
+            store(results, first * C, nc.scalar.copy if number % SCALAR_SHARE == 0 else nc.vector.tensor_copy)
+
+        gathered_from = E * C
+        gathers_written = 0
+        written_groups = 0
+        for e in range(E - 1, -3, -1):
+            while gathered_from > max(e - GATHER_AHEAD, 0) * C:
+                width = GATHER_WIDTHS[gathers_written]
+                gather(gathers_written, gathered_from - width, gathered_from)
+                gathered_from = gathered_from - width
+                gathers_written = gathers_written + 1
+            for first, last in QUANTISED + [(0, 1)]:
                 if e == last - 1:
-                    group_tile[first] = ring.tile([P, (last - first) * C, 4], BF16, name="grouped", bufs=9, align_bytes=64)
+                    group_tile[first] = held.tile(
+                        [P, (last - first) * C, 4], BF16, name="grouped_%d" % first, align_bytes=64
+                    )
                     for other in range(first, last):
                         grouped[other] = group_tile[first][:, (other - first) * C : (other - first + 1) * C, :]
-            if REORDERED > 0 and e == REORDERED + 2:
-                reorder_hot_scales()
-                for other in reversed(range(REORDERED)):
-                    reorder_hot_words(other)
-            if e >= REORDERED:
-                first_layer(e)
+            if e == HOT + GATHER_AHEAD:
+                reorder_hot()
+            if e >= HOT:
+                first_layer_cold(e)
             elif e >= 0:
                 first_layer_hot(e)
-            if REORDERED <= e + 1 < E:
-                turn(e + 1, 4 + tenants % 4)
-                tenants = tenants + 1
-                weave(e + 1)
+            if HOT <= e + 1 < E:
+                turn_and_weave(e + 1)
             for first, last in QUANTISED:
-                if first == e + (1 if first >= REORDERED else 0):
-                    quantise(first, last)
-            for first, last in GROUPS:
-                if first == e + (7 if first >= 8 else 5):
-                    second_layer(first, last, 4 + tenants % 4)
-                    tenants = tenants + 1
-        for number, (first, last) in enumerate([group for group in GROUPS if group[0] < 5 - 2]):
-            second_layer(first, last, 4 + (tenants + number) % 4)
+                if first == e + (1 if first >= HOT else 0):
+                    codes, scales = quantise("h_%d" % first, group_tile[first][:])
+                    for other in range(first, last):
+                        slots = slice((other - first) * C, (other - first + 1) * C)
+                        quantised[other] = (codes[:, slots], scales[:, slots])
+            for number, (first, last) in enumerate(STORED):
+                if first == e + (LAG_EARLY if first >= EARLY_FROM else LAG_LATE):
+                    second_layer(number, first, last)
+                    written_groups = number + 1
+        for number in range(written_groups, len(STORED)):
+            second_layer(number, *STORED[number])
+
+        for half, copy in ((1, nc.scalar.copy), (0, nc.vector.tensor_copy)):
+            codes, scales = quantise("last_%d" % half, grouped[0][:, half * P : (half + 1) * P, :])
+            results = shared_bank([P, P])
+            second_product(results[:], 0, codes[:], scales[:])
+            store(results, half * P, copy)

@@ -18,7 +18,7 @@ RELU = mybir.ActivationFunctionType.Relu
 
 P = 128
 
-GATHER_WIDTHS = [P, P] + [C] * 3 + [2 * C] * 6
+GATHER_WIDTHS = [P, P] + [C] * 3 + [2 * C] * 3 + [3 * C] * 2
 GATHER_ROOMS = 3
 GATHER_AHEAD = 2
 
@@ -185,7 +185,7 @@ def tile_moe_hot_s_mlp_relu_kernel(
                     )
                 read = sums[:].rearrange("p t s -> p s t")
                 written = grouped[e][:, half * P : (half + 1) * P, :]
-                if half == 0 and e > 0:
+                if half == 1 and e > 0:
                     nc.vector.tensor_scalar_max(written, read, 0.0)
                 else:
                     nc.scalar.activation(written, read, RELU)

@@ -17,18 +17,13 @@ FP4X4 = mybir.dt.float4_e2m1fn_x4
 RELU = mybir.ActivationFunctionType.Relu
 
 P = 128
-
-GATHER_WIDTHS = [P, P] + [C] * 3 + [2 * C] * 3 + [3 * C] * 2
-GATHER_ROOMS = 3
-GATHER_AHEAD = 2
-
+BANKS = 8
+TURNED = 2
+GATHER_HALVES = [1, 1, 2, 4, 4, 4, 4, 6, 6]
+REORDER_COUNTS = [1, 1, 2, 2, 2, 2, 1]
 QUANTISED = [(12, 16), (8, 12), (6, 8), (4, 6), (2, 4), (1, 2)]
 STORED = [(14, 16), (12, 14), (10, 12), (8, 10), (6, 8), (4, 6), (2, 4), (1, 2)]
-SCALAR_SHARE = 3
-LAG_EARLY, LAG_LATE, EARLY_FROM = 7, 4, 8
-
-SUM_BANKS = 4
-SHARED_BANKS = 4
+ON_SCALAR = [3, 4, 5, 7]
 
 
 def tile_moe_hot_s_mlp_relu_kernel(
@@ -38,7 +33,6 @@ def tile_moe_hot_s_mlp_relu_kernel(
     nc = tc.nc
     with ExitStack() as ctx:
         held = ctx.enter_context(tc.tile_pool(name="held", bufs=1))
-        ring = ctx.enter_context(tc.tile_pool(name="ring", bufs=3))
         psum = ctx.enter_context(tc.psum_pool(name="psum", bufs=1))
 
         w1, s1, w2, s2 = {}, {}, {}, {}
@@ -51,7 +45,7 @@ def tile_moe_hot_s_mlp_relu_kernel(
             tile = held.tile([P, last - first, rows.shape[2]], U8, name=name, align_bytes=64)
             nc.sync.dma_start(tile[:].bitcast(I32), rows.bitcast(I32))
             for e in range(first, last):
-                into[e] = tile[:, e - first, :]
+                into[e] = (tile, e - first)
 
         def zeroed_planes(name, count, width, engine):
             tile = held.tile([P, count, width], U8, name=name, align_bytes=64)
@@ -64,15 +58,23 @@ def tile_moe_hot_s_mlp_relu_kernel(
             for r in range(4):
                 nc.sync.dma_start(tile[r:P:32, :, :].bitcast(I32), rows[r].bitcast(I32))
             for e in range(first, last):
-                into[e] = tile[:, e - first, :]
+                into[e] = (tile, e - first)
+
+        def rows_of(table, first, last):
+            tile, place = table[first]
+            return tile[:, place : place + last - first, :]
+
+        def row_of(table, e):
+            tile, place = table[e]
+            return tile[:, place, :]
 
         s1_first = zeroed_planes("s1_first", 4, H, nc.vector)
         s1_second = zeroed_planes("s1_second", 4, H, nc.vector)
         identity = held.tile([P, P], F32, name="identity")
         make_identity(nc, identity[:])
         s1_third = zeroed_planes("s1_third", 5, H, nc.gpsimd)
-        s2_cold = zeroed_planes("s2_cold", E - HOT, N, nc.gpsimd)
         hot_packed = zeroed_planes("hot_packed", 1, H, nc.gpsimd)
+        s2_cold = zeroed_planes("s2_cold", E - HOT, N, nc.gpsimd)
         s2_hot = zeroed_planes("s2_hot", HOT, N, nc.gpsimd)
 
         token_scales = held.tile([P, T], U8, name="token_scales", align_bytes=64)
@@ -83,8 +85,8 @@ def tile_moe_hot_s_mlp_relu_kernel(
             nc.sync.dma_start(
                 token_scales[32 * q : 32 * (q + 1), :].bitcast(I32), quadrants[q].to_broadcast([8, 4, T // 4])
             )
-        nc.sync.dma_start(offsets[:], offs)
         nc.sync.dma_start(token_words[:], x_words.rearrange("s p t d -> p (s t d)").bitcast(I32))
+        nc.sync.dma_start(offsets[:], offs)
 
         load_words(w1, "w1_first", w1h_words, w1c_words, 14, 16)
         load_scales(s1, s1_first, w1h_scales, w1c_scales, 12, 16)
@@ -93,53 +95,92 @@ def tile_moe_hot_s_mlp_relu_kernel(
         load_scales(s1, s1_second, w1h_scales, w1c_scales, 8, 12)
         load_words(w1, "w1_fourth", w1h_words, w1c_words, HOT, 8)
         load_scales(s1, s1_third, w1h_scales, w1c_scales, HOT, 8)
-        load_scales(s2, s2_cold, w2h_scales, w2c_scales, HOT, E)
-        load_words(w2, "w2_cold", w2h_words, w2c_words, HOT, E)
         hot_rows = w1h_scales.rearrange("e s (q r) n -> q (e s) r n", r=4).bitcast(I32)
         for q in range(4):
             nc.sync.dma_start(hot_packed[32 * q : 32 * q + 4 * HOT, 0, :].bitcast(I32), hot_rows[q])
         load_words(w1, "w1_hot", w1h_words, w1c_words, 0, HOT)
-        load_scales(s2, s2_hot, w2h_scales, w2c_scales, 0, HOT)
+        load_words(w2, "w2_cold", w2h_words, w2c_words, HOT, E)
+        load_scales(s2, s2_cold, w2h_scales, w2c_scales, HOT, E)
         load_words(w2, "w2_hot", w2h_words, w2c_words, 0, HOT)
+        load_scales(s2, s2_hot, w2h_scales, w2c_scales, 0, HOT)
+
+        ordered_words, ordered_plane = {}, {}
+
+        def reorder_cold(first, last):
+            count = last - first
+            words = held.tile([P, count, 2 * H], U8, name="words_%d" % first, align_bytes=64)
+            planes = held.tile([P, count, H], U8, name="planes_%d" % first, align_bytes=64)
+            nc.gpsimd.tensor_copy(
+                words[:].bitcast(U16).rearrange("p e (t m) -> p e t m", t=4),
+                rows_of(w1, first, last).bitcast(U16).rearrange("p e (m t) -> p e t m", t=4),
+            )
+            nc.gpsimd.tensor_copy(
+                planes[:].rearrange("p e (t m) -> p e t m", t=4),
+                rows_of(s1, first, last).rearrange("p e (m t) -> p e t m", t=4),
+            )
+            for e in range(first, last):
+                ordered_words[e] = words[:, e - first, :]
+                ordered_plane[e] = planes[:, e - first, :]
+
+        last = E - TURNED
+        for count in REORDER_COUNTS:
+            reorder_cold(last - count, last)
+            last = last - count
+        plane = held.tile([P, H], U8, name="hot_plane", align_bytes=64)
+        nc.gpsimd.tensor_copy(
+            plane[:].rearrange("p (t m) -> p t m", t=4), hot_packed[:, 0, :].rearrange("p (m t) -> p t m", t=4)
+        )
+        for e in reversed(range(HOT)):
+            ordered_plane[e] = plane[4 * e : P, :]
+            words = held.tile([P, H], U32, name="hot_words_%d" % e, align_bytes=64)
+            nc.gpsimd.tensor_copy(
+                words[:].rearrange("p (t b n) -> p b t n", t=4, n=4),
+                row_of(w1, e).bitcast(U32).rearrange("p (b n t) -> p b t n", t=4, n=4),
+            )
+            ordered_words[e] = words[:].bitcast(U8)
 
         def codes_of(words, e):
             return words.bitcast(FP8X4 if e < HOT else FP4X4)
 
-        def sum_bank(e, half, shape):
-            return psum.tile(shape, F32, name="bank_%d" % ((2 * e + half) % SUM_BANKS))
-
         tenants = []
 
-        def shared_bank(shape):
-            tenants.append(psum.tile(shape, F32, name="bank_%d" % (SUM_BANKS + len(tenants) % SHARED_BANKS)))
+        def next_bank(shape):
+            tenants.append(psum.tile(shape, F32, name="bank_%d" % (len(tenants) % BANKS)))
             return tenants[-1]
 
         slot_words, slot_scales = {}, {}
-
-        def gather(number, first, last):
-            listed = offsets[:, first // 16 : last // 16]
-            room = number % GATHER_ROOMS
-            words = held.tile([P, last - first], U32, name="slot_words_%d" % room, align_bytes=64)
-            scales = held.tile([P, last - first], U8, name="slot_scales_%d" % room, align_bytes=64)
+        last = 2 * E
+        for halves in GATHER_HALVES:
+            first = last - halves
+            listed = offsets[:, first * P // 16 : last * P // 16]
+            words = held.tile([P, halves * P], U32, name="slot_words_%d" % first, align_bytes=64)
+            scales = held.tile([P, halves * P], U8, name="slot_scales_%d" % first, align_bytes=64)
             nc.vector.tensor_copy(words[:], token_words[:].bitcast(U32).indirect(listed))
             nc.vector.tensor_copy(scales[:], token_scales[:].indirect(listed))
-            for s in range(first, last, P):
-                slot_words[s // P] = words[:, s - first : s - first + P]
-                slot_scales[s // P] = scales[:, s - first : s - first + P]
+            for s in range(first, last):
+                slot_words[s] = words[:, (s - first) * P : (s - first + 1) * P]
+                slot_scales[s] = scales[:, (s - first) * P : (s - first + 1) * P]
+            last = first
 
         grouped, group_tile = {}, {}
-        hidden, quantised = {}, {}
+        for first, last in QUANTISED + [(0, 1)]:
+            tile = held.tile([P, (last - first) * C, 4], BF16, name="grouped_%d" % first, align_bytes=64)
+            group_tile[first] = tile
+            for e in range(first, last):
+                grouped[e] = tile[:, (e - first) * C : (e - first + 1) * C, :]
 
-        def first_layer_cold(e):
-            hidden[e] = ring.tile([P, 2, 2, P, 2], BF16, name="hidden", align_bytes=64)
+        hidden = {}
+
+        def first_layer_turned(e):
+            hidden[e] = held.tile([P, 2, 2, P, 2], BF16, name="hidden_%d" % e, align_bytes=64)
             for half in (1, 0):
-                sums = sum_bank(e, half, [P, H])
+                sums = next_bank([P, H])
                 nc.tensor.matmul_mx(
                     out=sums[:],
                     lhsT=slot_words[2 * e + half].bitcast(FP8X4),
                     lhsT_scale=slot_scales[2 * e + half],
-                    rhs=codes_of(w1[e], e),
-                    rhs_scale=s1[e],
+                    rhs=codes_of(row_of(w1, e), e),
+                    rhs_scale=row_of(s1, e),
                     start=True,
                     stop=True,
                 )
@@ -147,7 +188,7 @@ def tile_moe_hot_s_mlp_relu_kernel(
 
         def turn_and_weave(e):
             pairs = hidden[e][:].rearrange("s half u p v -> s half u (p v)").bitcast(F32)
-            turned = shared_bank([P, 2, C])
+            turned = next_bank([P, 2, C])
             for half in range(2):
                 for u in range(2):
                     nc.tensor.transpose(turned[:, u, half * P : (half + 1) * P], pairs[:, half, u, :], identity[:])
@@ -156,39 +197,31 @@ def tile_moe_hot_s_mlp_relu_kernel(
                 turned[:].rearrange("p u c -> p c u"),
             )
 
-        def reorder_hot():
-            plane = held.tile([P, H], U8, name="hot_plane", align_bytes=64)
-            nc.vector.tensor_copy(
-                plane[:].rearrange("p (t m) -> p t m", t=4), hot_packed[:, 0, :].rearrange("p (m t) -> p t m", t=4)
-            )
-            for e in reversed(range(HOT)):
-                s1[e] = plane[4 * e : P, :]
-                words = held.tile([P, H], U32, name="hot_words_%d" % e, align_bytes=64)
-                nc.vector.tensor_copy(
-                    words[:].rearrange("p (t b n) -> p b t n", t=4, n=4),
-                    w1[e].bitcast(U32).rearrange("p (b n t) -> p b t n", t=4, n=4),
-                )
-                w1[e] = words[:]
-
-        def first_layer_hot(e):
+        def first_layer(e):
+            width = (4 if e < HOT else 2) * P
             for half in (1, 0):
-                sums = sum_bank(e, half, [P, 4, P])
+                sums = next_bank([P, 4, P])
                 for t in range(4):
                     nc.tensor.matmul_mx(
                         out=sums[:, t, :],
-                        lhsT=w1[e][:, t * P : (t + 1) * P].bitcast(FP8X4),
-                        lhsT_scale=s1[e][:, t * P : (t + 1) * P],
+                        lhsT=codes_of(ordered_words[e][:, t * width : (t + 1) * width], e),
+                        lhsT_scale=ordered_plane[e][:, t * P : (t + 1) * P],
                         rhs=slot_words[2 * e + half].bitcast(FP8X4),
                         rhs_scale=slot_scales[2 * e + half],
                         start=True,
                         stop=True,
                     )
-                read = sums[:].rearrange("p t s -> p s t")
-                written = grouped[e][:, half * P : (half + 1) * P, :]
-                if half == 1 and e > 0:
-                    nc.vector.tensor_scalar_max(written, read, 0.0)
-                else:
-                    nc.scalar.activation(written, read, RELU)
+                nc.scalar.activation(
+                    grouped[e][:, half * P : (half + 1) * P, :], sums[:].rearrange("p t s -> p s t"), RELU
+                )
+
+        for e in reversed(range(E)):
+            if e >= E - TURNED:
+                first_layer_turned(e)
+            else:
+                first_layer(e)
+            if E - TURNED <= e + 1 < E:
+                turn_and_weave(e + 1)
 
         def quantise(name, values):
             columns = values.shape[1]
@@ -202,8 +235,8 @@ def tile_moe_hot_s_mlp_relu_kernel(
         def second_product(results, e, codes, scales):
             nc.tensor.matmul_mx(
                 out=results,
-                lhsT=codes_of(w2[e], e),
-                lhsT_scale=s2[e],
+                lhsT=codes_of(row_of(w2, e), e),
+                lhsT_scale=row_of(s2, e),
                 rhs=codes.bitcast(FP8X4),
                 rhs_scale=scales,
                 start=True,
@@ -216,51 +249,21 @@ def tile_moe_hot_s_mlp_relu_kernel(
             copy(staged[:], results[:])
             nc.sync.dma_start(out[:, first_slot : first_slot + columns], staged[:])
 
-        def second_layer(number, first, last):
-            results = shared_bank([P, (last - first) * C])
-            for e in range(first, last):
-                second_product(results[:, (e - first) * C : (e - first + 1) * C], e, *quantised[e])
-            store(results, first * C, nc.scalar.copy if number % SCALAR_SHARE == 0 else nc.vector.tensor_copy)
-
-        gathered_from = E * C
-        gathers_written = 0
-        written_groups = 0
-        for e in range(E - 1, -3, -1):
-            while gathered_from > max(e - GATHER_AHEAD, 0) * C:
-                width = GATHER_WIDTHS[gathers_written]
-                gather(gathers_written, gathered_from - width, gathered_from)
-                gathered_from = gathered_from - width
-                gathers_written = gathers_written + 1
-            for first, last in QUANTISED + [(0, 1)]:
-                if e == last - 1:
-                    group_tile[first] = held.tile(
-                        [P, (last - first) * C, 4], BF16, name="grouped_%d" % first, align_bytes=64
-                    )
-                    for other in range(first, last):
-                        grouped[other] = group_tile[first][:, (other - first) * C : (other - first + 1) * C, :]
-            if e == HOT + GATHER_AHEAD:
-                reorder_hot()
-            if e >= HOT:
-                first_layer_cold(e)
-            elif e >= 0:
-                first_layer_hot(e)
-            if HOT <= e + 1 < E:
-                turn_and_weave(e + 1)
-            for first, last in QUANTISED:
-                if first == e + (1 if first >= HOT else 0):
-                    codes, scales = quantise("h_%d" % first, group_tile[first][:])
-                    for other in range(first, last):
-                        slots = slice((other - first) * C, (other - first + 1) * C)
-                        quantised[other] = (codes[:, slots], scales[:, slots])
+        quantised = {}
+        for low, high in QUANTISED:
+            codes, scales = quantise("h_%d" % low, group_tile[low][:])
+            for e in range(low, high):
+                slots = slice((e - low) * C, (e - low + 1) * C)
+                quantised[e] = (codes[:, slots], scales[:, slots])
             for number, (first, last) in enumerate(STORED):
-                if first == e + (LAG_EARLY if first >= EARLY_FROM else LAG_LATE):
-                    second_layer(number, first, last)
-                    written_groups = number + 1
-        for number in range(written_groups, len(STORED)):
-            second_layer(number, *STORED[number])
+                if low <= first < high:
+                    results = next_bank([P, (last - first) * C])
+                    for e in range(first, last):
+                        second_product(results[:, (e - first) * C : (e - first + 1) * C], e, *quantised[e])
+                    store(results, first * C, nc.scalar.copy if number in ON_SCALAR else nc.vector.tensor_copy)
 
-        for half, copy in ((1, nc.scalar.copy), (0, nc.vector.tensor_copy)):
+        for half, copy in ((1, nc.vector.tensor_copy), (0, nc.scalar.copy)):
             codes, scales = quantise("last_%d" % half, grouped[0][:, half * P : (half + 1) * P, :])
-            results = shared_bank([P, P])
+            results = next_bank([P, P])
             second_product(results[:], 0, codes[:], scales[:])
             store(results, half * P, copy)

@@ -19,11 +19,12 @@ RELU = mybir.ActivationFunctionType.Relu
 P = 128
 BANKS = 8
 TURNED = 2
-GATHER_HALVES = [1, 1, 2, 4, 4, 4, 4, 6, 6]
-REORDER_COUNTS = [1, 1, 2, 2, 2, 2, 1]
+GATHER_HALVES = [1, 1, 2, 2, 2, 4, 4, 4, 4, 4, 4]
+WORD_ROOMS, SCALE_ROOMS = 3, 3
 QUANTISED = [(12, 16), (8, 12), (6, 8), (4, 6), (2, 4), (1, 2)]
 STORED = [(14, 16), (12, 14), (10, 12), (8, 10), (6, 8), (4, 6), (2, 4), (1, 2)]
-ON_SCALAR = [3, 4, 5, 7]
+ON_SCALAR = [0, 1, 4, 5, 6]
+SECOND_BEHIND = {12: 3, 8: 1, 6: 1, 4: 0, 2: 0, 1: 0}
 
 
 def tile_moe_hot_s_mlp_relu_kernel(
@@ -52,11 +53,11 @@ def tile_moe_hot_s_mlp_relu_kernel(
             engine.memset(tile[:].bitcast(I32), 0)
             return tile
 
-        def load_scales(into, tile, hot, cold, first, last):
+        def load_scales(into, tile, hot, cold, first, last, row=0):
             source, base = (hot, 0) if first < HOT else (cold, HOT)
             rows = source.rearrange("e s (q r) n -> r q (e s) n", r=4)[:, :, first - base : last - base, :]
             for r in range(4):
-                nc.sync.dma_start(tile[r:P:32, :, :].bitcast(I32), rows[r].bitcast(I32))
+                nc.sync.dma_start(tile[row + r : P : 32, :, :].bitcast(I32), rows[r].bitcast(I32))
             for e in range(first, last):
                 into[e] = (tile, e - first)
 
@@ -69,11 +70,11 @@ def tile_moe_hot_s_mlp_relu_kernel(
             return tile[:, place, :]
 
         s1_first = zeroed_planes("s1_first", 4, H, nc.vector)
-        s1_second = zeroed_planes("s1_second", 4, H, nc.vector)
+        packed = zeroed_planes("packed", 4, H, nc.vector)
         identity = held.tile([P, P], F32, name="identity")
         make_identity(nc, identity[:])
-        s1_third = zeroed_planes("s1_third", 5, H, nc.gpsimd)
         hot_packed = zeroed_planes("hot_packed", 1, H, nc.gpsimd)
+        unpacked = zeroed_planes("unpacked", 4, H, nc.gpsimd)
         s2_cold = zeroed_planes("s2_cold", E - HOT, N, nc.gpsimd)
         s2_hot = zeroed_planes("s2_hot", HOT, N, nc.gpsimd)
 
@@ -85,53 +86,63 @@ def tile_moe_hot_s_mlp_relu_kernel(
             nc.sync.dma_start(
                 token_scales[32 * q : 32 * (q + 1), :].bitcast(I32), quadrants[q].to_broadcast([8, 4, T // 4])
             )
-        nc.sync.dma_start(token_words[:], x_words.rearrange("s p t d -> p (s t d)").bitcast(I32))
         nc.sync.dma_start(offsets[:], offs)
+        nc.sync.dma_start(token_words[:], x_words.rearrange("s p t d -> p (s t d)").bitcast(I32))
 
         load_words(w1, "w1_first", w1h_words, w1c_words, 14, 16)
         load_scales(s1, s1_first, w1h_scales, w1c_scales, 12, 16)
-        load_words(w1, "w1_second", w1h_words, w1c_words, 12, 14)
-        load_words(w1, "w1_third", w1h_words, w1c_words, 8, 12)
-        load_scales(s1, s1_second, w1h_scales, w1c_scales, 8, 12)
-        load_words(w1, "w1_fourth", w1h_words, w1c_words, HOT, 8)
-        load_scales(s1, s1_third, w1h_scales, w1c_scales, HOT, 8)
+        load_words(w1, "w1_second", w1h_words, w1c_words, 10, 14)
+        load_scales(s1, packed, w1h_scales, w1c_scales, 8, 12)
+        load_scales(s1, packed, w1h_scales, w1c_scales, 4, 8, row=4)
+        load_words(w1, "w1_third", w1h_words, w1c_words, HOT, 10)
+        load_scales(s1, hot_packed, w1h_scales, w1c_scales, HOT, 4)
         hot_rows = w1h_scales.rearrange("e s (q r) n -> q (e s) r n", r=4).bitcast(I32)
         for q in range(4):
-            nc.sync.dma_start(hot_packed[32 * q : 32 * q + 4 * HOT, 0, :].bitcast(I32), hot_rows[q])
-        load_words(w1, "w1_hot", w1h_words, w1c_words, 0, HOT)
+            nc.sync.dma_start(hot_packed[32 * q + 4 : 32 * q + 16, 0, :].bitcast(I32), hot_rows[q])
         load_words(w2, "w2_cold", w2h_words, w2c_words, HOT, E)
         load_scales(s2, s2_cold, w2h_scales, w2c_scales, HOT, E)
-        load_words(w2, "w2_hot", w2h_words, w2c_words, 0, HOT)
-        load_scales(s2, s2_hot, w2h_scales, w2c_scales, 0, HOT)
 
         ordered_words, ordered_plane = {}, {}
 
-        def reorder_cold(first, last):
-            count = last - first
-            words = held.tile([P, count, 2 * H], U8, name="words_%d" % first, align_bytes=64)
-            planes = held.tile([P, count, H], U8, name="planes_%d" % first, align_bytes=64)
+        def reorder_words(first, last):
+            words = held.tile([P, last - first, 2 * H], U8, name="words_%d" % first, align_bytes=64)
             nc.gpsimd.tensor_copy(
                 words[:].bitcast(U16).rearrange("p e (t m) -> p e t m", t=4),
                 rows_of(w1, first, last).bitcast(U16).rearrange("p e (m t) -> p e t m", t=4),
             )
+            for e in range(first, last):
+                ordered_words[e] = words[:, e - first, :]
+
+        def reorder_planes(planes, first, last):
             nc.gpsimd.tensor_copy(
-                planes[:].rearrange("p e (t m) -> p e t m", t=4),
+                planes.rearrange("p e (t m) -> p e t m", t=4),
                 rows_of(s1, first, last).rearrange("p e (m t) -> p e t m", t=4),
             )
             for e in range(first, last):
-                ordered_words[e] = words[:, e - first, :]
                 ordered_plane[e] = planes[:, e - first, :]
 
-        last = E - TURNED
-        for count in REORDER_COUNTS:
-            reorder_cold(last - count, last)
-            last = last - count
-        plane = held.tile([P, H], U8, name="hot_plane", align_bytes=64)
-        nc.gpsimd.tensor_copy(
-            plane[:].rearrange("p (t m) -> p t m", t=4), hot_packed[:, 0, :].rearrange("p (m t) -> p t m", t=4)
-        )
+        for e in reversed(range(12, E - TURNED)):
+            reorder_words(e, e + 1)
+            plane = held.tile([P, 1, H], U8, name="plane_%d" % e, align_bytes=64)
+            reorder_planes(plane[:], e, e + 1)
+        packed_ordered = held.tile([P, 4, H], U8, name="packed_ordered", align_bytes=64)
+        for first in (10, 8):
+            reorder_planes(packed_ordered[:, first - 8 : first - 6, :], first, first + 2)
+            reorder_words(first, first + 2)
+        for r in range(4):
+            nc.sync.dma_start(unpacked[r:P:32, :, :].bitcast(I32), packed_ordered[4 + r : P : 32, :, :].bitcast(I32))
+        for e in range(4, 8):
+            ordered_plane[e] = unpacked[:, e - 4, :]
+        load_words(w1, "w1_hot", w1h_words, w1c_words, 0, HOT)
+        load_words(w2, "w2_hot", w2h_words, w2c_words, 0, HOT)
+        load_scales(s2, s2_hot, w2h_scales, w2c_scales, 0, HOT)
+        for first in (6, 4):
+            reorder_words(first, first + 2)
+        plane = held.tile([P, 1, H], U8, name="hot_plane", align_bytes=64)
+        reorder_planes(plane[:], HOT, HOT + 1)
+        reorder_words(HOT, HOT + 1)
         for e in reversed(range(HOT)):
-            ordered_plane[e] = plane[4 * e : P, :]
+            ordered_plane[e] = plane[4 * (e + 1) : P, 0, :]
             words = held.tile([P, H], U32, name="hot_words_%d" % e, align_bytes=64)
             nc.gpsimd.tensor_copy(
                 words[:].rearrange("p (t b n) -> p b t n", t=4, n=4),
@@ -149,18 +160,29 @@ def tile_moe_hot_s_mlp_relu_kernel(
             return tenants[-1]
 
         slot_words, slot_scales = {}, {}
-        last = 2 * E
-        for halves in GATHER_HALVES:
-            first = last - halves
-            listed = offsets[:, first * P // 16 : last * P // 16]
-            words = held.tile([P, halves * P], U32, name="slot_words_%d" % first, align_bytes=64)
-            scales = held.tile([P, halves * P], U8, name="slot_scales_%d" % first, align_bytes=64)
-            nc.vector.tensor_copy(words[:], token_words[:].bitcast(U32).indirect(listed))
-            nc.vector.tensor_copy(scales[:], token_scales[:].indirect(listed))
+
+        def gather(into, name, dtype, table, first, last):
+            tile = held.tile([P, (last - first) * P], dtype, name=name, align_bytes=64)
+            nc.vector.tensor_copy(tile[:], table.indirect(offsets[:, first * P // 16 : last * P // 16]))
             for s in range(first, last):
-                slot_words[s] = words[:, (s - first) * P : (s - first + 1) * P]
-                slot_scales[s] = scales[:, (s - first) * P : (s - first + 1) * P]
-            last = first
+                into[s] = tile[:, (s - first) * P : (s - first + 1) * P]
+
+        cuts = [2 * E - sum(GATHER_HALVES[:number]) for number in range(len(GATHER_HALVES) + 1)]
+
+        def gather_words(number):
+            name = "slot_words_%d" % (number % WORD_ROOMS)
+            gather(slot_words, name, U32, token_words[:].bitcast(U32), cuts[number + 1], cuts[number])
+
+        def gather_scales(number):
+            name = "slot_scales_%d" % (number % SCALE_ROOMS)
+            gather(slot_scales, name, U8, token_scales[:], cuts[number + 1], cuts[number])
+
+        def gather_into_free_rooms(done_from):
+            for number in range(len(GATHER_HALVES)):
+                for rooms, table, call in ((WORD_ROOMS, slot_words, gather_words), (SCALE_ROOMS, slot_scales, gather_scales)):
+                    free = number < rooms or cuts[number - rooms + 1] >= done_from
+                    if free and cuts[number + 1] not in table:
+                        call(number)
 
         grouped, group_tile = {}, {}
         for first, last in QUANTISED + [(0, 1)]:
@@ -215,18 +237,10 @@ def tile_moe_hot_s_mlp_relu_kernel(
                     grouped[e][:, half * P : (half + 1) * P, :], sums[:].rearrange("p t s -> p s t"), RELU
                 )
 
-        for e in reversed(range(E)):
-            if e >= E - TURNED:
-                first_layer_turned(e)
-            else:
-                first_layer(e)
-            if E - TURNED <= e + 1 < E:
-                turn_and_weave(e + 1)
-
-        def quantise(name, values):
+        def quantise(name, values, room=None, scale_room=None):
             columns = values.shape[1]
-            codes = held.tile([P, columns], U32, name=name + "_codes", align_bytes=64)
-            scales = held.tile([P, columns], U8, name=name + "_scales", align_bytes=64)
+            codes = held.tile([P, columns], U32, name=room or name + "_codes", align_bytes=64)
+            scales = held.tile([P, columns], U8, name=scale_room or name + "_scales", align_bytes=64)
             nc.vector.quantize_mx(
                 out=codes[:].bitcast(FP8X4), scales=scales[:], in_=values.rearrange("p c t -> p (c t)")
             )
@@ -245,13 +259,16 @@ def tile_moe_hot_s_mlp_relu_kernel(
 
         def store(results, first_slot, copy):
             columns = results.shape[1]
-            staged = held.tile([P, columns], F32, name="staged_%d" % first_slot)
+            name = "grouped_0" if first_slot == C else "staged_%d" % first_slot
+            staged = held.tile([P, columns], F32, name=name, align_bytes=64)
             copy(staged[:], results[:])
             nc.sync.dma_start(out[:, first_slot : first_slot + columns], staged[:])
 
         quantised = {}
-        for low, high in QUANTISED:
-            codes, scales = quantise("h_%d" % low, group_tile[low][:])
+        deferred = []
+
+        def second_layer(low, high):
+            codes, scales = quantise("h_%d" % low, group_tile[low][:], "wide_codes" if low >= 8 else None, "words_8" if low == 12 else None)
             for e in range(low, high):
                 slots = slice((e - low) * C, (e - low + 1) * C)
                 quantised[e] = (codes[:, slots], scales[:, slots])
@@ -260,10 +277,30 @@ def tile_moe_hot_s_mlp_relu_kernel(
                     results = next_bank([P, (last - first) * C])
                     for e in range(first, last):
                         second_product(results[:, (e - first) * C : (e - first + 1) * C], e, *quantised[e])
-                    store(results, first * C, nc.scalar.copy if number in ON_SCALAR else nc.vector.tensor_copy)
+                    copy = nc.scalar.copy if number in ON_SCALAR else nc.vector.tensor_copy
+                    if first == 1:
+                        deferred.append((results, first * C, copy))
+                    else:
+                        store(results, first * C, copy)
+
+        for e in reversed(range(E)):
+            gather_into_free_rooms(2 * e + 2)
+            if e >= E - TURNED:
+                first_layer_turned(e)
+            else:
+                first_layer(e)
+            if E - TURNED <= e + 2 < E:
+                turn_and_weave(e + 2)
+            for low, high in QUANTISED:
+                if SECOND_BEHIND[low] == e:
+                    second_layer(low, high)
+        waiting = {}
+        for half in (1, 0):
+            waiting[half] = quantise("last_%d" % half, grouped[0][:, half * P : (half + 1) * P, :])
+        store(*deferred[0])
 
         for half, copy in ((1, nc.vector.tensor_copy), (0, nc.scalar.copy)):
-            codes, scales = quantise("last_%d" % half, grouped[0][:, half * P : (half + 1) * P, :])
+            codes, scales = waiting[half]
             results = next_bank([P, P])
             second_product(results[:], 0, codes[:], scales[:])
             store(results, half * P, copy)

@@ -18,13 +18,14 @@ RELU = mybir.ActivationFunctionType.Relu
 
 P = 128
 BANKS = 8
-TURNED = 2
+TURNED = 3
 GATHER_HALVES = [1, 1, 2, 2, 2, 4, 4, 4, 4, 4, 4]
 WORD_ROOMS, SCALE_ROOMS = 3, 3
-QUANTISED = [(12, 16), (8, 12), (6, 8), (4, 6), (2, 4), (1, 2)]
+QUANTISED = [(12, 16), (8, 12), (4, 8), (2, 4), (1, 2)]
 STORED = [(14, 16), (12, 14), (10, 12), (8, 10), (6, 8), (4, 6), (2, 4), (1, 2)]
-ON_SCALAR = [0, 1, 4, 5, 6]
-SECOND_BEHIND = {12: 3, 8: 1, 6: 1, 4: 0, 2: 0, 1: 0}
+HELD_BY = {12: "words_5", 8: "words_3"}
+ON_SCALAR = [0, 1, 2, 3, 6]
+SECOND_BEHIND = {12: 2, 8: 1, 4: 0, 2: 0, 1: 0}
 
 
 def tile_moe_hot_s_mlp_relu_kernel(
@@ -57,7 +58,7 @@ def tile_moe_hot_s_mlp_relu_kernel(
             source, base = (hot, 0) if first < HOT else (cold, HOT)
             rows = source.rearrange("e s (q r) n -> r q (e s) n", r=4)[:, :, first - base : last - base, :]
             for r in range(4):
-                nc.sync.dma_start(tile[row + r : P : 32, :, :].bitcast(I32), rows[r].bitcast(I32))
+                nc.sync.dma_start(tile[row + r : P : 32, 0 : last - first, :].bitcast(I32), rows[r].bitcast(I32))
             for e in range(first, last):
                 into[e] = (tile, e - first)
 
@@ -69,11 +70,10 @@ def tile_moe_hot_s_mlp_relu_kernel(
             tile, place = table[e]
             return tile[:, place, :]
 
-        s1_first = zeroed_planes("s1_first", 4, H, nc.vector)
+        s1_first = zeroed_planes("s1_first", 5, H, nc.vector)
         packed = zeroed_planes("packed", 4, H, nc.vector)
         identity = held.tile([P, P], F32, name="identity")
         make_identity(nc, identity[:])
-        hot_packed = zeroed_planes("hot_packed", 1, H, nc.gpsimd)
         unpacked = zeroed_planes("unpacked", 4, H, nc.gpsimd)
         s2_cold = zeroed_planes("s2_cold", E - HOT, N, nc.gpsimd)
         s2_hot = zeroed_planes("s2_hot", HOT, N, nc.gpsimd)
@@ -90,15 +90,14 @@ def tile_moe_hot_s_mlp_relu_kernel(
         nc.sync.dma_start(token_words[:], x_words.rearrange("s p t d -> p (s t d)").bitcast(I32))
 
         load_words(w1, "w1_first", w1h_words, w1c_words, 14, 16)
-        load_scales(s1, s1_first, w1h_scales, w1c_scales, 12, 16)
-        load_words(w1, "w1_second", w1h_words, w1c_words, 10, 14)
-        load_scales(s1, packed, w1h_scales, w1c_scales, 8, 12)
-        load_scales(s1, packed, w1h_scales, w1c_scales, 4, 8, row=4)
-        load_words(w1, "w1_third", w1h_words, w1c_words, HOT, 10)
-        load_scales(s1, hot_packed, w1h_scales, w1c_scales, HOT, 4)
-        hot_rows = w1h_scales.rearrange("e s (q r) n -> q (e s) r n", r=4).bitcast(I32)
-        for q in range(4):
-            nc.sync.dma_start(hot_packed[32 * q + 4 : 32 * q + 16, 0, :].bitcast(I32), hot_rows[q])
+        load_scales(s1, s1_first, w1h_scales, w1c_scales, 11, 16)
+        load_words(w1, "w1_second", w1h_words, w1c_words, 11, 14)
+        load_words(w1, "w1_third", w1h_words, w1c_words, 9, 11)
+        load_scales(s1, packed, w1h_scales, w1c_scales, 7, 11)
+        load_scales(s1, packed, w1h_scales, w1c_scales, HOT, 7, row=4)
+        load_scales(s1, packed, w1h_scales, w1c_scales, 0, HOT, row=8)
+        load_words(w1, "w1_fourth", w1h_words, w1c_words, HOT, 9)
+        load_words(w1, "w1_hot", w1h_words, w1c_words, 0, HOT)
         load_words(w2, "w2_cold", w2h_words, w2c_words, HOT, E)
         load_scales(s2, s2_cold, w2h_scales, w2c_scales, HOT, E)
 
@@ -121,28 +120,23 @@ def tile_moe_hot_s_mlp_relu_kernel(
             for e in range(first, last):
                 ordered_plane[e] = planes[:, e - first, :]
 
-        for e in reversed(range(12, E - TURNED)):
-            reorder_words(e, e + 1)
-            plane = held.tile([P, 1, H], U8, name="plane_%d" % e, align_bytes=64)
-            reorder_planes(plane[:], e, e + 1)
+        direct_ordered = held.tile([P, 2, H], U8, name="direct_ordered", align_bytes=64)
         packed_ordered = held.tile([P, 4, H], U8, name="packed_ordered", align_bytes=64)
-        for first in (10, 8):
-            reorder_planes(packed_ordered[:, first - 8 : first - 6, :], first, first + 2)
-            reorder_words(first, first + 2)
+        reorder_planes(direct_ordered[:], 11, 13)
+        reorder_words(11, 13)
+        reorder_words(9, 11)
+        reorder_planes(packed_ordered[:, 2:4, :], 9, 11)
+        reorder_planes(packed_ordered[:, 0:2, :], 7, 9)
         for r in range(4):
             nc.sync.dma_start(unpacked[r:P:32, :, :].bitcast(I32), packed_ordered[4 + r : P : 32, :, :].bitcast(I32))
-        for e in range(4, 8):
-            ordered_plane[e] = unpacked[:, e - 4, :]
-        load_words(w1, "w1_hot", w1h_words, w1c_words, 0, HOT)
+        for e in range(HOT, 7):
+            ordered_plane[e] = unpacked[:, e - HOT, :]
         load_words(w2, "w2_hot", w2h_words, w2c_words, 0, HOT)
         load_scales(s2, s2_hot, w2h_scales, w2c_scales, 0, HOT)
-        for first in (6, 4):
+        for first in (7, 5, 3):
             reorder_words(first, first + 2)
-        plane = held.tile([P, 1, H], U8, name="hot_plane", align_bytes=64)
-        reorder_planes(plane[:], HOT, HOT + 1)
-        reorder_words(HOT, HOT + 1)
         for e in reversed(range(HOT)):
-            ordered_plane[e] = plane[4 * (e + 1) : P, 0, :]
+            ordered_plane[e] = packed_ordered[8:P, e, :]
             words = held.tile([P, H], U32, name="hot_words_%d" % e, align_bytes=64)
             nc.gpsimd.tensor_copy(
                 words[:].rearrange("p (t b n) -> p b t n", t=4, n=4),
@@ -268,7 +262,7 @@ def tile_moe_hot_s_mlp_relu_kernel(
         deferred = []
 
         def second_layer(low, high):
-            codes, scales = quantise("h_%d" % low, group_tile[low][:], "wide_codes" if low >= 8 else None, "words_8" if low == 12 else None)
+            codes, scales = quantise("h_%d" % low, group_tile[low][:], HELD_BY.get(low))
             for e in range(low, high):
                 slots = slice((e - low) * C, (e - low + 1) * C)
                 quantised[e] = (codes[:, slots], scales[:, slots])
@@ -289,8 +283,8 @@ def tile_moe_hot_s_mlp_relu_kernel(
                 first_layer_turned(e)
             else:
                 first_layer(e)
-            if E - TURNED <= e + 2 < E:
-                turn_and_weave(e + 2)
+            if E - TURNED <= e + 3 < E:
+                turn_and_weave(e + 3)
             for low, high in QUANTISED:
                 if SECOND_BEHIND[low] == e:
                     second_layer(low, high)

@@ -19,13 +19,13 @@ RELU = mybir.ActivationFunctionType.Relu
 P = 128
 BANKS = 8
 TURNED = 3
-GATHER_HALVES = [1, 1, 2, 2, 2, 4, 4, 4, 4, 4, 4]
+GATHER_HALVES = [1, 1, 2, 2, 2, 2, 4, 4, 4, 4, 4, 2]
 WORD_ROOMS, SCALE_ROOMS = 3, 3
 QUANTISED = [(12, 16), (8, 12), (4, 8), (2, 4), (1, 2)]
 STORED = [(14, 16), (12, 14), (10, 12), (8, 10), (6, 8), (4, 6), (2, 4), (1, 2)]
-HELD_BY = {12: "words_5", 8: "words_3"}
-ON_SCALAR = [0, 1, 2, 3, 6]
-SECOND_BEHIND = {12: 2, 8: 1, 4: 0, 2: 0, 1: 0}
+HELD_BY = {12: "words_7", 8: "words_5"}
+ON_SCALAR = [0, 1, 6]
+SECOND_BEHIND = {12: 2, 8: 0, 4: 0, 2: 0, 1: 0}
 
 
 def tile_moe_hot_s_mlp_relu_kernel(

@@ -18,14 +18,18 @@ RELU = mybir.ActivationFunctionType.Relu
 
 P = 128
 BANKS = 8
-TURNED = 3
-GATHER_HALVES = [1, 1, 2, 2, 2, 2, 4, 4, 4, 4, 4, 2]
-WORD_ROOMS, SCALE_ROOMS = 3, 3
+
+TURNED_FROM = 13
+TURN_LAG = 3
+DIRECT_FROM, SHIFTED_TO = 11, 7
+
+GATHER_HALVES = [1, 1] + [2] * 4 + [4] * 5 + [2]
+GATHER_ROOMS = 3
+
 QUANTISED = [(12, 16), (8, 12), (4, 8), (2, 4), (1, 2)]
-STORED = [(14, 16), (12, 14), (10, 12), (8, 10), (6, 8), (4, 6), (2, 4), (1, 2)]
-HELD_BY = {12: "words_7", 8: "words_5"}
-ON_SCALAR = [0, 1, 6]
-SECOND_BEHIND = {12: 2, 8: 0, 4: 0, 2: 0, 1: 0}
+CODE_ROOMS = {12: "words_7", 8: "words_5"}
+EARLY_SECOND_BEHIND = 2
+VECTOR_RESULTS = (6, 12)
 
 
 def tile_moe_hot_s_mlp_relu_kernel(
@@ -49,16 +53,16 @@ def tile_moe_hot_s_mlp_relu_kernel(
             for e in range(first, last):
                 into[e] = (tile, e - first)
 
-        def zeroed_planes(name, count, width, engine):
+        def zeroed_planes(name, count, width):
             tile = held.tile([P, count, width], U8, name=name, align_bytes=64)
-            engine.memset(tile[:].bitcast(I32), 0)
+            nc.vector.memset(tile[:].bitcast(I32), 0)
             return tile
 
-        def load_scales(into, tile, hot, cold, first, last, row=0):
+        def load_scales(into, tile, hot, cold, first, last, lower=0):
             source, base = (hot, 0) if first < HOT else (cold, HOT)
             rows = source.rearrange("e s (q r) n -> r q (e s) n", r=4)[:, :, first - base : last - base, :]
             for r in range(4):
-                nc.sync.dma_start(tile[row + r : P : 32, 0 : last - first, :].bitcast(I32), rows[r].bitcast(I32))
+                nc.sync.dma_start(tile[lower + r : P : 32, 0 : last - first, :].bitcast(I32), rows[r].bitcast(I32))
             for e in range(first, last):
                 into[e] = (tile, e - first)
 
@@ -70,13 +74,13 @@ def tile_moe_hot_s_mlp_relu_kernel(
             tile, place = table[e]
             return tile[:, place, :]
 
-        s1_first = zeroed_planes("s1_first", 5, H, nc.vector)
-        packed = zeroed_planes("packed", 4, H, nc.vector)
+        direct = zeroed_planes("direct", E - DIRECT_FROM, H)
+        packed = zeroed_planes("packed", DIRECT_FROM - SHIFTED_TO, H)
+        s2_cold = zeroed_planes("s2_cold", E - HOT, N)
+        moved_up = zeroed_planes("moved_up", SHIFTED_TO - HOT, H)
+        s2_hot = zeroed_planes("s2_hot", HOT, N)
         identity = held.tile([P, P], F32, name="identity")
         make_identity(nc, identity[:])
-        unpacked = zeroed_planes("unpacked", 4, H, nc.gpsimd)
-        s2_cold = zeroed_planes("s2_cold", E - HOT, N, nc.gpsimd)
-        s2_hot = zeroed_planes("s2_hot", HOT, N, nc.gpsimd)
 
         token_scales = held.tile([P, T], U8, name="token_scales", align_bytes=64)
         token_words = held.tile([P, T], I32, name="token_words", align_bytes=64)
@@ -89,13 +93,13 @@ def tile_moe_hot_s_mlp_relu_kernel(
         nc.sync.dma_start(offsets[:], offs)
         nc.sync.dma_start(token_words[:], x_words.rearrange("s p t d -> p (s t d)").bitcast(I32))
 
-        load_words(w1, "w1_first", w1h_words, w1c_words, 14, 16)
-        load_scales(s1, s1_first, w1h_scales, w1c_scales, 11, 16)
-        load_words(w1, "w1_second", w1h_words, w1c_words, 11, 14)
-        load_words(w1, "w1_third", w1h_words, w1c_words, 9, 11)
-        load_scales(s1, packed, w1h_scales, w1c_scales, 7, 11)
-        load_scales(s1, packed, w1h_scales, w1c_scales, HOT, 7, row=4)
-        load_scales(s1, packed, w1h_scales, w1c_scales, 0, HOT, row=8)
+        load_words(w1, "w1_first", w1h_words, w1c_words, 14, E)
+        load_scales(s1, direct, w1h_scales, w1c_scales, DIRECT_FROM, E)
+        load_words(w1, "w1_second", w1h_words, w1c_words, DIRECT_FROM, 14)
+        load_words(w1, "w1_third", w1h_words, w1c_words, 9, DIRECT_FROM)
+        load_scales(s1, packed, w1h_scales, w1c_scales, SHIFTED_TO, DIRECT_FROM)
+        load_scales(s1, packed, w1h_scales, w1c_scales, HOT, SHIFTED_TO, lower=4)
+        load_scales(s1, packed, w1h_scales, w1c_scales, 0, HOT, lower=8)
         load_words(w1, "w1_fourth", w1h_words, w1c_words, HOT, 9)
         load_words(w1, "w1_hot", w1h_words, w1c_words, 0, HOT)
         load_words(w2, "w2_cold", w2h_words, w2c_words, HOT, E)
@@ -103,7 +107,7 @@ def tile_moe_hot_s_mlp_relu_kernel(
 
         ordered_words, ordered_plane = {}, {}
 
-        def reorder_words(first, last):
+        def reorder_cold_words(first, last):
             words = held.tile([P, last - first, 2 * H], U8, name="words_%d" % first, align_bytes=64)
             nc.gpsimd.tensor_copy(
                 words[:].bitcast(U16).rearrange("p e (t m) -> p e t m", t=4),
@@ -120,29 +124,32 @@ def tile_moe_hot_s_mlp_relu_kernel(
             for e in range(first, last):
                 ordered_plane[e] = planes[:, e - first, :]
 
-        direct_ordered = held.tile([P, 2, H], U8, name="direct_ordered", align_bytes=64)
-        packed_ordered = held.tile([P, 4, H], U8, name="packed_ordered", align_bytes=64)
-        reorder_planes(direct_ordered[:], 11, 13)
-        reorder_words(11, 13)
-        reorder_words(9, 11)
-        reorder_planes(packed_ordered[:, 2:4, :], 9, 11)
-        reorder_planes(packed_ordered[:, 0:2, :], 7, 9)
-        for r in range(4):
-            nc.sync.dma_start(unpacked[r:P:32, :, :].bitcast(I32), packed_ordered[4 + r : P : 32, :, :].bitcast(I32))
-        for e in range(HOT, 7):
-            ordered_plane[e] = unpacked[:, e - HOT, :]
-        load_words(w2, "w2_hot", w2h_words, w2c_words, 0, HOT)
-        load_scales(s2, s2_hot, w2h_scales, w2c_scales, 0, HOT)
-        for first in (7, 5, 3):
-            reorder_words(first, first + 2)
-        for e in reversed(range(HOT)):
-            ordered_plane[e] = packed_ordered[8:P, e, :]
+        def reorder_hot_words(e):
             words = held.tile([P, H], U32, name="hot_words_%d" % e, align_bytes=64)
             nc.gpsimd.tensor_copy(
                 words[:].rearrange("p (t b n) -> p b t n", t=4, n=4),
                 row_of(w1, e).bitcast(U32).rearrange("p (b n t) -> p b t n", t=4, n=4),
             )
             ordered_words[e] = words[:].bitcast(U8)
+
+        direct_ordered = held.tile([P, TURNED_FROM - DIRECT_FROM, H], U8, name="direct_ordered", align_bytes=64)
+        packed_ordered = held.tile([P, DIRECT_FROM - SHIFTED_TO, H], U8, name="packed_ordered", align_bytes=64)
+        reorder_planes(direct_ordered[:], DIRECT_FROM, TURNED_FROM)
+        reorder_cold_words(DIRECT_FROM, TURNED_FROM)
+        reorder_cold_words(9, DIRECT_FROM)
+        reorder_planes(packed_ordered[:, 2:4, :], 9, DIRECT_FROM)
+        reorder_planes(packed_ordered[:, 0:2, :], SHIFTED_TO, 9)
+        for r in range(4):
+            nc.sync.dma_start(moved_up[r:P:32, :, :].bitcast(I32), packed_ordered[4 + r : P : 32, :, :].bitcast(I32))
+        for e in range(HOT, SHIFTED_TO):
+            ordered_plane[e] = moved_up[:, e - HOT, :]
+        load_words(w2, "w2_hot", w2h_words, w2c_words, 0, HOT)
+        load_scales(s2, s2_hot, w2h_scales, w2c_scales, 0, HOT)
+        for first in range(SHIFTED_TO, HOT - 1, -2):
+            reorder_cold_words(first, first + 2)
+        for e in reversed(range(HOT)):
+            ordered_plane[e] = packed_ordered[8:P, e, :]
+            reorder_hot_words(e)
 
         def codes_of(words, e):
             return words.bitcast(FP8X4 if e < HOT else FP4X4)
@@ -154,29 +161,25 @@ def tile_moe_hot_s_mlp_relu_kernel(
             return tenants[-1]
 
         slot_words, slot_scales = {}, {}
-
-        def gather(into, name, dtype, table, first, last):
-            tile = held.tile([P, (last - first) * P], dtype, name=name, align_bytes=64)
-            nc.vector.tensor_copy(tile[:], table.indirect(offsets[:, first * P // 16 : last * P // 16]))
-            for s in range(first, last):
-                into[s] = tile[:, (s - first) * P : (s - first + 1) * P]
-
         cuts = [2 * E - sum(GATHER_HALVES[:number]) for number in range(len(GATHER_HALVES) + 1)]
 
-        def gather_words(number):
-            name = "slot_words_%d" % (number % WORD_ROOMS)
-            gather(slot_words, name, U32, token_words[:].bitcast(U32), cuts[number + 1], cuts[number])
+        def gather(number):
+            first, last = cuts[number + 1], cuts[number]
+            listed = offsets[:, first * P // 16 : last * P // 16]
+            room = number % GATHER_ROOMS
+            words = held.tile([P, (last - first) * P], U32, name="slot_words_%d" % room, align_bytes=64)
+            nc.vector.tensor_copy(words[:], token_words[:].bitcast(U32).indirect(listed))
+            scales = held.tile([P, (last - first) * P], U8, name="slot_scales_%d" % room, align_bytes=64)
+            nc.vector.tensor_copy(scales[:], token_scales[:].indirect(listed))
+            for s in range(first, last):
+                slot_words[s] = words[:, (s - first) * P : (s - first + 1) * P]
+                slot_scales[s] = scales[:, (s - first) * P : (s - first + 1) * P]
 
-        def gather_scales(number):
-            name = "slot_scales_%d" % (number % SCALE_ROOMS)
-            gather(slot_scales, name, U8, token_scales[:], cuts[number + 1], cuts[number])
-
-        def gather_into_free_rooms(done_from):
+        def gather_into_free_rooms(multiplied_from):
             for number in range(len(GATHER_HALVES)):
-                for rooms, table, call in ((WORD_ROOMS, slot_words, gather_words), (SCALE_ROOMS, slot_scales, gather_scales)):
-                    free = number < rooms or cuts[number - rooms + 1] >= done_from
-                    if free and cuts[number + 1] not in table:
-                        call(number)
+                free = number < GATHER_ROOMS or cuts[number - GATHER_ROOMS + 1] >= multiplied_from
+                if free and cuts[number + 1] not in slot_words:
+                    gather(number)
 
         grouped, group_tile = {}, {}
         for first, last in QUANTISED + [(0, 1)]:
@@ -213,7 +216,7 @@ def tile_moe_hot_s_mlp_relu_kernel(
                 turned[:].rearrange("p u c -> p c u"),
             )
 
-        def first_layer(e):
+        def first_layer_reordered(e):
             width = (4 if e < HOT else 2) * P
             for half in (1, 0):
                 sums = next_bank([P, 4, P])
@@ -231,10 +234,10 @@ def tile_moe_hot_s_mlp_relu_kernel(
                     grouped[e][:, half * P : (half + 1) * P, :], sums[:].rearrange("p t s -> p s t"), RELU
                 )
 
-        def quantise(name, values, room=None, scale_room=None):
+        def quantise(name, values, code_room):
             columns = values.shape[1]
-            codes = held.tile([P, columns], U32, name=room or name + "_codes", align_bytes=64)
-            scales = held.tile([P, columns], U8, name=scale_room or name + "_scales", align_bytes=64)
+            codes = held.tile([P, columns], U32, name=code_room, align_bytes=64)
+            scales = held.tile([P, columns], U8, name=name + "_scales", align_bytes=64)
             nc.vector.quantize_mx(
                 out=codes[:].bitcast(FP8X4), scales=scales[:], in_=values.rearrange("p c t -> p (c t)")
             )
@@ -253,48 +256,42 @@ def tile_moe_hot_s_mlp_relu_kernel(
 
         def store(results, first_slot, copy):
             columns = results.shape[1]
-            name = "grouped_0" if first_slot == C else "staged_%d" % first_slot
-            staged = held.tile([P, columns], F32, name=name, align_bytes=64)
+            staged = held.tile([P, columns], F32, name="staged_%d" % first_slot, align_bytes=64)
             copy(staged[:], results[:])
-            nc.sync.dma_start(out[:, first_slot : first_slot + columns], staged[:])
-
-        quantised = {}
-        deferred = []
+            queue = nc.scalar if first_slot < 2 * C else nc.sync
+            queue.dma_start(out[:, first_slot : first_slot + columns], staged[:])
 
         def second_layer(low, high):
-            codes, scales = quantise("h_%d" % low, group_tile[low][:], HELD_BY.get(low))
-            for e in range(low, high):
-                slots = slice((e - low) * C, (e - low + 1) * C)
-                quantised[e] = (codes[:, slots], scales[:, slots])
-            for number, (first, last) in enumerate(STORED):
-                if low <= first < high:
-                    results = next_bank([P, (last - first) * C])
-                    for e in range(first, last):
-                        second_product(results[:, (e - first) * C : (e - first + 1) * C], e, *quantised[e])
-                    copy = nc.scalar.copy if number in ON_SCALAR else nc.vector.tensor_copy
-                    if first == 1:
-                        deferred.append((results, first * C, copy))
-                    else:
-                        store(results, first * C, copy)
+            codes, scales = quantise("h_%d" % low, group_tile[low][:], CODE_ROOMS.get(low, "h_%d_codes" % low))
+            for first in reversed(range(low, high, 2)):
+                last = min(first + 2, high)
+                results = next_bank([P, (last - first) * C])
+                for e in range(first, last):
+                    slots = slice((e - low) * C, (e - low + 1) * C)
+                    second_product(
+                        results[:, (e - first) * C : (e - first + 1) * C], e, codes[:, slots], scales[:, slots]
+                    )
+                on_vector = VECTOR_RESULTS[0] <= first < VECTOR_RESULTS[1]
+                store(results, first * C, nc.vector.tensor_copy if on_vector else nc.scalar.copy)
 
         for e in reversed(range(E)):
-            gather_into_free_rooms(2 * e + 2)
-            if e >= E - TURNED:
+            gather_into_free_rooms(2 * (e + 1))
+            if e >= TURNED_FROM:
                 first_layer_turned(e)
             else:
-                first_layer(e)
-            if E - TURNED <= e + 3 < E:
-                turn_and_weave(e + 3)
-            for low, high in QUANTISED:
-                if SECOND_BEHIND[low] == e:
-                    second_layer(low, high)
-        waiting = {}
-        for half in (1, 0):
-            waiting[half] = quantise("last_%d" % half, grouped[0][:, half * P : (half + 1) * P, :])
-        store(*deferred[0])
+                first_layer_reordered(e)
+            if TURNED_FROM <= e + TURN_LAG < E:
+                turn_and_weave(e + TURN_LAG)
+            if e == EARLY_SECOND_BEHIND:
+                second_layer(*QUANTISED[0])
+        for low, high in QUANTISED[1:]:
+            second_layer(low, high)
 
-        for half, copy in ((1, nc.vector.tensor_copy), (0, nc.scalar.copy)):
-            codes, scales = waiting[half]
+        halves = [
+            (half, quantise("last_%d" % half, grouped[0][:, half * P : (half + 1) * P, :], "last_%d_codes" % half))
+            for half in (1, 0)
+        ]
+        for half, (codes, scales) in halves:
             results = next_bank([P, P])
             second_product(results[:], 0, codes[:], scales[:])
-            store(results, half * P, copy)
+            store(results, half * P, nc.vector.tensor_copy)

@@ -27,8 +27,8 @@ GATHER_HALVES = [1, 1] + [2] * 4 + [4] * 5 + [2]
 GATHER_ROOMS = 3
 
 QUANTISED = [(12, 16), (8, 12), (4, 8), (2, 4), (1, 2)]
-CODE_ROOMS = {12: "words_7", 8: "words_5"}
-EARLY_SECOND_BEHIND = 2
+CODE_ROOMS = {12: "words_9", 8: "words_5"}
+EARLY_SECOND_BEHIND = 3
 VECTOR_RESULTS = (6, 12)
 
 
@@ -124,13 +124,14 @@ def tile_moe_hot_s_mlp_relu_kernel(
             for e in range(first, last):
                 ordered_plane[e] = planes[:, e - first, :]
 
-        def reorder_hot_words(e):
-            words = held.tile([P, H], U32, name="hot_words_%d" % e, align_bytes=64)
+        def reorder_hot_words():
+            words = held.tile([P, HOT, H], U32, name="grouped_%d" % QUANTISED[0][0], align_bytes=64)
             nc.gpsimd.tensor_copy(
-                words[:].rearrange("p (t b n) -> p b t n", t=4, n=4),
-                row_of(w1, e).bitcast(U32).rearrange("p (b n t) -> p b t n", t=4, n=4),
+                words[:].rearrange("p e (t b n) -> p e b t n", t=4, n=4),
+                rows_of(w1, 0, HOT).bitcast(U32).rearrange("p e (b n t) -> p e b t n", t=4, n=4),
             )
-            ordered_words[e] = words[:].bitcast(U8)
+            for e in range(HOT):
+                ordered_words[e] = words[:, e, :].bitcast(U8)
 
         direct_ordered = held.tile([P, TURNED_FROM - DIRECT_FROM, H], U8, name="direct_ordered", align_bytes=64)
         packed_ordered = held.tile([P, DIRECT_FROM - SHIFTED_TO, H], U8, name="packed_ordered", align_bytes=64)
@@ -149,7 +150,6 @@ def tile_moe_hot_s_mlp_relu_kernel(
             reorder_cold_words(first, first + 2)
         for e in reversed(range(HOT)):
             ordered_plane[e] = packed_ordered[8:P, e, :]
-            reorder_hot_words(e)
 
         def codes_of(words, e):
             return words.bitcast(FP8X4 if e < HOT else FP4X4)
@@ -216,6 +216,13 @@ def tile_moe_hot_s_mlp_relu_kernel(
                 turned[:].rearrange("p u c -> p c u"),
             )
 
+        unread = []
+
+        def read_sums():
+            for written, sums in reversed(unread):
+                nc.scalar.activation(written, sums, RELU)
+            unread.clear()
+
         def first_layer_reordered(e):
             width = (4 if e < HOT else 2) * P
             for half in (1, 0):
@@ -230,9 +237,9 @@ def tile_moe_hot_s_mlp_relu_kernel(
                         start=True,
                         stop=True,
                     )
-                nc.scalar.activation(
-                    grouped[e][:, half * P : (half + 1) * P, :], sums[:].rearrange("p t s -> p s t"), RELU
-                )
+                unread.append((grouped[e][:, half * P : (half + 1) * P, :], sums[:].rearrange("p t s -> p s t")))
+            if not EARLY_SECOND_BEHIND <= e < EARLY_SECOND_BEHIND + 1:
+                read_sums()
 
         def quantise(name, values, code_room):
             columns = values.shape[1]
@@ -284,12 +291,14 @@ def tile_moe_hot_s_mlp_relu_kernel(
                 turn_and_weave(e + TURN_LAG)
             if e == EARLY_SECOND_BEHIND:
                 second_layer(*QUANTISED[0])
+                read_sums()
+                reorder_hot_words()
         for low, high in QUANTISED[1:]:
             second_layer(low, high)
 
         halves = [
             (half, quantise("last_%d" % half, grouped[0][:, half * P : (half + 1) * P, :], "last_%d_codes" % half))
-            for half in (1, 0)
+            for half in (0, 1)
         ]
         for half, (codes, scales) in halves:
             results = next_bank([P, P])

@@ -19,17 +19,14 @@ RELU = mybir.ActivationFunctionType.Relu
 P = 128
 BANKS = 8
 
-TURNED_FROM = 13
-TURN_LAG = 3
-DIRECT_FROM, SHIFTED_TO = 11, 7
+EARLY_FROM = 13
+PACKED_FROM = 5
+SCALAR_FROM = 14
 
-GATHER_HALVES = [1, 1] + [2] * 4 + [4] * 5 + [2]
-GATHER_ROOMS = 3
-
-QUANTISED = [(12, 16), (8, 12), (4, 8), (2, 4), (1, 2)]
-CODE_ROOMS = {12: "words_9", 8: "words_5"}
-EARLY_SECOND_BEHIND = 3
-VECTOR_RESULTS = (6, 12)
+WORD_TILES = [[(31, 32), (30, 31)], [(28, 30), (26, 28)]] + [[(s, s + 4)] for s in range(22, 1, -4)] + [[(0, 2)]]
+BYTE_TILES = [[(s, s + 4)] for s in range(28, -1, -4)]
+ROOMS = 2
+IN_TURN_FROM = 11
 
 
 def tile_moe_hot_s_mlp_relu_kernel(
@@ -41,7 +38,7 @@ def tile_moe_hot_s_mlp_relu_kernel(
         held = ctx.enter_context(tc.tile_pool(name="held", bufs=1))
         psum = ctx.enter_context(tc.psum_pool(name="psum", bufs=1))
 
-        w1, s1, w2, s2 = {}, {}, {}, {}
+        w1, w2 = {}, {}
 
         def load_words(into, name, hot, cold, first, last):
             if first < HOT:
@@ -53,18 +50,18 @@ def tile_moe_hot_s_mlp_relu_kernel(
             for e in range(first, last):
                 into[e] = (tile, e - first)
 
-        def zeroed_planes(name, count, width):
-            tile = held.tile([P, count, width], U8, name=name, align_bytes=64)
-            nc.vector.memset(tile[:].bitcast(I32), 0)
+        def zeroed(name, shape, engine=nc.vector):
+            tile = held.tile(shape, U8, name=name, align_bytes=64)
+            engine.memset(tile[:].bitcast(I32), 0)
             return tile
 
-        def load_scales(into, tile, hot, cold, first, last, lower=0):
+        def load_scales(tile, place, hot, cold, first, last, lower=0):
             source, base = (hot, 0) if first < HOT else (cold, HOT)
             rows = source.rearrange("e s (q r) n -> r q (e s) n", r=4)[:, :, first - base : last - base, :]
             for r in range(4):
-                nc.sync.dma_start(tile[lower + r : P : 32, 0 : last - first, :].bitcast(I32), rows[r].bitcast(I32))
-            for e in range(first, last):
-                into[e] = (tile, e - first)
+                nc.sync.dma_start(
+                    tile[lower + r : P : 32, place : place + last - first, :].bitcast(I32), rows[r].bitcast(I32)
+                )
 
         def rows_of(table, first, last):
             tile, place = table[first]
@@ -74,17 +71,17 @@ def tile_moe_hot_s_mlp_relu_kernel(
             tile, place = table[e]
             return tile[:, place, :]
 
-        direct = zeroed_planes("direct", E - DIRECT_FROM, H)
-        packed = zeroed_planes("packed", DIRECT_FROM - SHIFTED_TO, H)
-        s2_cold = zeroed_planes("s2_cold", E - HOT, N)
-        moved_up = zeroed_planes("moved_up", SHIFTED_TO - HOT, H)
-        s2_hot = zeroed_planes("s2_hot", HOT, N)
+        early = zeroed("early", [P, E - EARLY_FROM, H])
+        unpacked = zeroed("unpacked", [P, EARLY_FROM - PACKED_FROM, H])
+
         identity = held.tile([P, P], F32, name="identity")
         make_identity(nc, identity[:])
+        late = zeroed("late", [P, HOT, H], nc.gpsimd)
+        s2 = zeroed("s2", [P, E, N], nc.gpsimd)
 
-        token_scales = held.tile([P, T], U8, name="token_scales", align_bytes=64)
         token_words = held.tile([P, T], I32, name="token_words", align_bytes=64)
         offsets = held.tile([P, E * C // 16], U16, name="offsets")
+        token_scales = held.tile([P, T], U8, name="token_scales", align_bytes=64)
         quadrants = x_scales.rearrange("s (q r) t -> q s r t", r=4).bitcast(I32)
         for q in range(4):
             nc.sync.dma_start(
@@ -92,18 +89,16 @@ def tile_moe_hot_s_mlp_relu_kernel(
             )
         nc.sync.dma_start(offsets[:], offs)
         nc.sync.dma_start(token_words[:], x_words.rearrange("s p t d -> p (s t d)").bitcast(I32))
+        packed = held.tile([P, H], U8, name="packed", align_bytes=64)
+        nc.sync.dma_start(
+            packed[:].bitcast(I32),
+            w1c_scales.rearrange("e s b n -> b (e s) n")[:, PACKED_FROM - HOT : EARLY_FROM - HOT, :].bitcast(I32),
+        )
 
-        load_words(w1, "w1_first", w1h_words, w1c_words, 14, E)
-        load_scales(s1, direct, w1h_scales, w1c_scales, DIRECT_FROM, E)
-        load_words(w1, "w1_second", w1h_words, w1c_words, DIRECT_FROM, 14)
-        load_words(w1, "w1_third", w1h_words, w1c_words, 9, DIRECT_FROM)
-        load_scales(s1, packed, w1h_scales, w1c_scales, SHIFTED_TO, DIRECT_FROM)
-        load_scales(s1, packed, w1h_scales, w1c_scales, HOT, SHIFTED_TO, lower=4)
-        load_scales(s1, packed, w1h_scales, w1c_scales, 0, HOT, lower=8)
-        load_words(w1, "w1_fourth", w1h_words, w1c_words, HOT, 9)
-        load_words(w1, "w1_hot", w1h_words, w1c_words, 0, HOT)
-        load_words(w2, "w2_cold", w2h_words, w2c_words, HOT, E)
-        load_scales(s2, s2_cold, w2h_scales, w2c_scales, HOT, E)
+        load_words(w1, "slot_scales_1", w1h_words, w1c_words, SCALAR_FROM, E)
+        load_scales(early, 0, w1h_scales, w1c_scales, EARLY_FROM, E)
+        load_words(w1, "w1_second", w1h_words, w1c_words, 12, SCALAR_FROM)
+        load_words(w1, "w1_third", w1h_words, w1c_words, 8, 12)
 
         ordered_words, ordered_plane = {}, {}
 
@@ -116,40 +111,61 @@ def tile_moe_hot_s_mlp_relu_kernel(
             for e in range(first, last):
                 ordered_words[e] = words[:, e - first, :]
 
-        def reorder_planes(planes, first, last):
+        def reorder_planes(planes, loaded):
             nc.gpsimd.tensor_copy(
-                planes.rearrange("p e (t m) -> p e t m", t=4),
-                rows_of(s1, first, last).rearrange("p e (m t) -> p e t m", t=4),
+                planes.rearrange("p e (t m) -> p e t m", t=4), loaded.rearrange("p e (m t) -> p e t m", t=4)
             )
-            for e in range(first, last):
-                ordered_plane[e] = planes[:, e - first, :]
 
-        def reorder_hot_words():
-            words = held.tile([P, HOT, H], U32, name="grouped_%d" % QUANTISED[0][0], align_bytes=64)
-            nc.gpsimd.tensor_copy(
-                words[:].rearrange("p e (t b n) -> p e b t n", t=4, n=4),
-                rows_of(w1, 0, HOT).bitcast(U32).rearrange("p e (b n t) -> p e b t n", t=4, n=4),
+        for e in reversed(range(SCALAR_FROM, E - 1)):
+            words = held.tile([P, 2 * H], U8, name="words_%d" % e, align_bytes=64)
+            nc.scalar.copy(
+                words[:].bitcast(U16).rearrange("p (t b n) -> p b t n", t=4, n=8),
+                row_of(w1, e).bitcast(U16).rearrange("p (b n t) -> p b t n", t=4, n=8),
             )
-            for e in range(HOT):
-                ordered_words[e] = words[:, e, :].bitcast(U8)
+            ordered_words[e] = words[:]
 
-        direct_ordered = held.tile([P, TURNED_FROM - DIRECT_FROM, H], U8, name="direct_ordered", align_bytes=64)
-        packed_ordered = held.tile([P, DIRECT_FROM - SHIFTED_TO, H], U8, name="packed_ordered", align_bytes=64)
-        reorder_planes(direct_ordered[:], DIRECT_FROM, TURNED_FROM)
-        reorder_cold_words(DIRECT_FROM, TURNED_FROM)
-        reorder_cold_words(9, DIRECT_FROM)
-        reorder_planes(packed_ordered[:, 2:4, :], 9, DIRECT_FROM)
-        reorder_planes(packed_ordered[:, 0:2, :], SHIFTED_TO, 9)
-        for r in range(4):
-            nc.sync.dma_start(moved_up[r:P:32, :, :].bitcast(I32), packed_ordered[4 + r : P : 32, :, :].bitcast(I32))
-        for e in range(HOT, SHIFTED_TO):
-            ordered_plane[e] = moved_up[:, e - HOT, :]
+        early_ordered = held.tile([P, E - 1 - EARLY_FROM, H], U8, name="early_ordered", align_bytes=64)
+        packed_ordered = held.tile([P, 1, H], U8, name="packed_ordered", align_bytes=64)
+        late_ordered = held.tile([P, HOT, H], U8, name="late_ordered", align_bytes=64)
+        reorder_planes(packed_ordered[:], packed[:].unsqueeze(1))
+        reorder_planes(early_ordered[:, 1:2, :], early[:, 1:2, :])
+        for q in (0, 2, 1, 3):
+            nc.sync.dma_start(
+                unpacked[32 * q : 32 * q + 4, :, :].bitcast(I32),
+                packed_ordered[32 * q : 32 * (q + 1), 0, :].bitcast(I32),
+            )
+        reorder_cold_words(13, 14)
+        reorder_planes(early_ordered[:, 0:1, :], early[:, 0:1, :])
+        reorder_cold_words(12, 13)
+
+        load_words(w1, "w1_fourth", w1h_words, w1c_words, HOT, 8)
+        load_scales(late, 0, w1h_scales, w1c_scales, HOT, PACKED_FROM)
+        load_scales(late, 0, w1h_scales, w1c_scales, 0, HOT, lower=4)
+        load_words(w2, "w2_cold", w2h_words, w2c_words, HOT, E)
+        load_scales(s2, HOT, w2h_scales, w2c_scales, HOT, E)
+        load_words(w1, "w1_hot", w1h_words, w1c_words, 0, HOT)
         load_words(w2, "w2_hot", w2h_words, w2c_words, 0, HOT)
-        load_scales(s2, s2_hot, w2h_scales, w2c_scales, 0, HOT)
-        for first in range(SHIFTED_TO, HOT - 1, -2):
+        load_scales(s2, 0, w2h_scales, w2c_scales, 0, HOT)
+
+        for first in range(10, 3, -2):
             reorder_cold_words(first, first + 2)
-        for e in reversed(range(HOT)):
-            ordered_plane[e] = packed_ordered[8:P, e, :]
+        reorder_cold_words(HOT, HOT + 1)
+        reorder_planes(late_ordered[:], late[:])
+        hot_words = held.tile([P, HOT, H], U32, name="hot_words", align_bytes=64)
+        nc.gpsimd.tensor_copy(
+            hot_words[:].rearrange("p e (t b n) -> p e b t n", t=4, n=4),
+            rows_of(w1, 0, HOT).bitcast(U32).rearrange("p e (b n t) -> p e b t n", t=4, n=4),
+        )
+        for e in range(E - 1):
+            if e >= EARLY_FROM:
+                ordered_plane[e] = early_ordered[:, e - EARLY_FROM, :]
+            elif e >= PACKED_FROM:
+                ordered_plane[e] = unpacked[:, e - PACKED_FROM, :]
+            elif e >= HOT:
+                ordered_plane[e] = late_ordered[:, e - HOT, :]
+            else:
+                ordered_plane[e] = late_ordered[4:P, e, :]
+                ordered_words[e] = hot_words[:, e, :].bitcast(U8)
 
         def codes_of(words, e):
             return words.bitcast(FP8X4 if e < HOT else FP4X4)
@@ -161,37 +177,40 @@ def tile_moe_hot_s_mlp_relu_kernel(
             return tenants[-1]
 
         slot_words, slot_scales = {}, {}
-        cuts = [2 * E - sum(GATHER_HALVES[:number]) for number in range(len(GATHER_HALVES) + 1)]
 
-        def gather(number):
-            first, last = cuts[number + 1], cuts[number]
-            listed = offsets[:, first * P // 16 : last * P // 16]
-            room = number % GATHER_ROOMS
-            words = held.tile([P, (last - first) * P], U32, name="slot_words_%d" % room, align_bytes=64)
-            nc.vector.tensor_copy(words[:], token_words[:].bitcast(U32).indirect(listed))
-            scales = held.tile([P, (last - first) * P], U8, name="slot_scales_%d" % room, align_bytes=64)
-            nc.vector.tensor_copy(scales[:], token_scales[:].indirect(listed))
-            for s in range(first, last):
-                slot_words[s] = words[:, (s - first) * P : (s - first + 1) * P]
-                slot_scales[s] = scales[:, (s - first) * P : (s - first + 1) * P]
+        def gather(cuts, number, name, dtype, window, into):
+            pieces = cuts[number]
+            low, high = pieces[-1][0], pieces[0][1]
+            tile = held.tile([P, (high - low) * P], dtype, name="%s_%d" % (name, number % ROOMS), align_bytes=64)
+            for first, last in pieces:
+                listed = offsets[:, first * P // 16 : last * P // 16]
+                nc.vector.tensor_copy(tile[:, (first - low) * P : (last - low) * P], window.indirect(listed))
+            for s in range(low, high):
+                into[s] = tile[:, (s - low) * P : (s - low + 1) * P]
 
         def gather_into_free_rooms(multiplied_from):
-            for number in range(len(GATHER_HALVES)):
-                free = number < GATHER_ROOMS or cuts[number - GATHER_ROOMS + 1] >= multiplied_from
-                if free and cuts[number + 1] not in slot_words:
-                    gather(number)
+            for number in range(len(WORD_TILES)):
+                for cuts, name, dtype, window, into in (
+                    (BYTE_TILES, "slot_scales", U8, token_scales[:], slot_scales),
+                    (WORD_TILES, "slot_words", U32, token_words[:].bitcast(U32), slot_words),
+                ):
+                    if number == len(cuts):
+                        continue
+                    free = number < ROOMS or cuts[number - ROOMS][-1][0] >= multiplied_from
+                    if free and cuts[number][-1][0] not in into:
+                        gather(cuts, number, name, dtype, window, into)
 
+        groups = [(12, 16), (8, 12), (4, 8), (2, 4), (1, 2), (0, 1)]
         grouped, group_tile = {}, {}
-        for first, last in QUANTISED + [(0, 1)]:
+        for first, last in groups:
             tile = held.tile([P, (last - first) * C, 4], BF16, name="grouped_%d" % first, align_bytes=64)
             group_tile[first] = tile
             for e in range(first, last):
                 grouped[e] = tile[:, (e - first) * C : (e - first + 1) * C, :]
 
-        hidden = {}
+        hidden = held.tile([P, 2, 2, P, 2], BF16, name="hidden", align_bytes=64)
 
         def first_layer_turned(e):
-            hidden[e] = held.tile([P, 2, 2, P, 2], BF16, name="hidden_%d" % e, align_bytes=64)
             for half in (1, 0):
                 sums = next_bank([P, H])
                 nc.tensor.matmul_mx(
@@ -199,14 +218,14 @@ def tile_moe_hot_s_mlp_relu_kernel(
                     lhsT=slot_words[2 * e + half].bitcast(FP8X4),
                     lhsT_scale=slot_scales[2 * e + half],
                     rhs=codes_of(row_of(w1, e), e),
-                    rhs_scale=row_of(s1, e),
+                    rhs_scale=early[:, e - EARLY_FROM, :],
                     start=True,
                     stop=True,
                 )
-                nc.scalar.activation(hidden[e][:, half], sums[:].rearrange("s (p u v) -> s u p v", u=2, v=2), RELU)
+                nc.scalar.activation(hidden[:, half], sums[:].rearrange("s (p u v) -> s u p v", u=2, v=2), RELU)
 
         def turn_and_weave(e):
-            pairs = hidden[e][:].rearrange("s half u p v -> s half u (p v)").bitcast(F32)
+            pairs = hidden[:].rearrange("s half u p v -> s half u (p v)").bitcast(F32)
             turned = next_bank([P, 2, C])
             for half in range(2):
                 for u in range(2):
@@ -216,15 +235,9 @@ def tile_moe_hot_s_mlp_relu_kernel(
                 turned[:].rearrange("p u c -> p c u"),
             )
 
-        unread = []
-
-        def read_sums():
-            for written, sums in reversed(unread):
-                nc.scalar.activation(written, sums, RELU)
-            unread.clear()
-
-        def first_layer_reordered(e):
+        def first_layer(e):
             width = (4 if e < HOT else 2) * P
+            unread = []
             for half in (1, 0):
                 sums = next_bank([P, 4, P])
                 for t in range(4):
@@ -238,8 +251,8 @@ def tile_moe_hot_s_mlp_relu_kernel(
                         stop=True,
                     )
                 unread.append((grouped[e][:, half * P : (half + 1) * P, :], sums[:].rearrange("p t s -> p s t")))
-            if not EARLY_SECOND_BEHIND <= e < EARLY_SECOND_BEHIND + 1:
-                read_sums()
+            for written, sums in unread if e >= IN_TURN_FROM or e == 0 else reversed(unread):
+                nc.scalar.activation(written, sums, RELU)
 
         def quantise(name, values, code_room):
             columns = values.shape[1]
@@ -254,22 +267,22 @@ def tile_moe_hot_s_mlp_relu_kernel(
             nc.tensor.matmul_mx(
                 out=results,
                 lhsT=codes_of(row_of(w2, e), e),
-                lhsT_scale=row_of(s2, e),
+                lhsT_scale=s2[:, e, :],
                 rhs=codes.bitcast(FP8X4),
                 rhs_scale=scales,
                 start=True,
                 stop=True,
             )
 
-        def store(results, first_slot, copy):
+        def store(results, first_slot, copy, queue):
             columns = results.shape[1]
             staged = held.tile([P, columns], F32, name="staged_%d" % first_slot, align_bytes=64)
             copy(staged[:], results[:])
-            queue = nc.scalar if first_slot < 2 * C else nc.sync
             queue.dma_start(out[:, first_slot : first_slot + columns], staged[:])
 
-        def second_layer(low, high):
-            codes, scales = quantise("h_%d" % low, group_tile[low][:], CODE_ROOMS.get(low, "h_%d_codes" % low))
+        on_vector = (6, 4, 1)
+
+        def second_layer(low, high, codes, scales):
             for first in reversed(range(low, high, 2)):
                 last = min(first + 2, high)
                 results = next_bank([P, (last - first) * C])
@@ -278,29 +291,38 @@ def tile_moe_hot_s_mlp_relu_kernel(
                     second_product(
                         results[:, (e - first) * C : (e - first + 1) * C], e, codes[:, slots], scales[:, slots]
                     )
-                on_vector = VECTOR_RESULTS[0] <= first < VECTOR_RESULTS[1]
-                store(results, first * C, nc.vector.tensor_copy if on_vector else nc.scalar.copy)
+                copy = nc.vector.tensor_copy if first in on_vector else nc.scalar.copy
+                store(results, first * C, copy, nc.sync)
 
+        quantised = {}
+        gather_into_free_rooms(2 * E)
         for e in reversed(range(E)):
-            gather_into_free_rooms(2 * (e + 1))
-            if e >= TURNED_FROM:
+            if e == E - 1:
                 first_layer_turned(e)
             else:
-                first_layer_reordered(e)
-            if TURNED_FROM <= e + TURN_LAG < E:
-                turn_and_weave(e + TURN_LAG)
-            if e == EARLY_SECOND_BEHIND:
-                second_layer(*QUANTISED[0])
-                read_sums()
-                reorder_hot_words()
-        for low, high in QUANTISED[1:]:
-            second_layer(low, high)
+                first_layer(e)
+            if e == E - 3:
+                turn_and_weave(E - 1)
+            if e == 4:
+                quantised[8] = quantise("h_8", group_tile[8][:], "words_4")
+            gather_into_free_rooms(2 * e)
+            if e == 6:
+                quantised[12] = quantise("h_12", group_tile[12][:], "words_6")
+            if e == 3:
+                second_layer(12, 16, *quantised[12])
+            if e == 2:
+                second_layer(8, 12, *quantised[8])
+        for low, high in groups[2:5]:
+            second_layer(low, high, *quantise("h_%d" % low, group_tile[low][:], "h_%d_codes" % low))
 
         halves = [
             (half, quantise("last_%d" % half, grouped[0][:, half * P : (half + 1) * P, :], "last_%d_codes" % half))
-            for half in (0, 1)
+            for half in (1, 0)
         ]
         for half, (codes, scales) in halves:
             results = next_bank([P, P])
             second_product(results[:], 0, codes[:], scales[:])
-            store(results, half * P, nc.vector.tensor_copy)
+            if half:
+                store(results, half * P, nc.vector.tensor_copy, nc.sync)
+            else:
+                store(results, half * P, nc.scalar.copy, nc.scalar)

@@ -27,6 +27,7 @@ WORD_TILES = [[(31, 32), (30, 31)], [(28, 30), (26, 28)]] + [[(s, s + 4)] for s 
 BYTE_TILES = [[(s, s + 4)] for s in range(28, -1, -4)]
 ROOMS = 2
 IN_TURN_FROM = 11
+BEHIND = {6: ("sums", 2, 0), 4: ("sums", 2, 1), 2: ("sums", 1, 0)}
 
 
 def tile_moe_hot_s_mlp_relu_kernel(
@@ -147,9 +148,8 @@ def tile_moe_hot_s_mlp_relu_kernel(
         load_words(w2, "w2_hot", w2h_words, w2c_words, 0, HOT)
         load_scales(s2, 0, w2h_scales, w2c_scales, 0, HOT)
 
-        for first in range(10, 3, -2):
-            reorder_cold_words(first, first + 2)
-        reorder_cold_words(HOT, HOT + 1)
+        for first, last in ((10, 12), (8, 10), (7, 8), (5, 7), (3, 5)):
+            reorder_cold_words(first, last)
         reorder_planes(late_ordered[:], late[:])
         hot_words = held.tile([P, HOT, H], U32, name="hot_words", align_bytes=64)
         nc.gpsimd.tensor_copy(
@@ -172,9 +172,14 @@ def tile_moe_hot_s_mlp_relu_kernel(
 
         tenants = []
 
-        def next_bank(shape):
-            tenants.append(psum.tile(shape, F32, name="bank_%d" % (len(tenants) % BANKS)))
-            return tenants[-1]
+        def next_bank(shape, key=None, behind=None):
+            if behind is None:
+                tenants.append(key)
+                behind = key
+            elif key is not None:
+                tenants[tenants.index(behind)] = key
+                behind = key
+            return psum.tile(shape, F32, name="bank_%d" % (tenants.index(behind) % BANKS))
 
         slot_words, slot_scales = {}, {}
 
@@ -212,7 +217,7 @@ def tile_moe_hot_s_mlp_relu_kernel(
 
         def first_layer_turned(e):
             for half in (1, 0):
-                sums = next_bank([P, H])
+                sums = next_bank([P, H], ("sums", e, half))
                 nc.tensor.matmul_mx(
                     out=sums[:],
                     lhsT=slot_words[2 * e + half].bitcast(FP8X4),
@@ -226,7 +231,7 @@ def tile_moe_hot_s_mlp_relu_kernel(
 
         def turn_and_weave(e):
             pairs = hidden[:].rearrange("s half u p v -> s half u (p v)").bitcast(F32)
-            turned = next_bank([P, 2, C])
+            turned = next_bank([P, 2, C], ("turned", e))
             for half in range(2):
                 for u in range(2):
                     nc.tensor.transpose(turned[:, u, half * P : (half + 1) * P], pairs[:, half, u, :], identity[:])
@@ -239,7 +244,7 @@ def tile_moe_hot_s_mlp_relu_kernel(
             width = (4 if e < HOT else 2) * P
             unread = []
             for half in (1, 0):
-                sums = next_bank([P, 4, P])
+                sums = next_bank([P, 4, P], ("sums", e, half))
                 for t in range(4):
                     nc.tensor.matmul_mx(
                         out=sums[:, t, :],
@@ -285,7 +290,7 @@ def tile_moe_hot_s_mlp_relu_kernel(
         def second_layer(low, high, codes, scales):
             for first in reversed(range(low, high, 2)):
                 last = min(first + 2, high)
-                results = next_bank([P, (last - first) * C])
+                results = next_bank([P, (last - first) * C], ("results", first), BEHIND.get(first))
                 for e in range(first, last):
                     slots = slice((e - low) * C, (e - low + 1) * C)
                     second_product(
@@ -303,14 +308,12 @@ def tile_moe_hot_s_mlp_relu_kernel(
                 first_layer(e)
             if e == E - 3:
                 turn_and_weave(E - 1)
-            if e == 4:
-                quantised[8] = quantise("h_8", group_tile[8][:], "words_4")
+            if e == 5:
+                quantised[12] = quantise("h_12", group_tile[12][:], "words_5")
+                quantised[8] = quantise("h_8", group_tile[8][:], "words_8")
             gather_into_free_rooms(2 * e)
-            if e == 6:
-                quantised[12] = quantise("h_12", group_tile[12][:], "words_6")
             if e == 3:
                 second_layer(12, 16, *quantised[12])
-            if e == 2:
                 second_layer(8, 12, *quantised[8])
         for low, high in groups[2:5]:
             second_layer(low, high, *quantise("h_%d" % low, group_tile[low][:], "h_%d_codes" % low))
@@ -320,7 +323,7 @@ def tile_moe_hot_s_mlp_relu_kernel(
             for half in (1, 0)
         ]
         for half, (codes, scales) in halves:
-            results = next_bank([P, P])
+            results = next_bank([P, P], ("last", half))
             second_product(results[:], 0, codes[:], scales[:])
             if half:
                 store(results, half * P, nc.vector.tensor_copy, nc.sync)

@@ -23,9 +23,6 @@ EARLY_FROM = 13
 PACKED_FROM = 5
 SCALAR_FROM = 14
 
-WORD_TILES = [[(31, 32), (30, 31)], [(28, 30), (26, 28)]] + [[(s, s + 4)] for s in range(22, 1, -4)] + [[(0, 2)]]
-BYTE_TILES = [[(s, s + 4)] for s in range(28, -1, -4)]
-ROOMS = 2
 IN_TURN_FROM = 11
 BEHIND = {6: ("sums", 2, 0), 4: ("sums", 2, 1), 2: ("sums", 1, 0)}
 
@@ -96,7 +93,7 @@ def tile_moe_hot_s_mlp_relu_kernel(
             w1c_scales.rearrange("e s b n -> b (e s) n")[:, PACKED_FROM - HOT : EARLY_FROM - HOT, :].bitcast(I32),
         )
 
-        load_words(w1, "slot_scales_1", w1h_words, w1c_words, SCALAR_FROM, E)
+        load_words(w1, "w1_first", w1h_words, w1c_words, SCALAR_FROM, E)
         load_scales(early, 0, w1h_scales, w1c_scales, EARLY_FROM, E)
         load_words(w1, "w1_second", w1h_words, w1c_words, 12, SCALAR_FROM)
         load_words(w1, "w1_third", w1h_words, w1c_words, 8, 12)
@@ -183,27 +180,28 @@ def tile_moe_hot_s_mlp_relu_kernel(
 
         slot_words, slot_scales = {}, {}
 
-        def gather(cuts, number, name, dtype, window, into):
-            pieces = cuts[number]
-            low, high = pieces[-1][0], pieces[0][1]
-            tile = held.tile([P, (high - low) * P], dtype, name="%s_%d" % (name, number % ROOMS), align_bytes=64)
-            for first, last in pieces:
-                listed = offsets[:, first * P // 16 : last * P // 16]
-                nc.vector.tensor_copy(tile[:, (first - low) * P : (last - low) * P], window.indirect(listed))
+        def gathered(name, dtype, low, high, into):
+            tile = held.tile([P, (high - low) * P], dtype, name=name, align_bytes=64)
             for s in range(low, high):
                 into[s] = tile[:, (s - low) * P : (s - low + 1) * P]
+            return tile, low
 
-        def gather_into_free_rooms(multiplied_from):
-            for number in range(len(WORD_TILES)):
-                for cuts, name, dtype, window, into in (
-                    (BYTE_TILES, "slot_scales", U8, token_scales[:], slot_scales),
-                    (WORD_TILES, "slot_words", U32, token_words[:].bitcast(U32), slot_words),
-                ):
-                    if number == len(cuts):
-                        continue
-                    free = number < ROOMS or cuts[number - ROOMS][-1][0] >= multiplied_from
-                    if free and cuts[number][-1][0] not in into:
-                        gather(cuts, number, name, dtype, window, into)
+        def gather(room, window, first, last):
+            tile, low = room
+            listed = offsets[:, first * P // 16 : last * P // 16]
+            nc.vector.tensor_copy(tile[:, (first - low) * P : (last - low) * P], window.indirect(listed))
+
+        word_window, byte_window = token_words[:].bitcast(U32), token_scales[:]
+        first_bytes = gathered("first_bytes", U8, 28, 32, slot_scales)
+        first_words = gathered("first_words", U32, 30, 32, slot_words)
+        second_words = gathered("second_words", U32, 26, 30, slot_words)
+        second_bytes = gathered("packed", U8, 24, 28, slot_scales)
+        gather(first_bytes, byte_window, 28, 32)
+        gather(first_words, word_window, 31, 32)
+        gather(first_words, word_window, 30, 31)
+        gather(second_words, word_window, 28, 30)
+        gather(second_words, word_window, 26, 28)
+        gather(second_bytes, byte_window, 24, 28)
 
         groups = [(12, 16), (8, 12), (4, 8), (2, 4), (1, 2), (0, 1)]
         grouped, group_tile = {}, {}
@@ -300,7 +298,6 @@ def tile_moe_hot_s_mlp_relu_kernel(
                 store(results, first * C, copy, nc.sync)
 
         quantised = {}
-        gather_into_free_rooms(2 * E)
         for e in reversed(range(E)):
             if e == E - 1:
                 first_layer_turned(e)
@@ -311,7 +308,17 @@ def tile_moe_hot_s_mlp_relu_kernel(
             if e == 5:
                 quantised[12] = quantise("h_12", group_tile[12][:], "words_5")
                 quantised[8] = quantise("h_8", group_tile[8][:], "words_8")
-            gather_into_free_rooms(2 * e)
+                last_words = gathered("grouped_12", U32, 0, 6, slot_words)
+                last_bytes = gathered("grouped_8", U8, 0, 4, slot_scales)
+                gather(last_words, word_window, 2, 6)
+                gather(last_bytes, byte_window, 0, 4)
+                gather(last_words, word_window, 0, 2)
+            if e == E - 1:
+                most_words = gathered("first_words", U32, 6, 26, slot_words)
+                most_bytes = gathered("w1_first", U8, 4, 24, slot_scales)
+                for first in range(22, 5, -4):
+                    gather(most_words, word_window, first, first + 4)
+                    gather(most_bytes, byte_window, first - 2, first + 2)
             if e == 3:
                 second_layer(12, 16, *quantised[12])
                 second_layer(8, 12, *quantised[8])

@@ -1,7 +1,6 @@
 from contextlib import ExitStack
 
 import concourse.mybir as mybir
-from concourse.masks import make_identity
 
 K, T, E, C, H, N, HOT = 512, 1024, 16, 256, 512, 128, 3
 FLOPS = 2 * E * C * (K * H + H * N)
@@ -70,10 +69,19 @@ def tile_moe_hot_s_mlp_relu_kernel(
             return tile[:, place, :]
 
         early = zeroed("early", [P, E - EARLY_FROM, H])
-        unpacked = zeroed("unpacked", [P, EARLY_FROM - PACKED_FROM, H])
+        unpacked = zeroed("unpacked", [P, EARLY_FROM - PACKED_FROM, H], nc.gpsimd)
 
         identity = held.tile([P, P], F32, name="identity")
-        make_identity(nc, identity[:])
+        ones = held.tile([P, 32], F32, name="ones")
+        along = held.tile([P, 32], F32, name="along", align_bytes=64)
+        across = held.tile([P, 32], F32, name="across", align_bytes=64)
+        nc.vector.memset(ones[:], 1.0)
+        nc.vector.memset(identity[:], 0.0)
+        nc.vector.tensor_tensor_scan(along[:], ones[:], ones[:], 0.0, mybir.AluOpType.mult, mybir.AluOpType.add)
+        nc.vector.transpose(across[:], along[:])
+        for q in range(4):
+            rows = slice(32 * q, 32 * (q + 1))
+            nc.vector.tensor_tensor(identity[rows, rows], along[rows, :], across[rows, :], mybir.AluOpType.is_equal)
         late = zeroed("late", [P, HOT, H], nc.gpsimd)
         s2 = zeroed("s2", [P, E, N], nc.gpsimd)
 
@@ -81,11 +89,12 @@ def tile_moe_hot_s_mlp_relu_kernel(
         offsets = held.tile([P, E * C // 16], U16, name="offsets")
         token_scales = held.tile([P, T], U8, name="token_scales", align_bytes=64)
         quadrants = x_scales.rearrange("s (q r) t -> q s r t", r=4).bitcast(I32)
-        for q in range(4):
-            nc.sync.dma_start(
+        nc.sync.dma_start(offsets[:], offs)
+        for q in (0, 2, 1, 3):
+            queue = nc.sync if q % 2 else nc.scalar
+            queue.dma_start(
                 token_scales[32 * q : 32 * (q + 1), :].bitcast(I32), quadrants[q].to_broadcast([8, 4, T // 4])
             )
-        nc.sync.dma_start(offsets[:], offs)
         nc.sync.dma_start(token_words[:], x_words.rearrange("s p t d -> p (s t d)").bitcast(I32))
         packed = held.tile([P, H], U8, name="packed", align_bytes=64)
         nc.sync.dma_start(
@@ -126,14 +135,13 @@ def tile_moe_hot_s_mlp_relu_kernel(
         packed_ordered = held.tile([P, 1, H], U8, name="packed_ordered", align_bytes=64)
         late_ordered = held.tile([P, HOT, H], U8, name="late_ordered", align_bytes=64)
         reorder_planes(packed_ordered[:], packed[:].unsqueeze(1))
-        reorder_planes(early_ordered[:, 1:2, :], early[:, 1:2, :])
+        reorder_planes(early_ordered[:], early[:, 0:2, :])
         for q in (0, 2, 1, 3):
             nc.sync.dma_start(
                 unpacked[32 * q : 32 * q + 4, :, :].bitcast(I32),
                 packed_ordered[32 * q : 32 * (q + 1), 0, :].bitcast(I32),
             )
         reorder_cold_words(13, 14)
-        reorder_planes(early_ordered[:, 0:1, :], early[:, 0:1, :])
         reorder_cold_words(12, 13)
 
         load_words(w1, "w1_fourth", w1h_words, w1c_words, HOT, 8)
@@ -199,11 +207,10 @@ def tile_moe_hot_s_mlp_relu_kernel(
         gather(first_bytes, byte_window, 28, 32)
         gather(first_words, word_window, 31, 32)
         gather(first_words, word_window, 30, 31)
-        gather(second_words, word_window, 28, 30)
-        gather(second_words, word_window, 26, 28)
+        gather(second_words, word_window, 26, 30)
         gather(second_bytes, byte_window, 24, 28)
 
-        groups = [(12, 16), (8, 12), (4, 8), (2, 4), (1, 2), (0, 1)]
+        groups = [(12, 16), (8, 12), (6, 8), (4, 6), (2, 4), (1, 2), (0, 1)]
         grouped, group_tile = {}, {}
         for first, last in groups:
             tile = held.tile([P, (last - first) * C, 4], BF16, name="grouped_%d" % first, align_bytes=64)
@@ -215,17 +222,23 @@ def tile_moe_hot_s_mlp_relu_kernel(
 
         def first_layer_turned(e):
             for half in (1, 0):
-                sums = next_bank([P, H], ("sums", e, half))
-                nc.tensor.matmul_mx(
-                    out=sums[:],
-                    lhsT=slot_words[2 * e + half].bitcast(FP8X4),
-                    lhsT_scale=slot_scales[2 * e + half],
-                    rhs=codes_of(row_of(w1, e), e),
-                    rhs_scale=early[:, e - EARLY_FROM, :],
-                    start=True,
-                    stop=True,
-                )
-                nc.scalar.activation(hidden[:, half], sums[:].rearrange("s (p u v) -> s u p v", u=2, v=2), RELU)
+                width = H // 2 if half else H
+                for low in range(0, H, width):
+                    sums = next_bank([P, width], ("sums", e, half, low))
+                    nc.tensor.matmul_mx(
+                        out=sums[:],
+                        lhsT=slot_words[2 * e + half].bitcast(FP8X4),
+                        lhsT_scale=slot_scales[2 * e + half],
+                        rhs=codes_of(row_of(w1, e)[:, 2 * low : 2 * (low + width)], e),
+                        rhs_scale=early[:, e - EARLY_FROM, low : low + width],
+                        start=True,
+                        stop=True,
+                    )
+                    nc.scalar.activation(
+                        hidden[:, half, :, low // 4 : (low + width) // 4, :],
+                        sums[:].rearrange("s (p u v) -> s u p v", u=2, v=2),
+                        RELU,
+                    )
 
         def turn_and_weave(e):
             pairs = hidden[:].rearrange("s half u p v -> s half u (p v)").bitcast(F32)
@@ -283,7 +296,7 @@ def tile_moe_hot_s_mlp_relu_kernel(
             copy(staged[:], results[:])
             queue.dma_start(out[:, first_slot : first_slot + columns], staged[:])
 
-        on_vector = (6, 4, 1)
+        on_vector = (6, 4)
 
         def second_layer(low, high, codes, scales):
             for first in reversed(range(low, high, 2)):
@@ -322,7 +335,7 @@ def tile_moe_hot_s_mlp_relu_kernel(
             if e == 3:
                 second_layer(12, 16, *quantised[12])
                 second_layer(8, 12, *quantised[8])
-        for low, high in groups[2:5]:
+        for low, high in groups[2:6]:
             second_layer(low, high, *quantise("h_%d" % low, group_tile[low][:], "h_%d_codes" % low))
 
         halves = [

@@ -1,6 +1,7 @@
 from contextlib import ExitStack
 
 import concourse.mybir as mybir
+from concourse.masks import make_identity
 
 K, T, E, C, H, N, HOT = 512, 1024, 16, 256, 512, 128, 3
 FLOPS = 2 * E * C * (K * H + H * N)
@@ -69,21 +70,12 @@ def tile_moe_hot_s_mlp_relu_kernel(
             return tile[:, place, :]
 
         early = zeroed("early", [P, E - EARLY_FROM, H])
-        unpacked = zeroed("unpacked", [P, EARLY_FROM - PACKED_FROM, H], nc.gpsimd)
+        unpacked = zeroed("unpacked", [P, EARLY_FROM - PACKED_FROM, H])
 
         identity = held.tile([P, P], F32, name="identity")
-        ones = held.tile([P, 32], F32, name="ones")
-        along = held.tile([P, 32], F32, name="along", align_bytes=64)
-        across = held.tile([P, 32], F32, name="across", align_bytes=64)
-        nc.vector.memset(ones[:], 1.0)
-        nc.vector.memset(identity[:], 0.0)
-        nc.vector.tensor_tensor_scan(along[:], ones[:], ones[:], 0.0, mybir.AluOpType.mult, mybir.AluOpType.add)
-        nc.vector.transpose(across[:], along[:])
-        for q in range(4):
-            rows = slice(32 * q, 32 * (q + 1))
-            nc.vector.tensor_tensor(identity[rows, rows], along[rows, :], across[rows, :], mybir.AluOpType.is_equal)
-        late = zeroed("late", [P, HOT, H], nc.gpsimd)
-        s2 = zeroed("s2", [P, E, N], nc.gpsimd)
+        make_identity(nc, identity[:])
+        late = zeroed("late", [P, HOT, H])
+        s2 = zeroed("s2", [P, E, N])
 
         token_words = held.tile([P, T], I32, name="token_words", align_bytes=64)
         offsets = held.tile([P, E * C // 16], U16, name="offsets")

@@ -87,12 +87,12 @@ def tile_moe_hot_s_mlp_relu_kernel(
             queue.dma_start(
                 token_scales[32 * q : 32 * (q + 1), :].bitcast(I32), quadrants[q].to_broadcast([8, 4, T // 4])
             )
-        nc.sync.dma_start(token_words[:], x_words.rearrange("s p t d -> p (s t d)").bitcast(I32))
         packed = held.tile([P, H], U8, name="packed", align_bytes=64)
         nc.sync.dma_start(
             packed[:].bitcast(I32),
             w1c_scales.rearrange("e s b n -> b (e s) n")[:, PACKED_FROM - HOT : EARLY_FROM - HOT, :].bitcast(I32),
         )
+        nc.sync.dma_start(token_words[:], x_words.rearrange("s p t d -> p (s t d)").bitcast(I32))
 
         load_words(w1, "w1_first", w1h_words, w1c_words, SCALAR_FROM, E)
         load_scales(early, 0, w1h_scales, w1c_scales, EARLY_FROM, E)
@@ -127,13 +127,14 @@ def tile_moe_hot_s_mlp_relu_kernel(
         packed_ordered = held.tile([P, 1, H], U8, name="packed_ordered", align_bytes=64)
         late_ordered = held.tile([P, HOT, H], U8, name="late_ordered", align_bytes=64)
         reorder_planes(packed_ordered[:], packed[:].unsqueeze(1))
-        reorder_planes(early_ordered[:], early[:, 0:2, :])
+        reorder_planes(early_ordered[:, 1:2, :], early[:, 1:2, :])
         for q in (0, 2, 1, 3):
             nc.sync.dma_start(
                 unpacked[32 * q : 32 * q + 4, :, :].bitcast(I32),
                 packed_ordered[32 * q : 32 * (q + 1), 0, :].bitcast(I32),
             )
         reorder_cold_words(13, 14)
+        reorder_planes(early_ordered[:, 0:1, :], early[:, 0:1, :])
         reorder_cold_words(12, 13)
 
         load_words(w1, "w1_fourth", w1h_words, w1c_words, HOT, 8)
@@ -199,7 +200,8 @@ def tile_moe_hot_s_mlp_relu_kernel(
         gather(first_bytes, byte_window, 28, 32)
         gather(first_words, word_window, 31, 32)
         gather(first_words, word_window, 30, 31)
-        gather(second_words, word_window, 26, 30)
+        gather(second_words, word_window, 28, 30)
+        gather(second_words, word_window, 26, 28)
         gather(second_bytes, byte_window, 24, 28)
 
         groups = [(12, 16), (8, 12), (6, 8), (4, 6), (2, 4), (1, 2), (0, 1)]

@@ -83,12 +83,11 @@ def tile_moe_hot_s_mlp_relu_kernel(
         quadrants = x_scales.rearrange("s (q r) t -> q s r t", r=4).bitcast(I32)
         nc.sync.dma_start(offsets[:], offs)
         for q in (0, 2, 1, 3):
-            queue = nc.sync if q % 2 else nc.scalar
-            queue.dma_start(
+            nc.sync.dma_start(
                 token_scales[32 * q : 32 * (q + 1), :].bitcast(I32), quadrants[q].to_broadcast([8, 4, T // 4])
             )
         packed = held.tile([P, H], U8, name="packed", align_bytes=64)
-        nc.sync.dma_start(
+        nc.scalar.dma_start(
             packed[:].bitcast(I32),
             w1c_scales.rearrange("e s b n -> b (e s) n")[:, PACKED_FROM - HOT : EARLY_FROM - HOT, :].bitcast(I32),
         )

@@ -21,10 +21,7 @@ BANKS = 8
 
 EARLY_FROM = 13
 PACKED_FROM = 5
-SCALAR_FROM = 14
-
 IN_TURN_FROM = 11
-BEHIND = {6: ("sums", 2, 0), 4: ("sums", 2, 1), 2: ("sums", 1, 0)}
 
 
 def tile_moe_hot_s_mlp_relu_kernel(
@@ -48,16 +45,16 @@ def tile_moe_hot_s_mlp_relu_kernel(
             for e in range(first, last):
                 into[e] = (tile, e - first)
 
-        def zeroed(name, shape, engine=nc.vector):
+        def zeroed(name, shape):
             tile = held.tile(shape, U8, name=name, align_bytes=64)
-            engine.memset(tile[:].bitcast(I32), 0)
+            nc.vector.memset(tile[:].bitcast(I32), 0)
             return tile
 
-        def load_scales(tile, place, hot, cold, first, last, lower=0):
+        def load_scales(queue, tile, place, hot, cold, first, last, lower=0):
             source, base = (hot, 0) if first < HOT else (cold, HOT)
             rows = source.rearrange("e s (q r) n -> r q (e s) n", r=4)[:, :, first - base : last - base, :]
             for r in range(4):
-                nc.sync.dma_start(
+                queue.dma_start(
                     tile[lower + r : P : 32, place : place + last - first, :].bitcast(I32), rows[r].bitcast(I32)
                 )
 
@@ -69,9 +66,8 @@ def tile_moe_hot_s_mlp_relu_kernel(
             tile, place = table[e]
             return tile[:, place, :]
 
-        early = zeroed("early", [P, E - EARLY_FROM, H])
         unpacked = zeroed("unpacked", [P, EARLY_FROM - PACKED_FROM, H])
-
+        early = zeroed("early", [P, E - EARLY_FROM, H])
         identity = held.tile([P, P], F32, name="identity")
         make_identity(nc, identity[:])
         late = zeroed("late", [P, HOT, H])
@@ -92,11 +88,10 @@ def tile_moe_hot_s_mlp_relu_kernel(
             w1c_scales.rearrange("e s b n -> b (e s) n")[:, PACKED_FROM - HOT : EARLY_FROM - HOT, :].bitcast(I32),
         )
         nc.sync.dma_start(token_words[:], x_words.rearrange("s p t d -> p (s t d)").bitcast(I32))
-
-        load_words(w1, "w1_first", w1h_words, w1c_words, SCALAR_FROM, E)
-        load_scales(early, 0, w1h_scales, w1c_scales, EARLY_FROM, E)
-        load_words(w1, "w1_second", w1h_words, w1c_words, 12, SCALAR_FROM)
-        load_words(w1, "w1_third", w1h_words, w1c_words, 8, 12)
+        load_words(w1, "w1_15", w1h_words, w1c_words, 14, 16)
+        load_scales(nc.sync, early, 0, w1h_scales, w1c_scales, EARLY_FROM, E)
+        load_words(w1, "w1_12", w1h_words, w1c_words, 12, 14)
+        load_words(w1, "w1_8", w1h_words, w1c_words, 8, 12)
 
         ordered_words, ordered_plane = {}, {}
 
@@ -114,13 +109,12 @@ def tile_moe_hot_s_mlp_relu_kernel(
                 planes.rearrange("p e (t m) -> p e t m", t=4), loaded.rearrange("p e (m t) -> p e t m", t=4)
             )
 
-        for e in reversed(range(SCALAR_FROM, E - 1)):
-            words = held.tile([P, 2 * H], U8, name="words_%d" % e, align_bytes=64)
-            nc.scalar.copy(
-                words[:].bitcast(U16).rearrange("p (t b n) -> p b t n", t=4, n=8),
-                row_of(w1, e).bitcast(U16).rearrange("p (b n t) -> p b t n", t=4, n=8),
-            )
-            ordered_words[e] = words[:]
+        words_14 = held.tile([P, 2 * H], U8, name="words_14", align_bytes=64)
+        nc.scalar.copy(
+            words_14[:].bitcast(U16).rearrange("p (t b n) -> p b t n", t=4, n=8),
+            row_of(w1, 14).bitcast(U16).rearrange("p (b n t) -> p b t n", t=4, n=8),
+        )
+        ordered_words[14] = words_14[:]
 
         early_ordered = held.tile([P, E - 1 - EARLY_FROM, H], U8, name="early_ordered", align_bytes=64)
         packed_ordered = held.tile([P, 1, H], U8, name="packed_ordered", align_bytes=64)
@@ -136,14 +130,14 @@ def tile_moe_hot_s_mlp_relu_kernel(
         reorder_planes(early_ordered[:, 0:1, :], early[:, 0:1, :])
         reorder_cold_words(12, 13)
 
-        load_words(w1, "w1_fourth", w1h_words, w1c_words, HOT, 8)
-        load_scales(late, 0, w1h_scales, w1c_scales, HOT, PACKED_FROM)
-        load_scales(late, 0, w1h_scales, w1c_scales, 0, HOT, lower=4)
+        load_words(w1, "w1_3", w1h_words, w1c_words, HOT, 8)
+        load_scales(nc.sync, late, 0, w1h_scales, w1c_scales, HOT, PACKED_FROM)
+        load_scales(nc.sync, late, 0, w1h_scales, w1c_scales, 0, HOT, lower=4)
         load_words(w2, "w2_cold", w2h_words, w2c_words, HOT, E)
-        load_scales(s2, HOT, w2h_scales, w2c_scales, HOT, E)
         load_words(w1, "w1_hot", w1h_words, w1c_words, 0, HOT)
+        load_scales(nc.sync, s2, HOT, w2h_scales, w2c_scales, HOT, E)
         load_words(w2, "w2_hot", w2h_words, w2c_words, 0, HOT)
-        load_scales(s2, 0, w2h_scales, w2c_scales, 0, HOT)
+        load_scales(nc.sync, s2, 0, w2h_scales, w2c_scales, 0, HOT)
 
         for first, last in ((10, 12), (8, 10), (7, 8), (5, 7), (3, 5)):
             reorder_cold_words(first, last)
@@ -167,16 +161,11 @@ def tile_moe_hot_s_mlp_relu_kernel(
         def codes_of(words, e):
             return words.bitcast(FP8X4 if e < HOT else FP4X4)
 
-        tenants = []
+        bank_of = {}
 
-        def next_bank(shape, key=None, behind=None):
-            if behind is None:
-                tenants.append(key)
-                behind = key
-            elif key is not None:
-                tenants[tenants.index(behind)] = key
-                behind = key
-            return psum.tile(shape, F32, name="bank_%d" % (tenants.index(behind) % BANKS))
+        def bank(shape, key, behind=None):
+            bank_of[key] = len(bank_of) % BANKS if behind is None else bank_of[behind]
+            return psum.tile(shape, F32, name="bank_%d" % bank_of[key])
 
         slot_words, slot_scales = {}, {}
 
@@ -192,16 +181,6 @@ def tile_moe_hot_s_mlp_relu_kernel(
             nc.vector.tensor_copy(tile[:, (first - low) * P : (last - low) * P], window.indirect(listed))
 
         word_window, byte_window = token_words[:].bitcast(U32), token_scales[:]
-        first_bytes = gathered("first_bytes", U8, 28, 32, slot_scales)
-        first_words = gathered("first_words", U32, 30, 32, slot_words)
-        second_words = gathered("second_words", U32, 26, 30, slot_words)
-        second_bytes = gathered("packed", U8, 24, 28, slot_scales)
-        gather(first_bytes, byte_window, 28, 32)
-        gather(first_words, word_window, 31, 32)
-        gather(first_words, word_window, 30, 31)
-        gather(second_words, word_window, 28, 30)
-        gather(second_words, word_window, 26, 28)
-        gather(second_bytes, byte_window, 24, 28)
 
         groups = [(12, 16), (8, 12), (6, 8), (4, 6), (2, 4), (1, 2), (0, 1)]
         grouped, group_tile = {}, {}
@@ -213,29 +192,27 @@ def tile_moe_hot_s_mlp_relu_kernel(
 
         hidden = held.tile([P, 2, 2, P, 2], BF16, name="hidden", align_bytes=64)
 
-        def first_layer_turned(e):
-            for half in (1, 0):
-                width = H // 2 if half else H
-                for low in range(0, H, width):
-                    sums = next_bank([P, width], ("sums", e, half, low))
-                    nc.tensor.matmul_mx(
-                        out=sums[:],
-                        lhsT=slot_words[2 * e + half].bitcast(FP8X4),
-                        lhsT_scale=slot_scales[2 * e + half],
-                        rhs=codes_of(row_of(w1, e)[:, 2 * low : 2 * (low + width)], e),
-                        rhs_scale=early[:, e - EARLY_FROM, low : low + width],
-                        start=True,
-                        stop=True,
-                    )
-                    nc.scalar.activation(
-                        hidden[:, half, :, low // 4 : (low + width) // 4, :],
-                        sums[:].rearrange("s (p u v) -> s u p v", u=2, v=2),
-                        RELU,
-                    )
+        def turned_product(e, half, width):
+            for low in range(0, H, width):
+                sums = bank([P, width], ("sums", e, half, low))
+                nc.tensor.matmul_mx(
+                    out=sums[:],
+                    lhsT=slot_words[2 * e + half].bitcast(FP8X4),
+                    lhsT_scale=slot_scales[2 * e + half],
+                    rhs=codes_of(row_of(w1, e)[:, 2 * low : 2 * (low + width)], e),
+                    rhs_scale=early[:, e - EARLY_FROM, low : low + width],
+                    start=True,
+                    stop=True,
+                )
+                nc.scalar.activation(
+                    hidden[:, half, :, low // 4 : (low + width) // 4, :],
+                    sums[:].rearrange("s (p u v) -> s u p v", u=2, v=2),
+                    RELU,
+                )
 
         def turn_and_weave(e):
             pairs = hidden[:].rearrange("s half u p v -> s half u (p v)").bitcast(F32)
-            turned = next_bank([P, 2, C], ("turned", e))
+            turned = bank([P, 2, C], ("turned", e))
             for half in range(2):
                 for u in range(2):
                     nc.tensor.transpose(turned[:, u, half * P : (half + 1) * P], pairs[:, half, u, :], identity[:])
@@ -244,44 +221,48 @@ def tile_moe_hot_s_mlp_relu_kernel(
                 turned[:].rearrange("p u c -> p c u"),
             )
 
-        def first_layer(e):
+        def first_product(e, half, behind=None):
             width = (4 if e < HOT else 2) * P
-            unread = []
-            for half in (1, 0):
-                sums = next_bank([P, 4, P], ("sums", e, half))
-                for t in range(4):
-                    nc.tensor.matmul_mx(
-                        out=sums[:, t, :],
-                        lhsT=codes_of(ordered_words[e][:, t * width : (t + 1) * width], e),
-                        lhsT_scale=ordered_plane[e][:, t * P : (t + 1) * P],
-                        rhs=slot_words[2 * e + half].bitcast(FP8X4),
-                        rhs_scale=slot_scales[2 * e + half],
-                        start=True,
-                        stop=True,
-                    )
-                unread.append((grouped[e][:, half * P : (half + 1) * P, :], sums[:].rearrange("p t s -> p s t")))
-            for written, sums in unread if e >= IN_TURN_FROM or e == 0 else reversed(unread):
-                nc.scalar.activation(written, sums, RELU)
+            sums = bank([P, 4, P], ("sums", e, half), behind)
+            for t in range(4):
+                nc.tensor.matmul_mx(
+                    out=sums[:, t, :],
+                    lhsT=codes_of(ordered_words[e][:, t * width : (t + 1) * width], e),
+                    lhsT_scale=ordered_plane[e][:, t * P : (t + 1) * P],
+                    rhs=slot_words[2 * e + half].bitcast(FP8X4),
+                    rhs_scale=slot_scales[2 * e + half],
+                    start=True,
+                    stop=True,
+                )
+            return grouped[e][:, half * P : (half + 1) * P, :], sums[:].rearrange("p t s -> p s t")
 
-        def quantise(name, values, code_room):
+        def relu_on_scalar(written, sums):
+            nc.scalar.activation(written, sums, RELU)
+
+        def quantise(values, code_room, scale_room):
             columns = values.shape[1]
             codes = held.tile([P, columns], U32, name=code_room, align_bytes=64)
-            scales = held.tile([P, columns], U8, name=name + "_scales", align_bytes=64)
+            scales = held.tile([P, columns], U8, name=scale_room, align_bytes=64)
             nc.vector.quantize_mx(
                 out=codes[:].bitcast(FP8X4), scales=scales[:], in_=values.rearrange("p c t -> p (c t)")
             )
             return codes, scales
 
-        def second_product(results, e, codes, scales):
-            nc.tensor.matmul_mx(
-                out=results,
-                lhsT=codes_of(row_of(w2, e), e),
-                lhsT_scale=s2[:, e, :],
-                rhs=codes.bitcast(FP8X4),
-                rhs_scale=scales,
-                start=True,
-                stop=True,
-            )
+        def second_product(first_slot, last_slot, quantised, low, behind):
+            codes, scales = quantised
+            results = bank([P, last_slot - first_slot], ("results", first_slot), behind)
+            for start in range(first_slot, last_slot, C):
+                e, end = start // C, min(start + C, last_slot)
+                nc.tensor.matmul_mx(
+                    out=results[:, start - first_slot : end - first_slot],
+                    lhsT=codes_of(row_of(w2, e), e),
+                    lhsT_scale=s2[:, e, :],
+                    rhs=codes[:, start - low : end - low].bitcast(FP8X4),
+                    rhs_scale=scales[:, start - low : end - low],
+                    start=True,
+                    stop=True,
+                )
+            return results
 
         def store(results, first_slot, copy, queue):
             columns = results.shape[1]
@@ -289,56 +270,63 @@ def tile_moe_hot_s_mlp_relu_kernel(
             copy(staged[:], results[:])
             queue.dma_start(out[:, first_slot : first_slot + columns], staged[:])
 
-        on_vector = (6, 4)
+        def pair_out(e, quantised, low, behind):
+            results = second_product(e * C, (e + 2) * C, quantised, low * C, behind)
+            store(results, e * C, nc.scalar.copy, nc.sync)
 
-        def second_layer(low, high, codes, scales):
-            for first in reversed(range(low, high, 2)):
-                last = min(first + 2, high)
-                results = next_bank([P, (last - first) * C], ("results", first), BEHIND.get(first))
-                for e in range(first, last):
-                    slots = slice((e - low) * C, (e - low + 1) * C)
-                    second_product(
-                        results[:, (e - first) * C : (e - first + 1) * C], e, codes[:, slots], scales[:, slots]
-                    )
-                copy = nc.vector.tensor_copy if first in on_vector else nc.scalar.copy
-                store(results, first * C, copy, nc.sync)
+        first_bytes = gathered("first_bytes", U8, 28, 32, slot_scales)
+        gather(first_bytes, byte_window, 28, 32)
+        gather(gathered("slot_words_31", U32, 31, 32, slot_words), word_window, 31, 32)
+        gather(gathered("slot_words_30", U32, 30, 31, slot_words), word_window, 30, 31)
+        second_words = gathered("second_words", U32, 26, 30, slot_words)
+        gather(second_words, word_window, 28, 30)
+        gather(second_words, word_window, 26, 28)
+        turned_product(E - 1, 1, H // 2)
+        gather(gathered("slot_words_31", U8, 24, 28, slot_scales), byte_window, 24, 28)
+        turned_product(E - 1, 0, H)
+        most_words = gathered("slot_words_30", U32, 6, 26, slot_words)
+        most_bytes = gathered("w1_15", U8, 4, 24, slot_scales)
+        for first in range(22, 5, -4):
+            gather(most_words, word_window, first, first + 4)
+            gather(most_bytes, byte_window, first - 2, first + 2)
 
         quantised = {}
-        for e in reversed(range(E)):
-            if e == E - 1:
-                first_layer_turned(e)
-            else:
-                first_layer(e)
+        for e in reversed(range(HOT, E - 1)):
+            unread = [first_product(e, 1), first_product(e, 0, ("sums", 6, 1) if e == HOT else None)]
+            for written, sums in unread if e >= IN_TURN_FROM else reversed(unread):
+                relu_on_scalar(written, sums)
             if e == E - 3:
                 turn_and_weave(E - 1)
             if e == 5:
-                quantised[12] = quantise("h_12", group_tile[12][:], "words_5")
-                quantised[8] = quantise("h_8", group_tile[8][:], "words_8")
-                last_words = gathered("grouped_12", U32, 0, 6, slot_words)
-                last_bytes = gathered("grouped_8", U8, 0, 4, slot_scales)
-                gather(last_words, word_window, 2, 6)
-                gather(last_bytes, byte_window, 0, 4)
-                gather(last_words, word_window, 0, 2)
-            if e == E - 1:
-                most_words = gathered("first_words", U32, 6, 26, slot_words)
-                most_bytes = gathered("w1_first", U8, 4, 24, slot_scales)
-                for first in range(22, 5, -4):
-                    gather(most_words, word_window, first, first + 4)
-                    gather(most_bytes, byte_window, first - 2, first + 2)
-            if e == 3:
-                second_layer(12, 16, *quantised[12])
-                second_layer(8, 12, *quantised[8])
-        for low, high in groups[2:6]:
-            second_layer(low, high, *quantise("h_%d" % low, group_tile[low][:], "h_%d_codes" % low))
+                quantised[12] = quantise(group_tile[12][:], "words_5", "scales_12")
+                quantised[8] = quantise(group_tile[8][:], "words_8", "scales_8")
+                gather(gathered("grouped_12", U32, 2, 6, slot_words), word_window, 2, 6)
+                quantised[6] = quantise(group_tile[6][:], "codes_6", "scales_6")
 
-        halves = [
-            (half, quantise("last_%d" % half, grouped[0][:, half * P : (half + 1) * P, :], "last_%d_codes" % half))
+        gather(gathered("words_3", U8, 0, 4, slot_scales), byte_window, 0, 4)
+        gather(gathered("slot_words_30", U32, 0, 2, slot_words), word_window, 0, 2)
+        quantised[4] = quantise(group_tile[4][:], "codes_4", "scales_4")
+        pair_out(14, quantised[12], 12, ("sums", 4, 0))
+        pair_out(12, quantised[12], 12, ("sums", 4, 1))
+        pair_out(10, quantised[8], 8, ("sums", 3, 0))
+        pair_out(8, quantised[8], 8, ("sums", 3, 1))
+
+        relu_on_scalar(*first_product(2, 1, ("results", 14 * C)))
+        relu_on_scalar(*first_product(2, 0, ("results", 12 * C)))
+        quantised[2] = quantise(group_tile[2][:], "codes_2", "scales_2")
+        pair_out(6, quantised[6], 6, ("results", 10 * C))
+        relu_on_scalar(*first_product(1, 1, ("results", 8 * C)))
+        relu_on_scalar(*first_product(1, 0, ("sums", 2, 1)))
+        relu_on_scalar(*first_product(0, 1, ("sums", 2, 0)))
+        store(second_product(4 * C, 6 * C, quantised[4], 4 * C, ("results", 6 * C)), 4 * C, nc.vector.tensor_copy, nc.sync)
+        quantised[1] = quantise(group_tile[1][:], "codes_1", "scales_1")
+        relu_on_scalar(*first_product(0, 0, ("sums", 1, 1)))
+        store(second_product(3 * C, 4 * C, quantised[2], 2 * C, ("sums", 1, 0)), 3 * C, nc.vector.tensor_copy, nc.sync)
+        store(second_product(2 * C, 3 * C, quantised[2], 2 * C, ("results", 4 * C)), 2 * C, nc.scalar.copy, nc.sync)
+        store(second_product(C, 2 * C, quantised[1], C, ("sums", 0, 1)), C, nc.scalar.copy, nc.sync)
+        halves = {
+            half: quantise(grouped[0][:, half * P : (half + 1) * P, :], "codes_0_%d" % half, "scales_0_%d" % half)
             for half in (1, 0)
-        ]
-        for half, (codes, scales) in halves:
-            results = next_bank([P, P], ("last", half))
-            second_product(results[:], 0, codes[:], scales[:])
-            if half:
-                store(results, half * P, nc.vector.tensor_copy, nc.sync)
-            else:
-                store(results, half * P, nc.scalar.copy, nc.scalar)
+        }
+        store(second_product(P, C, halves[1], P, ("results", 3 * C)), P, nc.vector.tensor_copy, nc.sync)
+        store(second_product(0, P, halves[0], 0, ("sums", 0, 0)), 0, nc.scalar.copy, nc.scalar)

@@ -31,6 +31,7 @@ def tile_moe_hot_s_mlp_relu_kernel(
     nc = tc.nc
     with ExitStack() as ctx:
         held = ctx.enter_context(tc.tile_pool(name="held", bufs=1))
+        shared = ctx.enter_context(tc.tile_pool(name="shared", bufs=1))
         psum = ctx.enter_context(tc.psum_pool(name="psum", bufs=1))
 
         w1, w2 = {}, {}
@@ -68,8 +69,6 @@ def tile_moe_hot_s_mlp_relu_kernel(
 
         unpacked = zeroed("unpacked", [P, EARLY_FROM - PACKED_FROM, H])
         early = zeroed("early", [P, E - EARLY_FROM, H])
-        identity = held.tile([P, P], F32, name="identity")
-        make_identity(nc, identity[:])
         late = zeroed("late", [P, HOT, H])
         s2 = zeroed("s2", [P, E, N])
 
@@ -78,8 +77,8 @@ def tile_moe_hot_s_mlp_relu_kernel(
         token_scales = held.tile([P, T], U8, name="token_scales", align_bytes=64)
         quadrants = x_scales.rearrange("s (q r) t -> q s r t", r=4).bitcast(I32)
         nc.sync.dma_start(offsets[:], offs)
-        for q in (0, 2, 1, 3):
-            nc.sync.dma_start(
+        for q, queue in ((2, nc.scalar), (0, nc.sync), (1, nc.scalar), (3, nc.sync)):
+            queue.dma_start(
                 token_scales[32 * q : 32 * (q + 1), :].bitcast(I32), quadrants[q].to_broadcast([8, 4, T // 4])
             )
         packed = held.tile([P, H], U8, name="packed", align_bytes=64)
@@ -89,7 +88,7 @@ def tile_moe_hot_s_mlp_relu_kernel(
         )
         nc.sync.dma_start(token_words[:], x_words.rearrange("s p t d -> p (s t d)").bitcast(I32))
         load_words(w1, "w1_15", w1h_words, w1c_words, 14, 16)
-        load_scales(nc.sync, early, 0, w1h_scales, w1c_scales, EARLY_FROM, E)
+        load_scales(nc.scalar, early, 0, w1h_scales, w1c_scales, EARLY_FROM, E)
         load_words(w1, "w1_12", w1h_words, w1c_words, 12, 14)
         load_words(w1, "w1_8", w1h_words, w1c_words, 8, 12)
 
@@ -120,6 +119,8 @@ def tile_moe_hot_s_mlp_relu_kernel(
         packed_ordered = held.tile([P, 1, H], U8, name="packed_ordered", align_bytes=64)
         late_ordered = held.tile([P, HOT, H], U8, name="late_ordered", align_bytes=64)
         reorder_planes(packed_ordered[:], packed[:].unsqueeze(1))
+        identity = held.tile([P, P], F32, name="packed", align_bytes=64)
+        make_identity(nc, identity[:])
         reorder_planes(early_ordered[:, 1:2, :], early[:, 1:2, :])
         for q in (0, 2, 1, 3):
             nc.sync.dma_start(
@@ -134,8 +135,8 @@ def tile_moe_hot_s_mlp_relu_kernel(
         load_scales(nc.sync, late, 0, w1h_scales, w1c_scales, HOT, PACKED_FROM)
         load_scales(nc.sync, late, 0, w1h_scales, w1c_scales, 0, HOT, lower=4)
         load_words(w2, "w2_cold", w2h_words, w2c_words, HOT, E)
-        load_words(w1, "w1_hot", w1h_words, w1c_words, 0, HOT)
         load_scales(nc.sync, s2, HOT, w2h_scales, w2c_scales, HOT, E)
+        load_words(w1, "w1_hot", w1h_words, w1c_words, 0, HOT)
         load_words(w2, "w2_hot", w2h_words, w2c_words, 0, HOT)
         load_scales(nc.sync, s2, 0, w2h_scales, w2c_scales, 0, HOT)
 
@@ -169,8 +170,9 @@ def tile_moe_hot_s_mlp_relu_kernel(
 
         slot_words, slot_scales = {}, {}
 
-        def gathered(name, dtype, low, high, into):
-            tile = held.tile([P, (high - low) * P], dtype, name=name, align_bytes=64)
+        def gathered(name, dtype, low, high, into, offset=None):
+            pool = held if offset is None else shared
+            tile = pool.tile([P, (high - low) * P], dtype, name=name, align_bytes=64, offset=offset)
             for s in range(low, high):
                 into[s] = tile[:, (s - low) * P : (s - low + 1) * P]
             return tile, low
@@ -212,7 +214,7 @@ def tile_moe_hot_s_mlp_relu_kernel(
 
         def turn_and_weave(e):
             pairs = hidden[:].rearrange("s half u p v -> s half u (p v)").bitcast(F32)
-            turned = bank([P, 2, C], ("turned", e))
+            turned = bank([P, 2, C], ("turned", e), ("sums", e - 1, 0))
             for half in range(2):
                 for u in range(2):
                     nc.tensor.transpose(turned[:, u, half * P : (half + 1) * P], pairs[:, half, u, :], identity[:])
@@ -270,63 +272,54 @@ def tile_moe_hot_s_mlp_relu_kernel(
             copy(staged[:], results[:])
             queue.dma_start(out[:, first_slot : first_slot + columns], staged[:])
 
-        def pair_out(e, quantised, low, behind):
+        def pair_out(e, quantised, low, behind, copy):
             results = second_product(e * C, (e + 2) * C, quantised, low * C, behind)
-            store(results, e * C, nc.scalar.copy, nc.sync)
+            store(results, e * C, copy, nc.sync)
 
         first_bytes = gathered("first_bytes", U8, 28, 32, slot_scales)
         gather(first_bytes, byte_window, 28, 32)
         gather(gathered("slot_words_31", U32, 31, 32, slot_words), word_window, 31, 32)
-        gather(gathered("slot_words_30", U32, 30, 31, slot_words), word_window, 30, 31)
+        gather(gathered("slot_words_30", U32, 30, 31, slot_words, 18 * P), word_window, 30, 31)
         second_words = gathered("second_words", U32, 26, 30, slot_words)
         gather(second_words, word_window, 28, 30)
         gather(second_words, word_window, 26, 28)
         turned_product(E - 1, 1, H // 2)
         gather(gathered("slot_words_31", U8, 24, 28, slot_scales), byte_window, 24, 28)
         turned_product(E - 1, 0, H)
-        most_words = gathered("slot_words_30", U32, 6, 26, slot_words)
-        most_bytes = gathered("w1_15", U8, 4, 24, slot_scales)
+        most_words = gathered("most_words", U32, 6, 26, slot_words, 20 * P)
+        most_bytes = gathered("most_bytes", U8, 4, 24, slot_scales, 0)
         for first in range(22, 5, -4):
             gather(most_words, word_window, first, first + 4)
             gather(most_bytes, byte_window, first - 2, first + 2)
 
         quantised = {}
-        for e in reversed(range(HOT, E - 1)):
-            unread = [first_product(e, 1), first_product(e, 0, ("sums", 6, 1) if e == HOT else None)]
-            for written, sums in unread if e >= IN_TURN_FROM else reversed(unread):
+        for e in reversed(range(E - 1)):
+            unread = [first_product(e, half) for half in (1, 0)]
+            for written, sums in unread if e >= IN_TURN_FROM or e == 0 else reversed(unread):
                 relu_on_scalar(written, sums)
             if e == E - 3:
                 turn_and_weave(E - 1)
             if e == 5:
                 quantised[12] = quantise(group_tile[12][:], "words_5", "scales_12")
                 quantised[8] = quantise(group_tile[8][:], "words_8", "scales_8")
-                gather(gathered("grouped_12", U32, 2, 6, slot_words), word_window, 2, 6)
-                quantised[6] = quantise(group_tile[6][:], "codes_6", "scales_6")
+                last_words = gathered("grouped_12", U32, 0, 6, slot_words)
+                last_bytes = gathered("grouped_8", U8, 0, 4, slot_scales)
+                gather(last_words, word_window, 2, 6)
+                gather(last_bytes, byte_window, 0, 4)
+                gather(last_words, word_window, 0, 2)
+            if e == HOT:
+                for pair in (14, 12, 10, 8):
+                    low = pair // 4 * 4
+                    pair_out(pair, quantised[low], low, None, nc.scalar.copy)
 
-        gather(gathered("words_3", U8, 0, 4, slot_scales), byte_window, 0, 4)
-        gather(gathered("slot_words_30", U32, 0, 2, slot_words), word_window, 0, 2)
-        quantised[4] = quantise(group_tile[4][:], "codes_4", "scales_4")
-        pair_out(14, quantised[12], 12, ("sums", 4, 0))
-        pair_out(12, quantised[12], 12, ("sums", 4, 1))
-        pair_out(10, quantised[8], 8, ("sums", 3, 0))
-        pair_out(8, quantised[8], 8, ("sums", 3, 1))
-
-        relu_on_scalar(*first_product(2, 1, ("results", 14 * C)))
-        relu_on_scalar(*first_product(2, 0, ("results", 12 * C)))
-        quantised[2] = quantise(group_tile[2][:], "codes_2", "scales_2")
-        pair_out(6, quantised[6], 6, ("results", 10 * C))
-        relu_on_scalar(*first_product(1, 1, ("results", 8 * C)))
-        relu_on_scalar(*first_product(1, 0, ("sums", 2, 1)))
-        relu_on_scalar(*first_product(0, 1, ("sums", 2, 0)))
-        store(second_product(4 * C, 6 * C, quantised[4], 4 * C, ("results", 6 * C)), 4 * C, nc.vector.tensor_copy, nc.sync)
+        pair_out(6, quantise(group_tile[6][:], "codes_6", "scales_6"), 6, ("sums", 2, 0), nc.vector.tensor_copy)
+        pair_out(4, quantise(group_tile[4][:], "codes_4", "scales_4"), 4, ("sums", 2, 1), nc.vector.tensor_copy)
+        pair_out(2, quantise(group_tile[2][:], "codes_2", "scales_2"), 2, ("sums", 1, 0), nc.scalar.copy)
         quantised[1] = quantise(group_tile[1][:], "codes_1", "scales_1")
-        relu_on_scalar(*first_product(0, 0, ("sums", 1, 1)))
-        store(second_product(3 * C, 4 * C, quantised[2], 2 * C, ("sums", 1, 0)), 3 * C, nc.vector.tensor_copy, nc.sync)
-        store(second_product(2 * C, 3 * C, quantised[2], 2 * C, ("results", 4 * C)), 2 * C, nc.scalar.copy, nc.sync)
-        store(second_product(C, 2 * C, quantised[1], C, ("sums", 0, 1)), C, nc.scalar.copy, nc.sync)
+        store(second_product(C, 2 * C, quantised[1], C, ("results", 10 * C)), C, nc.scalar.copy, nc.sync)
         halves = {
             half: quantise(grouped[0][:, half * P : (half + 1) * P, :], "codes_0_%d" % half, "scales_0_%d" % half)
             for half in (1, 0)
         }
-        store(second_product(P, C, halves[1], P, ("results", 3 * C)), P, nc.vector.tensor_copy, nc.sync)
-        store(second_product(0, P, halves[0], 0, ("sums", 0, 0)), 0, nc.scalar.copy, nc.scalar)
+        store(second_product(P, C, halves[1], P, ("results", 8 * C)), P, nc.vector.tensor_copy, nc.sync)
+        store(second_product(0, P, halves[0], 0, ("results", 4 * C)), 0, nc.scalar.copy, nc.scalar)

@@ -46,9 +46,9 @@ def tile_moe_hot_s_mlp_relu_kernel(
             for e in range(first, last):
                 into[e] = (tile, e - first)
 
-        def zeroed(name, shape):
+        def zeroed(name, shape, engine):
             tile = held.tile(shape, U8, name=name, align_bytes=64)
-            nc.vector.memset(tile[:].bitcast(I32), 0)
+            engine.memset(tile[:].bitcast(I32), 0)
             return tile
 
         def load_scales(queue, tile, place, hot, cold, first, last, lower=0):
@@ -67,10 +67,12 @@ def tile_moe_hot_s_mlp_relu_kernel(
             tile, place = table[e]
             return tile[:, place, :]
 
-        unpacked = zeroed("unpacked", [P, EARLY_FROM - PACKED_FROM, H])
-        early = zeroed("early", [P, E - EARLY_FROM, H])
-        late = zeroed("late", [P, HOT, H])
-        s2 = zeroed("s2", [P, E, N])
+        early = zeroed("early", [P, E - EARLY_FROM, H], nc.vector)
+        unpacked = zeroed("unpacked", [P, EARLY_FROM - PACKED_FROM, H], nc.vector)
+        identity = held.tile([P, P], F32, name="identity")
+        make_identity(nc, identity[:])
+        late = zeroed("late", [P, HOT, H], nc.gpsimd)
+        s2 = zeroed("s2", [P, E, N], nc.gpsimd)
 
         token_words = held.tile([P, T], I32, name="token_words", align_bytes=64)
         offsets = held.tile([P, E * C // 16], U16, name="offsets")
@@ -88,7 +90,7 @@ def tile_moe_hot_s_mlp_relu_kernel(
         )
         nc.sync.dma_start(token_words[:], x_words.rearrange("s p t d -> p (s t d)").bitcast(I32))
         load_words(w1, "w1_15", w1h_words, w1c_words, 14, 16)
-        load_scales(nc.scalar, early, 0, w1h_scales, w1c_scales, EARLY_FROM, E)
+        load_scales(nc.sync, early, 0, w1h_scales, w1c_scales, EARLY_FROM, E)
         load_words(w1, "w1_12", w1h_words, w1c_words, 12, 14)
         load_words(w1, "w1_8", w1h_words, w1c_words, 8, 12)
 
@@ -119,8 +121,6 @@ def tile_moe_hot_s_mlp_relu_kernel(
         packed_ordered = held.tile([P, 1, H], U8, name="packed_ordered", align_bytes=64)
         late_ordered = held.tile([P, HOT, H], U8, name="late_ordered", align_bytes=64)
         reorder_planes(packed_ordered[:], packed[:].unsqueeze(1))
-        identity = held.tile([P, P], F32, name="packed", align_bytes=64)
-        make_identity(nc, identity[:])
         reorder_planes(early_ordered[:, 1:2, :], early[:, 1:2, :])
         for q in (0, 2, 1, 3):
             nc.sync.dma_start(
@@ -214,7 +214,7 @@ def tile_moe_hot_s_mlp_relu_kernel(
 
         def turn_and_weave(e):
             pairs = hidden[:].rearrange("s half u p v -> s half u (p v)").bitcast(F32)
-            turned = bank([P, 2, C], ("turned", e), ("sums", e - 1, 0))
+            turned = bank([P, 2, C], ("turned", e))
             for half in range(2):
                 for u in range(2):
                     nc.tensor.transpose(turned[:, u, half * P : (half + 1) * P], pairs[:, half, u, :], identity[:])
@@ -312,9 +312,11 @@ def tile_moe_hot_s_mlp_relu_kernel(
                     low = pair // 4 * 4
                     pair_out(pair, quantised[low], low, None, nc.scalar.copy)
 
-        pair_out(6, quantise(group_tile[6][:], "codes_6", "scales_6"), 6, ("sums", 2, 0), nc.vector.tensor_copy)
-        pair_out(4, quantise(group_tile[4][:], "codes_4", "scales_4"), 4, ("sums", 2, 1), nc.vector.tensor_copy)
-        pair_out(2, quantise(group_tile[2][:], "codes_2", "scales_2"), 2, ("sums", 1, 0), nc.scalar.copy)
+        for low in (6, 4, 2):
+            quantised[low] = quantise(group_tile[low][:], "codes_%d" % low, "scales_%d" % low)
+        pair_out(6, quantised[6], 6, ("sums", 2, 1), nc.vector.tensor_copy)
+        pair_out(4, quantised[4], 4, ("sums", 1, 0), nc.vector.tensor_copy)
+        pair_out(2, quantised[2], 2, ("sums", 2, 0), nc.scalar.copy)
         quantised[1] = quantise(group_tile[1][:], "codes_1", "scales_1")
         store(second_product(C, 2 * C, quantised[1], C, ("results", 10 * C)), C, nc.scalar.copy, nc.sync)
         halves = {
@@ -322,4 +324,4 @@ def tile_moe_hot_s_mlp_relu_kernel(
             for half in (1, 0)
         }
         store(second_product(P, C, halves[1], P, ("results", 8 * C)), P, nc.vector.tensor_copy, nc.sync)
-        store(second_product(0, P, halves[0], 0, ("results", 4 * C)), 0, nc.scalar.copy, nc.scalar)
+        store(second_product(0, P, halves[0], 0, ("results", 6 * C)), 0, nc.scalar.copy, nc.scalar)

from contextlib import ExitStack

import concourse.mybir as mybir
from concourse.masks import make_identity

K, T, E, C, H, N, HOT = 512, 1024, 16, 256, 512, 128, 3
FLOPS = 2 * E * C * (K * H + H * N)

F32 = mybir.dt.float32
BF16 = mybir.dt.bfloat16
I32 = mybir.dt.int32
U32 = mybir.dt.uint32
U16 = mybir.dt.uint16
U8 = mybir.dt.uint8
FP8X4 = mybir.dt.float8_e4m3fn_x4
FP4X4 = mybir.dt.float4_e2m1fn_x4
RELU = mybir.ActivationFunctionType.Relu

P = 128
BANKS = 8

EARLY_FROM = 13
PACKED_FROM = 5
IN_TURN_FROM = 11


def tile_moe_hot_s_mlp_relu_kernel(
    tc, x_words, x_scales, w1h_words, w1h_scales, w2h_words, w2h_scales,
    w1c_words, w1c_scales, w2c_words, w2c_scales, offs, out,
):
    nc = tc.nc
    with ExitStack() as ctx:
        held = ctx.enter_context(tc.tile_pool(name="held", bufs=1))
        shared = ctx.enter_context(tc.tile_pool(name="shared", bufs=1))
        psum = ctx.enter_context(tc.psum_pool(name="psum", bufs=1))

        w1, w2 = {}, {}

        def load_words(into, name, hot, cold, first, last):
            if first < HOT:
                rows = hot.rearrange("e s p n d -> p (e s) (n d)")[:, first:last, :]
            else:
                rows = cold.rearrange("e s p w -> p (e s) w")[:, first - HOT : last - HOT, :]
            tile = held.tile([P, last - first, rows.shape[2]], U8, name=name, align_bytes=64)
            nc.sync.dma_start(tile[:].bitcast(I32), rows.bitcast(I32))
            for e in range(first, last):
                into[e] = (tile, e - first)

        def zeroed(name, shape, engine):
            tile = held.tile(shape, U8, name=name, align_bytes=64)
            engine.memset(tile[:].bitcast(I32), 0)
            return tile

        def load_scales(queue, tile, place, hot, cold, first, last, lower=0):
            source, base = (hot, 0) if first < HOT else (cold, HOT)
            rows = source.rearrange("e s (q r) n -> r q (e s) n", r=4)[:, :, first - base : last - base, :]
            for r in range(4):
                queue.dma_start(
                    tile[lower + r : P : 32, place : place + last - first, :].bitcast(I32), rows[r].bitcast(I32)
                )

        def rows_of(table, first, last):
            tile, place = table[first]
            return tile[:, place : place + last - first, :]

        def row_of(table, e):
            tile, place = table[e]
            return tile[:, place, :]

        early = zeroed("early", [P, E - EARLY_FROM, H], nc.vector)
        unpacked = zeroed("unpacked", [P, EARLY_FROM - PACKED_FROM, H], nc.vector)
        identity = held.tile([P, P], F32, name="identity")
        make_identity(nc, identity[:])
        late = zeroed("late", [P, HOT, H], nc.gpsimd)
        s2 = zeroed("s2", [P, E, N], nc.gpsimd)

        token_words = held.tile([P, T], I32, name="token_words", align_bytes=64)
        offsets = held.tile([P, E * C // 16], U16, name="offsets")
        token_scales = held.tile([P, T], U8, name="token_scales", align_bytes=64)
        quadrants = x_scales.rearrange("s (q r) t -> q s r t", r=4).bitcast(I32)
        nc.sync.dma_start(offsets[:], offs)
        for q, queue in ((2, nc.scalar), (0, nc.sync), (1, nc.scalar), (3, nc.sync)):
            queue.dma_start(
                token_scales[32 * q : 32 * (q + 1), :].bitcast(I32), quadrants[q].to_broadcast([8, 4, T // 4])
            )
        packed = held.tile([P, H], U8, name="packed", align_bytes=64)
        nc.scalar.dma_start(
            packed[:].bitcast(I32),
            w1c_scales.rearrange("e s b n -> b (e s) n")[:, PACKED_FROM - HOT : EARLY_FROM - HOT, :].bitcast(I32),
        )
        nc.sync.dma_start(token_words[:], x_words.rearrange("s p t d -> p (s t d)").bitcast(I32))
        load_words(w1, "w1_15", w1h_words, w1c_words, 14, 16)
        load_scales(nc.sync, early, 0, w1h_scales, w1c_scales, EARLY_FROM, E)
        load_words(w1, "w1_12", w1h_words, w1c_words, 12, 14)
        load_words(w1, "w1_8", w1h_words, w1c_words, 8, 12)

        ordered_words, ordered_plane = {}, {}

        def reorder_cold_words(first, last):
            words = held.tile([P, last - first, 2 * H], U8, name="words_%d" % first, align_bytes=64)
            nc.gpsimd.tensor_copy(
                words[:].bitcast(U16).rearrange("p e (t m) -> p e t m", t=4),
                rows_of(w1, first, last).bitcast(U16).rearrange("p e (m t) -> p e t m", t=4),
            )
            for e in range(first, last):
                ordered_words[e] = words[:, e - first, :]

        def reorder_planes(planes, loaded):
            nc.gpsimd.tensor_copy(
                planes.rearrange("p e (t m) -> p e t m", t=4), loaded.rearrange("p e (m t) -> p e t m", t=4)
            )

        words_14 = held.tile([P, 2 * H], U8, name="words_14", align_bytes=64)
        nc.scalar.copy(
            words_14[:].bitcast(U16).rearrange("p (t b n) -> p b t n", t=4, n=8),
            row_of(w1, 14).bitcast(U16).rearrange("p (b n t) -> p b t n", t=4, n=8),
        )
        ordered_words[14] = words_14[:]

        early_ordered = held.tile([P, E - 1 - EARLY_FROM, H], U8, name="early_ordered", align_bytes=64)
        packed_ordered = held.tile([P, 1, H], U8, name="packed_ordered", align_bytes=64)
        late_ordered = held.tile([P, HOT, H], U8, name="late_ordered", align_bytes=64)
        reorder_planes(packed_ordered[:], packed[:].unsqueeze(1))
        reorder_planes(early_ordered[:, 1:2, :], early[:, 1:2, :])
        for q in (0, 2, 1, 3):
            nc.sync.dma_start(
                unpacked[32 * q : 32 * q + 4, :, :].bitcast(I32),
                packed_ordered[32 * q : 32 * (q + 1), 0, :].bitcast(I32),
            )
        reorder_cold_words(13, 14)
        reorder_planes(early_ordered[:, 0:1, :], early[:, 0:1, :])
        reorder_cold_words(12, 13)

        load_words(w1, "w1_3", w1h_words, w1c_words, HOT, 8)
        load_scales(nc.sync, late, 0, w1h_scales, w1c_scales, HOT, PACKED_FROM)
        load_scales(nc.sync, late, 0, w1h_scales, w1c_scales, 0, HOT, lower=4)
        load_words(w2, "w2_cold", w2h_words, w2c_words, HOT, E)
        load_scales(nc.sync, s2, HOT, w2h_scales, w2c_scales, HOT, E)
        load_words(w1, "w1_hot", w1h_words, w1c_words, 0, HOT)
        load_words(w2, "w2_hot", w2h_words, w2c_words, 0, HOT)
        load_scales(nc.sync, s2, 0, w2h_scales, w2c_scales, 0, HOT)

        for first, last in ((10, 12), (8, 10), (7, 8), (5, 7), (3, 5)):
            reorder_cold_words(first, last)
        reorder_planes(late_ordered[:], late[:])
        hot_words = held.tile([P, HOT, H], U32, name="hot_words", align_bytes=64)
        nc.gpsimd.tensor_copy(
            hot_words[:].rearrange("p e (t b n) -> p e b t n", t=4, n=4),
            rows_of(w1, 0, HOT).bitcast(U32).rearrange("p e (b n t) -> p e b t n", t=4, n=4),
        )
        for e in range(E - 1):
            if e >= EARLY_FROM:
                ordered_plane[e] = early_ordered[:, e - EARLY_FROM, :]
            elif e >= PACKED_FROM:
                ordered_plane[e] = unpacked[:, e - PACKED_FROM, :]
            elif e >= HOT:
                ordered_plane[e] = late_ordered[:, e - HOT, :]
            else:
                ordered_plane[e] = late_ordered[4:P, e, :]
                ordered_words[e] = hot_words[:, e, :].bitcast(U8)

        def codes_of(words, e):
            return words.bitcast(FP8X4 if e < HOT else FP4X4)

        bank_of = {}

        def bank(shape, key, behind=None):
            bank_of[key] = len(bank_of) % BANKS if behind is None else bank_of[behind]
            return psum.tile(shape, F32, name="bank_%d" % bank_of[key])

        slot_words, slot_scales = {}, {}

        def gathered(name, dtype, low, high, into, offset=None):
            pool = held if offset is None else shared
            tile = pool.tile([P, (high - low) * P], dtype, name=name, align_bytes=64, offset=offset)
            for s in range(low, high):
                into[s] = tile[:, (s - low) * P : (s - low + 1) * P]
            return tile, low

        def gather(room, window, first, last):
            tile, low = room
            listed = offsets[:, first * P // 16 : last * P // 16]
            nc.vector.tensor_copy(tile[:, (first - low) * P : (last - low) * P], window.indirect(listed))

        word_window, byte_window = token_words[:].bitcast(U32), token_scales[:]

        groups = [(12, 16), (8, 12), (6, 8), (4, 6), (2, 4), (1, 2), (0, 1)]
        grouped, group_tile = {}, {}
        for first, last in groups:
            tile = held.tile([P, (last - first) * C, 4], BF16, name="grouped_%d" % first, align_bytes=64)
            group_tile[first] = tile
            for e in range(first, last):
                grouped[e] = tile[:, (e - first) * C : (e - first + 1) * C, :]

        hidden = held.tile([P, 2, 2, P, 2], BF16, name="hidden", align_bytes=64)

        def turned_product(e, half, width):
            for low in range(0, H, width):
                sums = bank([P, width], ("sums", e, half, low))
                nc.tensor.matmul_mx(
                    out=sums[:],
                    lhsT=slot_words[2 * e + half].bitcast(FP8X4),
                    lhsT_scale=slot_scales[2 * e + half],
                    rhs=codes_of(row_of(w1, e)[:, 2 * low : 2 * (low + width)], e),
                    rhs_scale=early[:, e - EARLY_FROM, low : low + width],
                    start=True,
                    stop=True,
                )
                nc.scalar.activation(
                    hidden[:, half, :, low // 4 : (low + width) // 4, :],
                    sums[:].rearrange("s (p u v) -> s u p v", u=2, v=2),
                    RELU,
                )

        def turn_and_weave(e):
            pairs = hidden[:].rearrange("s half u p v -> s half u (p v)").bitcast(F32)
            turned = bank([P, 2, C], ("turned", e))
            for half in range(2):
                for u in range(2):
                    nc.tensor.transpose(turned[:, u, half * P : (half + 1) * P], pairs[:, half, u, :], identity[:])
            nc.scalar.copy(
                grouped[e].rearrange("p c t -> p (c t)").bitcast(F32).rearrange("p (c u) -> p c u", u=2),
                turned[:].rearrange("p u c -> p c u"),
            )

        def first_product(e, half, behind=None):
            width = (4 if e < HOT else 2) * P
            sums = bank([P, 4, P], ("sums", e, half), behind)
            for t in range(4):
                nc.tensor.matmul_mx(
                    out=sums[:, t, :],
                    lhsT=codes_of(ordered_words[e][:, t * width : (t + 1) * width], e),
                    lhsT_scale=ordered_plane[e][:, t * P : (t + 1) * P],
                    rhs=slot_words[2 * e + half].bitcast(FP8X4),
                    rhs_scale=slot_scales[2 * e + half],
                    start=True,
                    stop=True,
                )
            return grouped[e][:, half * P : (half + 1) * P, :], sums[:].rearrange("p t s -> p s t")

        def relu_on_scalar(written, sums):
            nc.scalar.activation(written, sums, RELU)

        def quantise(values, code_room, scale_room):
            columns = values.shape[1]
            codes = held.tile([P, columns], U32, name=code_room, align_bytes=64)
            scales = held.tile([P, columns], U8, name=scale_room, align_bytes=64)
            nc.vector.quantize_mx(
                out=codes[:].bitcast(FP8X4), scales=scales[:], in_=values.rearrange("p c t -> p (c t)")
            )
            return codes, scales

        def second_product(first_slot, last_slot, quantised, low, behind):
            codes, scales = quantised
            results = bank([P, last_slot - first_slot], ("results", first_slot), behind)
            for start in range(first_slot, last_slot, C):
                e, end = start // C, min(start + C, last_slot)
                nc.tensor.matmul_mx(
                    out=results[:, start - first_slot : end - first_slot],
                    lhsT=codes_of(row_of(w2, e), e),
                    lhsT_scale=s2[:, e, :],
                    rhs=codes[:, start - low : end - low].bitcast(FP8X4),
                    rhs_scale=scales[:, start - low : end - low],
                    start=True,
                    stop=True,
                )
            return results

        def store(results, first_slot, copy, queue):
            columns = results.shape[1]
            staged = held.tile([P, columns], F32, name="staged_%d" % first_slot, align_bytes=64)
            copy(staged[:], results[:])
            queue.dma_start(out[:, first_slot : first_slot + columns], staged[:])

        def pair_out(e, quantised, low, behind, copy):
            results = second_product(e * C, (e + 2) * C, quantised, low * C, behind)
            store(results, e * C, copy, nc.sync)

        first_bytes = gathered("first_bytes", U8, 28, 32, slot_scales)
        gather(first_bytes, byte_window, 28, 32)
        gather(gathered("slot_words_31", U32, 31, 32, slot_words), word_window, 31, 32)
        gather(gathered("slot_words_30", U32, 30, 31, slot_words, 18 * P), word_window, 30, 31)
        second_words = gathered("second_words", U32, 26, 30, slot_words)
        gather(second_words, word_window, 28, 30)
        gather(second_words, word_window, 26, 28)
        turned_product(E - 1, 1, H // 2)
        gather(gathered("slot_words_31", U8, 24, 28, slot_scales), byte_window, 24, 28)
        turned_product(E - 1, 0, H)
        most_words = gathered("most_words", U32, 6, 26, slot_words, 20 * P)
        most_bytes = gathered("most_bytes", U8, 4, 24, slot_scales, 0)
        for first in range(22, 5, -4):
            gather(most_words, word_window, first, first + 4)
            gather(most_bytes, byte_window, first - 2, first + 2)

        quantised = {}
        for e in reversed(range(E - 1)):
            unread = [first_product(e, half) for half in (1, 0)]
            for written, sums in unread if e >= IN_TURN_FROM or e == 0 else reversed(unread):
                relu_on_scalar(written, sums)
            if e == E - 3:
                turn_and_weave(E - 1)
            if e == 5:
                quantised[12] = quantise(group_tile[12][:], "words_5", "scales_12")
                quantised[8] = quantise(group_tile[8][:], "words_8", "scales_8")
                last_words = gathered("grouped_12", U32, 0, 6, slot_words)
                last_bytes = gathered("grouped_8", U8, 0, 4, slot_scales)
                gather(last_words, word_window, 2, 6)
                gather(last_bytes, byte_window, 0, 4)
                gather(last_words, word_window, 0, 2)
            if e == HOT:
                for pair in (14, 12, 10, 8):
                    low = pair // 4 * 4
                    pair_out(pair, quantised[low], low, None, nc.scalar.copy)

        for low in (6, 4, 2):
            quantised[low] = quantise(group_tile[low][:], "codes_%d" % low, "scales_%d" % low)
        pair_out(6, quantised[6], 6, ("sums", 2, 1), nc.vector.tensor_copy)
        pair_out(4, quantised[4], 4, ("sums", 1, 0), nc.vector.tensor_copy)
        pair_out(2, quantised[2], 2, ("sums", 2, 0), nc.scalar.copy)
        quantised[1] = quantise(group_tile[1][:], "codes_1", "scales_1")
        store(second_product(C, 2 * C, quantised[1], C, ("results", 10 * C)), C, nc.scalar.copy, nc.sync)
        halves = {
            half: quantise(grouped[0][:, half * P : (half + 1) * P, :], "codes_0_%d" % half, "scales_0_%d" % half)
            for half in (1, 0)
        }
        store(second_product(P, C, halves[1], P, ("results", 8 * C)), P, nc.vector.tensor_copy, nc.sync)
        store(second_product(0, P, halves[0], 0, ("results", 6 * C)), 0, nc.scalar.copy, nc.scalar)
